import numpy as np
import ml_dtypes


def mxq(x, axis, fmt="e4m3"):
    dtype, down = {"e4m3": (ml_dtypes.float8_e4m3fn, 7), "e5m2": (ml_dtypes.float8_e5m2, 14)}[fmt]
    v = np.moveaxis(np.asarray(x, np.float32).astype(ml_dtypes.bfloat16).astype(np.float64), axis, -1)
    blocks = v.reshape(v.shape[:-1] + (-1, 32))
    amax = np.abs(blocks).max(-1, keepdims=True)
    byte = np.maximum(np.where(amax > 0, np.frexp(amax)[1] - 1 + 127, 0) - down, 1)
    scale = np.exp2(byte - 127.0)
    codes = (blocks / scale).astype(np.float32).astype(dtype).astype(np.float64)
    return np.moveaxis((codes * scale).reshape(v.shape), -1, axis)


WIDE = False


def mx_kscale(k):
    if not WIDE:
        return np.ones(k)
    levels = np.array([10, -10, 5, -5, 0])
    if k % 512:
        return np.exp2(np.random.permutation(np.resize(levels, k // 32))).repeat(32)
    a = np.empty((k // 512, 16))
    for p in range(k // 512):
        a[p, :8] = np.random.permutation(np.resize(levels, 8))
        for g in range(8):
            far = levels[np.abs(levels - a[p, g]) >= 10]
            a[p, g + 8] = far[np.random.randint(len(far))]
    return np.exp2(a.ravel()).repeat(32)


def f64(x):
    return np.asarray(x).astype(np.float64)


def striped(idx):
    return np.tile(idx.reshape(-1, 16).T, (8, 1)).astype(np.uint16)


def unstriped(offs):
    return offs[:16].T.reshape(-1).astype(np.int64)


def striped8(idx):
    return np.concatenate([x.reshape(-1, 16).T for x in idx]).astype(np.uint16)


def runs(offs, k):
    lists = np.stack([offs[16 * r : 16 * r + 16].T.reshape(-1) for r in range(8)]).astype(np.int64)
    return lists[np.arange(k) % 512 // 64]


def pack_weight(w):
    k, n = w.shape
    w = f64(np.asarray(w, np.float32).astype(ml_dtypes.bfloat16)).reshape(k // 32, 32, n)
    amax = np.abs(w).max(1)
    byte = np.clip(np.where(amax > 0, np.frexp(amax)[1] - 1 + 127 - 7, 1), 1, 254)
    scaled = (w * np.exp2(127.0 - byte)[:, None, :]).reshape(k, n).astype(np.float32)
    words = np.ascontiguousarray(scaled.reshape(k // 512, 128, 4, n).transpose(0, 1, 3, 2)).astype(ml_dtypes.float8_e4m3fn).view(np.uint8)
    return words, np.ascontiguousarray(byte.astype(np.uint8).reshape(k // 512, 16, n))


def unpack_weight(words, scales):
    g, p, n, _ = words.shape
    vals = np.ascontiguousarray(words).view(ml_dtypes.float8_e4m3fn).astype(np.float64) * np.repeat(np.exp2(scales.astype(np.float64) - 127.0), 8, axis=1)[..., None]
    return vals.transpose(0, 1, 3, 2).reshape(g * 512, n)


E2M1 = np.array([0.0, 0.5, 1.0, 1.5, 2.0, 3.0, 4.0, 6.0, -0.0, -0.5, -1.0, -1.5, -2.0, -3.0, -4.0, -6.0])


def pack_fp4(w):
    k, n = w.shape
    w = f64(np.asarray(w, np.float32).astype(ml_dtypes.bfloat16)).reshape(k // 32, 32, n)
    amax = np.abs(w).max(1)
    mant, ex = np.frexp(amax / 6.0)
    byte = np.clip(np.where(amax > 0, np.where(mant > 0.5, ex, ex - 1) + 127, 1), 1, 254)
    scaled = (w * np.exp2(127.0 - byte)[:, None, :]).reshape(k, n).astype(np.float32)
    c = np.ascontiguousarray(scaled.reshape(k // 512, 128, 4, n).transpose(0, 1, 3, 2)).astype(ml_dtypes.float4_e2m1fn).view(np.uint8) & 0xF
    words = (c[..., 0::2] | (c[..., 1::2] << 4)).reshape(k // 512, 128, 2 * n)
    return np.ascontiguousarray(words), np.ascontiguousarray(byte.astype(np.uint8).reshape(k // 512, 16, n))


def unpack_fp4(words, scales):
    g, _, n = scales.shape
    words = np.ascontiguousarray(words).reshape(g, 128, n, 2)
    nib = np.empty((g, 128, n, 4), np.uint8)
    nib[..., 0::2] = words & 0xF
    nib[..., 1::2] = words >> 4
    vals = E2M1[nib] * np.repeat(np.exp2(scales.astype(np.float64) - 127.0), 8, axis=1)[..., None]
    return vals.transpose(0, 1, 3, 2).reshape(g * 512, n)


def planes(y):
    n, m = y.shape
    v = y.astype(np.float32).astype(ml_dtypes.bfloat16).astype(np.float64).reshape(n // 32, 32, m)
    top = np.abs(v).max(1)
    byte = np.clip(np.where(top > 0, np.frexp(top)[1] - 1 + 127 - 7, 1), 1, 254)
    codes = (v * np.exp2(127.0 - byte)[:, None, :]).reshape(n, m).astype(np.float32).astype(ml_dtypes.float8_e4m3fn).view(np.uint8)
    words = codes.reshape(n // 512, 128, 4, m).transpose(0, 1, 3, 2)
    return np.ascontiguousarray(words), np.ascontiguousarray(byte.astype(np.uint8).reshape(n // 512, 16, m))


K, T, S, N, H = 512, 2048, 512, 512, 512


def setup_inputs():
    n = np.random.standard_normal
    s = mx_kscale(K)[:, None]
    u = mx_kscale(H)
    packed_xT = pack_weight(n((K, T)) * s)
    packed_w2 = pack_fp4(n((K, N)) / np.sqrt(K) / s)
    packed_w3 = pack_fp4(n((H, N)) / np.sqrt(H) / u[:, None])
    return {
        "x_words": packed_xT[0],
        "x_scales": packed_xT[1],
        "w1": (n((K, H)) / np.sqrt(K) / s * u).astype(np.float32),
        "w2_words": packed_w2[0],
        "w2_scales": packed_w2[1],
        "w3_words": packed_w3[0],
        "w3_scales": packed_w3[1],
        "offs": striped(np.random.permutation(T)[:S]),
        "in1": striped8(np.stack([np.random.permutation(S) for _ in range(8)])),
        "in2": striped8(np.stack([np.random.permutation(S) for _ in range(8)])),
        "rev": striped8(np.stack([np.random.permutation(S) for _ in range(8)])),
    }


def reference(x_words, x_scales, w1, w2_words, w2_scales, w3_words, w3_scales, offs, in1, in2, rev):
    xq = unpack_weight(x_words, x_scales)[:, unstriped(offs)]
    h0 = unpack_fp4(w2_words, w2_scales).T @ xq
    y = mxq(f64(w1), 0, "e4m3").T @ xq
    z = y[np.arange(H)[:, None], runs(in1, H)] + y[np.arange(H)[:, None], runs(in2, H)] - (y[np.arange(H)[:, None], runs(rev, H)])
    o = h0 + (unpack_fp4(w3_words, w3_scales).T @ mxq(z, 0, "e4m3"))
    out_0 = o
    return (out_0,) + planes(out_0)

@@ -1,0 +1,208 @@
+from contextlib import ExitStack
+
+import concourse.mybir as mybir
+
+F32 = mybir.dt.float32
+BF16 = mybir.dt.bfloat16
+I32 = mybir.dt.int32
+U32 = mybir.dt.uint32
+U16 = mybir.dt.uint16
+U8 = mybir.dt.uint8
+FP8X4 = mybir.dt.float8_e4m3fn_x4
+FP4X4 = mybir.dt.float4_e2m1fn_x4
+ADD = mybir.AluOpType.add
+SUBTRACT = mybir.AluOpType.subtract
+
+P = 128
+PACK = 4
+T, S, H, N = 2048, 512, 512, 512
+HALF = S // 2
+BLOCK = 128
+CHUNKS = ((0, 256), (256, 128), (384, 128))
+
+FLOPS = 3 * 2 * 512 * 512 * 512
+
+
+def load_scale_rows(queue, plane, rows):
+    for q in range(4):
+        queue.dma_start(plane[32 * q : 32 * q + 4, :].bitcast(I32), rows[4 * q : 4 * q + 4, :].bitcast(I32))
+
+
+def entries(offsets, start, count):
+    return offsets[:, start // 16 : (start + count) // 16]
+
+
+def interleave(copy, dst, src):
+    copy(dst.rearrange("p (c i) t -> p c t i", i=4), src.rearrange("p t (c i) -> p c t i", i=4))
+
+
+def tile_picked_dmpnn8_none_po_kernel(
+    tc, x_words, x_scales, w1, w2_words, w2_scales, w3_words, w3_scales, offs, in1, in2, rev, out_0, out_1, out_2
+):
+    nc = tc.nc
+    with ExitStack() as ctx:
+        keep = ctx.enter_context(tc.tile_pool(name="keep", bufs=1))
+        ring = ctx.enter_context(tc.tile_pool(name="ring", bufs=2))
+        psum = ctx.enter_context(tc.psum_pool(name="psum", bufs=2))
+
+        x_scale_table = keep.tile([P, T], U8, align_bytes=64)
+        nc.vector.memset(x_scale_table[:].bitcast(I32), 0)
+        raw_scales = []
+        for name in ("w2", "w3"):
+            plane = keep.tile([P, N], U8, name=name + "_raw_scales", align_bytes=64)
+            nc.gpsimd.memset(plane[:].bitcast(I32), 0)
+            raw_scales.append(plane)
+
+        raw_words = []
+        for name, words in (("w2", w2_words), ("w3", w3_words)):
+            tile = keep.tile([P, 2 * N], U8, name=name + "_raw_words", align_bytes=64)
+            nc.sync.dma_start(tile[:].bitcast(I32), words[0].bitcast(I32))
+            raw_words.append(tile)
+        picked = keep.tile([P, S // 16], U16)
+        nc.sync.dma_start(picked[:], offs)
+        load_scale_rows(nc.scalar, x_scale_table, x_scales[0])
+        w1_rows = w1.rearrange("(p j) c -> p j c", j=PACK)
+        w1_raw = []
+        for h in range(2):
+            tile = keep.tile([P, PACK, H // 2], F32, name="w1_raw%d" % h, align_bytes=64)
+            nc.sync.dma_start(tile[:], w1_rows[:, :, h * (H // 2) : (h + 1) * (H // 2)])
+            w1_raw.append(tile)
+        x_table = keep.tile([P, T], U32, align_bytes=64)
+        nc.sync.dma_start(x_table[:].bitcast(I32), x_words[0].rearrange("p c r -> p (c r)").bitcast(I32))
+        lists = {}
+        for name, src in (("rev", rev), ("in2", in2), ("in1", in1)):
+            tile = keep.tile([P, S // 16], U16, name=name + "_list")
+            nc.sync.dma_start(tile[:], src)
+            lists[name] = tile
+        load_scale_rows(nc.gpsimd, raw_scales[0], w2_scales[0])
+        load_scale_rows(nc.gpsimd, raw_scales[1], w3_scales[0])
+
+        dealt_words, dealt_scales = [], []
+        for w in range(2):
+            tile = keep.tile([P, 2 * N], U8, name="dealt_words%d" % w, align_bytes=64)
+            nc.vector.tensor_copy(
+                tile[:].rearrange("p (t m b) -> p m t b", t=PACK, b=2),
+                raw_words[w][:].rearrange("p (m t b) -> p m t b", t=PACK, b=2),
+            )
+            dealt_words.append(tile)
+
+        x_picked_scales = keep.tile([P, S], U8, align_bytes=64)
+        nc.vector.tensor_copy(x_picked_scales[:], x_scale_table[:].indirect(picked[:]))
+
+        w1_grouped = keep.tile([P, PACK * H], BF16, align_bytes=64)
+        w1_view = w1_grouped[:].rearrange("p (t m j) -> p m j t", t=PACK, j=PACK)
+        for h in range(2):
+            nc.scalar.copy(
+                w1_view[:, 64 * h : 64 * (h + 1), :, :],
+                w1_raw[h][:].rearrange("p j (m t) -> p m j t", t=PACK),
+            )
+        w1_codes = keep.tile([P, H], U32, align_bytes=64)
+        w1_scales = keep.tile([P, H], U8, align_bytes=64)
+        nc.vector.quantize_mx(out=w1_codes[:].bitcast(FP8X4), scales=w1_scales[:], in_=w1_grouped[:])
+
+        for w in range(2):
+            tile = keep.tile([P, N], U8, name="dealt_scales%d" % w, align_bytes=64)
+            nc.vector.tensor_copy(
+                tile[:].rearrange("p (t m) -> p m t", t=PACK),
+                raw_scales[w][:].rearrange("p (m t) -> p m t", t=PACK),
+            )
+            dealt_scales.append(tile)
+
+        x_picked = keep.tile([P, S], U32, align_bytes=64)
+        y = [keep.tile([P, S], F32, name="y%d" % t, align_bytes=64) for t in range(PACK)]
+        for h in range(2):
+            cols = slice(h * HALF, (h + 1) * HALF)
+            nc.vector.tensor_copy(x_picked[:, cols], x_table[:].indirect(entries(picked, h * HALF, HALF)))
+            for t in range(PACK):
+                bank = psum.tile([P, HALF], F32, name="y_bank", tag="bank%d" % t)
+                feats = slice(t * P, (t + 1) * P)
+                nc.tensor.matmul_mx(
+                    out=bank[:],
+                    lhsT=w1_codes[:, feats].bitcast(FP8X4),
+                    lhsT_scale=w1_scales[:, feats],
+                    rhs=x_picked[:, cols].bitcast(FP8X4),
+                    rhs_scale=x_picked_scales[:, cols],
+                    start=True,
+                    stop=True,
+                )
+                if h == 1 and t == 0:
+                    nc.vector.tensor_copy(y[t][:, cols], bank[:])
+                else:
+                    nc.scalar.copy(y[t][:, cols], bank[:])
+
+        z_codes = keep.tile([P, S], U32, align_bytes=64)
+        z_scales = keep.tile([P, S], U8, align_bytes=64)
+        o_codes = keep.tile([P, S], U32, align_bytes=64)
+        o_scales = keep.tile([P, S], U8, align_bytes=64)
+        out_rows = out_0.rearrange("(p t) j -> p t j", t=PACK)
+        out_words = out_1[0].rearrange("p c r -> p (c r)").bitcast(I32)
+
+        def weights(w, t):
+            return dict(
+                lhsT=dealt_words[w][:, 2 * P * t : 2 * P * (t + 1)].bitcast(FP4X4),
+                lhsT_scale=dealt_scales[w][:, P * t : P * (t + 1)],
+            )
+
+        for start, width in CHUNKS:
+            last = start + width == S
+            cols = slice(start, start + width)
+            z = ring.tile([P, PACK, width], F32, name="z", align_bytes=64)
+            for pair in ((0, 1), (2, 3)):
+                first = {t: ring.tile([P, width], F32, name="first%d" % (t % 2), align_bytes=64) for t in pair}
+                second = {t: ring.tile([P, width], F32, name="second%d" % (t % 2), align_bytes=64) for t in pair}
+                for t in pair:
+                    nc.vector.tensor_copy(first[t][:], y[t][:].indirect(entries(lists["rev"], start, width)))
+                for t in pair:
+                    nc.vector.tensor_tensor(
+                        second[t][:], y[t][:].indirect(entries(lists["in2"], start, width)), first[t][:], SUBTRACT
+                    )
+                for t in pair:
+                    nc.vector.tensor_tensor(
+                        z[:, t, :], y[t][:].indirect(entries(lists["in1"], start, width)), second[t][:], ADD
+                    )
+            regroup = nc.vector.tensor_copy if last else nc.scalar.copy
+            z_grouped = ring.tile([P, width, PACK], BF16, name="z_grouped", align_bytes=64)
+            interleave(regroup, z_grouped[:], z[:])
+            nc.vector.quantize_mx(
+                out=z_codes[:, cols].bitcast(FP8X4),
+                scales=z_scales[:, cols],
+                in_=z_grouped[:].rearrange("p c t -> p (c t)"),
+            )
+            o = ring.tile([P, PACK, width], F32, name="o", align_bytes=64)
+            for b0 in range(0, width, BLOCK):
+                block = slice(start + b0, start + b0 + BLOCK)
+                banks = [psum.tile([P, BLOCK], F32, name="o_bank", tag="bank%d" % t) for t in range(PACK)]
+                for t in range(PACK):
+                    nc.tensor.matmul_mx(
+                        out=banks[t][:],
+                        rhs=x_picked[:, block].bitcast(FP8X4),
+                        rhs_scale=x_picked_scales[:, block],
+                        start=True,
+                        stop=False,
+                        **weights(0, t),
+                    )
+                for t in range(PACK):
+                    nc.tensor.matmul_mx(
+                        out=banks[t][:],
+                        rhs=z_codes[:, block].bitcast(FP8X4),
+                        rhs_scale=z_scales[:, block],
+                        start=False,
+                        stop=True,
+                        **weights(1, t),
+                    )
+                    drain = nc.vector.tensor_copy if last and t % 2 == 1 else nc.scalar.copy
+                    drain(o[:, t, b0 : b0 + BLOCK], banks[t][:])
+            nc.sync.dma_start(out_rows[:, :, cols], o[:])
+            o_grouped = ring.tile([P, width, PACK], BF16, name="o_grouped", align_bytes=64)
+            interleave(regroup, o_grouped[:], o[:])
+            nc.vector.quantize_mx(
+                out=o_codes[:, cols].bitcast(FP8X4),
+                scales=o_scales[:, cols],
+                in_=o_grouped[:].rearrange("p c t -> p (c t)"),
+            )
+            nc.sync.dma_start(out_words[:, cols], o_codes[:, cols].bitcast(I32))
+        for q in range(4):
+            queue = nc.scalar if q % 2 else nc.sync
+            queue.dma_start(
+                out_2[0, 4 * q : 4 * q + 4, :].bitcast(I32), o_scales[32 * q : 32 * q + 4, :].bitcast(I32)
+            )

@@ -23,8 +23,8 @@ CHUNKS = ((0, 256), (256, 128), (384, 128))
 FLOPS = 3 * 2 * 512 * 512 * 512
 
 
-def load_scale_rows(queue, plane, rows):
-    for q in range(4):
+def load_scale_rows(queues, plane, rows):
+    for q, queue in enumerate(queues):
         queue.dma_start(plane[32 * q : 32 * q + 4, :].bitcast(I32), rows[4 * q : 4 * q + 4, :].bitcast(I32))
 
 
@@ -46,11 +46,11 @@ def tile_picked_dmpnn8_none_po_kernel(
         psum = ctx.enter_context(tc.psum_pool(name="psum", bufs=2))
 
         x_scale_table = keep.tile([P, T], U8, align_bytes=64)
-        nc.vector.memset(x_scale_table[:].bitcast(I32), 0)
+        nc.gpsimd.memset(x_scale_table[:].bitcast(I32), 0)
         raw_scales = []
         for name in ("w2", "w3"):
             plane = keep.tile([P, N], U8, name=name + "_raw_scales", align_bytes=64)
-            nc.gpsimd.memset(plane[:].bitcast(I32), 0)
+            nc.vector.memset(plane[:].bitcast(I32), 0)
             raw_scales.append(plane)
 
         raw_words = []
@@ -60,75 +60,76 @@ def tile_picked_dmpnn8_none_po_kernel(
             raw_words.append(tile)
         picked = keep.tile([P, S // 16], U16)
         nc.sync.dma_start(picked[:], offs)
-        load_scale_rows(nc.scalar, x_scale_table, x_scales[0])
+        load_scale_rows((nc.scalar,) * 4, x_scale_table, x_scales[0])
         w1_rows = w1.rearrange("(p j) c -> p j c", j=PACK)
         w1_raw = []
         for h in range(2):
             tile = keep.tile([P, PACK, H // 2], F32, name="w1_raw%d" % h, align_bytes=64)
             nc.sync.dma_start(tile[:], w1_rows[:, :, h * (H // 2) : (h + 1) * (H // 2)])
             w1_raw.append(tile)
-        x_table = keep.tile([P, T], U32, align_bytes=64)
+        x_table = keep.tile([P, T], U32, tag="x_table", align_bytes=64)
         nc.sync.dma_start(x_table[:].bitcast(I32), x_words[0].rearrange("p c r -> p (c r)").bitcast(I32))
         lists = {}
         for name, src in (("rev", rev), ("in2", in2), ("in1", in1)):
             tile = keep.tile([P, S // 16], U16, name=name + "_list")
             nc.sync.dma_start(tile[:], src)
             lists[name] = tile
-        load_scale_rows(nc.gpsimd, raw_scales[0], w2_scales[0])
-        load_scale_rows(nc.gpsimd, raw_scales[1], w3_scales[0])
+            if name == "rev":
+                load_scale_rows((nc.sync,) * 4, raw_scales[1], w3_scales[0])
+        load_scale_rows((nc.gpsimd,) * 4, raw_scales[0], w2_scales[0])
 
         dealt_words, dealt_scales = [], []
         for w in range(2):
             tile = keep.tile([P, 2 * N], U8, name="dealt_words%d" % w, align_bytes=64)
             nc.vector.tensor_copy(
-                tile[:].rearrange("p (t m b) -> p m t b", t=PACK, b=2),
-                raw_words[w][:].rearrange("p (m t b) -> p m t b", t=PACK, b=2),
+                tile[:].rearrange("p (t g m b) -> p g t m b", t=PACK, m=8, b=2),
+                raw_words[w][:].rearrange("p (g m t b) -> p g t m b", t=PACK, m=8, b=2),
             )
             dealt_words.append(tile)
 
         x_picked_scales = keep.tile([P, S], U8, align_bytes=64)
         nc.vector.tensor_copy(x_picked_scales[:], x_scale_table[:].indirect(picked[:]))
 
-        w1_grouped = keep.tile([P, PACK * H], BF16, align_bytes=64)
-        w1_view = w1_grouped[:].rearrange("p (t m j) -> p m j t", t=PACK, j=PACK)
-        for h in range(2):
-            nc.scalar.copy(
-                w1_view[:, 64 * h : 64 * (h + 1), :, :],
-                w1_raw[h][:].rearrange("p j (m t) -> p m j t", t=PACK),
-            )
         w1_codes = keep.tile([P, H], U32, align_bytes=64)
         w1_scales = keep.tile([P, H], U8, align_bytes=64)
-        nc.vector.quantize_mx(out=w1_codes[:].bitcast(FP8X4), scales=w1_scales[:], in_=w1_grouped[:])
+        for u, cast in enumerate((nc.scalar.copy, nc.vector.tensor_copy)):
+            grouped = keep.tile([P, 2 * H], BF16, name="w1_grouped", tag="w1_grouped%d" % u, align_bytes=64)
+            target = grouped[:].rearrange("p (t m j) -> p m j t", t=2, j=PACK)
+            for h in range(2):
+                source = w1_raw[h][:].rearrange("p j (m t) -> p m j t", t=PACK)
+                cast(target[:, 64 * h : 64 * (h + 1), :, :], source[:, :, :, 2 * u : 2 * u + 2])
+            feats = slice(2 * P * u, 2 * P * (u + 1))
+            nc.vector.quantize_mx(out=w1_codes[:, feats].bitcast(FP8X4), scales=w1_scales[:, feats], in_=grouped[:])
 
-        for w in range(2):
-            tile = keep.tile([P, N], U8, name="dealt_scales%d" % w, align_bytes=64)
-            nc.vector.tensor_copy(
-                tile[:].rearrange("p (t m) -> p m t", t=PACK),
-                raw_scales[w][:].rearrange("p (m t) -> p m t", t=PACK),
-            )
-            dealt_scales.append(tile)
-
-        x_picked = keep.tile([P, S], U32, align_bytes=64)
+        x_picked = [keep.tile([P, HALF], U32, name="x_picked", tag="w1_grouped%d" % h, align_bytes=64) for h in range(2)]
         y = [keep.tile([P, S], F32, name="y%d" % t, align_bytes=64) for t in range(PACK)]
         for h in range(2):
-            cols = slice(h * HALF, (h + 1) * HALF)
-            nc.vector.tensor_copy(x_picked[:, cols], x_table[:].indirect(entries(picked, h * HALF, HALF)))
-            for t in range(PACK):
+            nc.vector.tensor_copy(
+                x_picked[h][:], x_table[:].indirect(entries(picked, h * HALF, HALF))
+            )
+        both_scales = keep.tile([P, 2 * N], U8, tag="x_table", align_bytes=64)
+        for w in range(2):
+            part = both_scales[:, w * N : (w + 1) * N]
+            nc.vector.tensor_copy(
+                part.rearrange("p (t g m) -> p g t m", t=PACK, m=16),
+                raw_scales[w][:].rearrange("p (g m t) -> p g t m", t=PACK, m=16),
+            )
+            dealt_scales.append(part)
+        for t in range(PACK):
+            feats = slice(t * P, (t + 1) * P)
+            for h in range(2):
+                cols = slice(h * HALF, (h + 1) * HALF)
                 bank = psum.tile([P, HALF], F32, name="y_bank", tag="bank%d" % t)
-                feats = slice(t * P, (t + 1) * P)
                 nc.tensor.matmul_mx(
                     out=bank[:],
                     lhsT=w1_codes[:, feats].bitcast(FP8X4),
                     lhsT_scale=w1_scales[:, feats],
-                    rhs=x_picked[:, cols].bitcast(FP8X4),
+                    rhs=x_picked[h][:].bitcast(FP8X4),
                     rhs_scale=x_picked_scales[:, cols],
                     start=True,
                     stop=True,
                 )
-                if h == 1 and t == 0:
-                    nc.vector.tensor_copy(y[t][:, cols], bank[:])
-                else:
-                    nc.scalar.copy(y[t][:, cols], bank[:])
+                nc.scalar.copy(y[t][:, cols], bank[:])
 
         z_codes = keep.tile([P, S], U32, align_bytes=64)
         z_scales = keep.tile([P, S], U8, align_bytes=64)
@@ -143,64 +144,88 @@ def tile_picked_dmpnn8_none_po_kernel(
                 lhsT_scale=dealt_scales[w][:, P * t : P * (t + 1)],
             )
 
-        for start, width in CHUNKS:
-            last = start + width == S
+        def looked_up(t, name, start, width):
+            return y[t][:].indirect(entries(lists[name], start, width))
+
+        def messages(start, width):
             cols = slice(start, start + width)
-            z = ring.tile([P, PACK, width], F32, name="z", align_bytes=64)
-            for pair in ((0, 1), (2, 3)):
-                first = {t: ring.tile([P, width], F32, name="first%d" % (t % 2), align_bytes=64) for t in pair}
-                second = {t: ring.tile([P, width], F32, name="second%d" % (t % 2), align_bytes=64) for t in pair}
-                for t in pair:
-                    nc.vector.tensor_copy(first[t][:], y[t][:].indirect(entries(lists["rev"], start, width)))
-                for t in pair:
-                    nc.vector.tensor_tensor(
-                        second[t][:], y[t][:].indirect(entries(lists["in2"], start, width)), first[t][:], SUBTRACT
-                    )
-                for t in pair:
-                    nc.vector.tensor_tensor(
-                        z[:, t, :], y[t][:].indirect(entries(lists["in1"], start, width)), second[t][:], ADD
-                    )
-            regroup = nc.vector.tensor_copy if last else nc.scalar.copy
+            z = keep.tile([P, PACK, width], F32, name="z", align_bytes=64)
+            for planes in ((0, 1), (2, 3)) if start == 0 else ((0, 1, 2, 3),):
+                first = {t: keep.tile([P, width], F32, name="first%d" % t, align_bytes=64) for t in planes}
+                second = {t: keep.tile([P, width], F32, name="second%d" % t, align_bytes=64) for t in planes}
+                for t in planes:
+                    nc.vector.tensor_copy(first[t][:], looked_up(t, "rev", start, width))
+                for t in planes:
+                    nc.vector.tensor_tensor(second[t][:], looked_up(t, "in2", start, width), first[t][:], SUBTRACT)
+                for t in planes:
+                    nc.vector.tensor_tensor(z[:, t, :], looked_up(t, "in1", start, width), second[t][:], ADD)
             z_grouped = ring.tile([P, width, PACK], BF16, name="z_grouped", align_bytes=64)
-            interleave(regroup, z_grouped[:], z[:])
+            interleave(nc.vector.tensor_copy if cols.stop == S else nc.scalar.copy, z_grouped[:], z[:])
             nc.vector.quantize_mx(
                 out=z_codes[:, cols].bitcast(FP8X4),
                 scales=z_scales[:, cols],
                 in_=z_grouped[:].rearrange("p c t -> p (c t)"),
             )
-            o = ring.tile([P, PACK, width], F32, name="o", align_bytes=64)
-            for b0 in range(0, width, BLOCK):
-                block = slice(start + b0, start + b0 + BLOCK)
-                banks = [psum.tile([P, BLOCK], F32, name="o_bank", tag="bank%d" % t) for t in range(PACK)]
-                for t in range(PACK):
-                    nc.tensor.matmul_mx(
-                        out=banks[t][:],
-                        rhs=x_picked[:, block].bitcast(FP8X4),
-                        rhs_scale=x_picked_scales[:, block],
-                        start=True,
-                        stop=False,
-                        **weights(0, t),
-                    )
-                for t in range(PACK):
-                    nc.tensor.matmul_mx(
-                        out=banks[t][:],
-                        rhs=z_codes[:, block].bitcast(FP8X4),
-                        rhs_scale=z_scales[:, block],
-                        start=False,
-                        stop=True,
-                        **weights(1, t),
-                    )
-                    drain = nc.vector.tensor_copy if last and t % 2 == 1 else nc.scalar.copy
-                    drain(o[:, t, b0 : b0 + BLOCK], banks[t][:])
-            nc.sync.dma_start(out_rows[:, :, cols], o[:])
-            o_grouped = ring.tile([P, width, PACK], BF16, name="o_grouped", align_bytes=64)
-            interleave(regroup, o_grouped[:], o[:])
-            nc.vector.quantize_mx(
-                out=o_codes[:, cols].bitcast(FP8X4),
-                scales=o_scales[:, cols],
-                in_=o_grouped[:].rearrange("p c t -> p (c t)"),
+
+        def first_pass(bank, t, c0):
+            h, within = divmod(c0, HALF)
+            nc.tensor.matmul_mx(
+                out=bank,
+                rhs=x_picked[h][:, within : within + BLOCK].bitcast(FP8X4),
+                rhs_scale=x_picked_scales[:, c0 : c0 + BLOCK],
+                start=True,
+                stop=False,
+                **weights(0, t),
             )
-            nc.sync.dma_start(out_words[:, cols], o_codes[:, cols].bitcast(I32))
+
+        def second_pass(bank, t, c0):
+            nc.tensor.matmul_mx(
+                out=bank,
+                rhs=z_codes[:, c0 : c0 + BLOCK].bitcast(FP8X4),
+                rhs_scale=z_scales[:, c0 : c0 + BLOCK],
+                start=False,
+                stop=True,
+                **weights(1, t),
+            )
+
+        o_grouped = [keep.tile([P, HALF, PACK], BF16, name="o_grouped%d" % h, align_bytes=64) for h in range(2)]
+
+        def results(start, width):
+            o = keep.tile([P, PACK, width], F32, name="o%d" % start, align_bytes=64)
+            for c0 in range(start, start + width, BLOCK):
+                h, within = divmod(c0, HALF)
+                rounded = o_grouped[h][:, within : within + BLOCK, :]
+                if c0 + BLOCK < S:
+                    bank = psum.tile([P, PACK, BLOCK], F32, name="o_bank", tag="bank%d" % (c0 // BLOCK))
+                    for t in range(PACK):
+                        first_pass(bank[:, t, :], t, c0)
+                        second_pass(bank[:, t, :], t, c0)
+                    nc.scalar.copy(rounded, bank[:].rearrange("p t c -> p c t"))
+                    nc.scalar.copy(o[:, :, c0 - start : c0 - start + BLOCK], bank[:])
+                else:
+                    banks = [psum.tile([P, BLOCK], F32, name="o_bank", tag="bank%d" % t) for t in range(PACK)]
+                    for t in range(PACK):
+                        first_pass(banks[t][:], t, c0)
+                    for t in range(PACK):
+                        second_pass(banks[t][:], t, c0)
+                        nc.vector.tensor_copy(o[:, t, :], banks[t][:])
+                    interleave(nc.vector.tensor_copy, rounded, o[:])
+            nc.sync.dma_start(out_rows[:, :, start : start + width], o[:])
+            if (start + width) % HALF == 0:
+                h = start // HALF
+                cols = slice(h * HALF, (h + 1) * HALF)
+                nc.vector.quantize_mx(
+                    out=o_codes[:, cols].bitcast(FP8X4),
+                    scales=o_scales[:, cols],
+                    in_=o_grouped[h][:].rearrange("p c t -> p (c t)"),
+                )
+                nc.sync.dma_start(out_words[:, cols], o_codes[:, cols].bitcast(I32))
+
+        messages(*CHUNKS[0])
+        for n, chunk in enumerate(CHUNKS):
+            if n + 1 < len(CHUNKS):
+                messages(*CHUNKS[n + 1])
+            results(*chunk)
         for q in range(4):
             queue = nc.scalar if q % 2 else nc.sync
             queue.dma_start(

@@ -15,21 +15,23 @@ SUBTRACT = mybir.AluOpType.subtract
 
 P = 128
 PACK = 4
-T, S, H, N = 2048, 512, 512, 512
+QUADRANTS = 4
+GROUP = 16
+K, T, S, H, N = 512, 2048, 512, 512, 512
 HALF = S // 2
 BLOCK = 128
 CHUNKS = ((0, 256), (256, 128), (384, 128))
 
-FLOPS = 3 * 2 * 512 * 512 * 512
+FLOPS = 2 * K * H * S + 2 * K * N * S + 2 * H * N * S
 
 
-def load_scale_rows(queues, plane, rows):
-    for q, queue in enumerate(queues):
-        queue.dma_start(plane[32 * q : 32 * q + 4, :].bitcast(I32), rows[4 * q : 4 * q + 4, :].bitcast(I32))
+def load_scale_rows(queue, scale_tile, rows):
+    for q in range(QUADRANTS):
+        queue.dma_start(scale_tile[32 * q : 32 * q + 4, :].bitcast(I32), rows[4 * q : 4 * q + 4, :].bitcast(I32))
 
 
-def entries(offsets, start, count):
-    return offsets[:, start // 16 : (start + count) // 16]
+def entries(list_tile, start, count):
+    return list_tile[:, start // GROUP : (start + count) // GROUP]
 
 
 def interleave(copy, dst, src):
@@ -49,43 +51,46 @@ def tile_picked_dmpnn8_none_po_kernel(
         nc.gpsimd.memset(x_scale_table[:].bitcast(I32), 0)
         raw_scales = []
         for name in ("w2", "w3"):
-            plane = keep.tile([P, N], U8, name=name + "_raw_scales", align_bytes=64)
-            nc.vector.memset(plane[:].bitcast(I32), 0)
-            raw_scales.append(plane)
+            scale_tile = keep.tile([P, N], U8, name=name + "_raw_scales", align_bytes=64)
+            nc.vector.memset(scale_tile[:].bitcast(I32), 0)
+            raw_scales.append(scale_tile)
 
         raw_words = []
         for name, words in (("w2", w2_words), ("w3", w3_words)):
-            tile = keep.tile([P, 2 * N], U8, name=name + "_raw_words", align_bytes=64)
-            nc.sync.dma_start(tile[:].bitcast(I32), words[0].bitcast(I32))
-            raw_words.append(tile)
-        picked = keep.tile([P, S // 16], U16)
+            word_tile = keep.tile([P, 2 * N], U8, name=name + "_raw_words", align_bytes=64)
+            nc.sync.dma_start(word_tile[:].bitcast(I32), words[0].bitcast(I32))
+            raw_words.append(word_tile)
+        picked = keep.tile([P, S // GROUP], U16)
         nc.sync.dma_start(picked[:], offs)
-        load_scale_rows((nc.scalar,) * 4, x_scale_table, x_scales[0])
+        load_scale_rows(nc.scalar, x_scale_table, x_scales[0])
         w1_rows = w1.rearrange("(p j) c -> p j c", j=PACK)
         w1_raw = []
         for h in range(2):
-            tile = keep.tile([P, PACK, H // 2], F32, name="w1_raw%d" % h, align_bytes=64)
-            nc.sync.dma_start(tile[:], w1_rows[:, :, h * (H // 2) : (h + 1) * (H // 2)])
-            w1_raw.append(tile)
+            w1_half = keep.tile([P, PACK, H // 2], F32, name="w1_raw%d" % h, align_bytes=64)
+            nc.sync.dma_start(w1_half[:], w1_rows[:, :, h * (H // 2) : (h + 1) * (H // 2)])
+            w1_raw.append(w1_half)
         x_table = keep.tile([P, T], U32, tag="x_table", align_bytes=64)
         nc.sync.dma_start(x_table[:].bitcast(I32), x_words[0].rearrange("p c r -> p (c r)").bitcast(I32))
-        lists = {}
-        for name, src in (("rev", rev), ("in2", in2), ("in1", in1)):
-            tile = keep.tile([P, S // 16], U16, name=name + "_list")
-            nc.sync.dma_start(tile[:], src)
-            lists[name] = tile
-            if name == "rev":
-                load_scale_rows((nc.sync,) * 4, raw_scales[1], w3_scales[0])
-        load_scale_rows((nc.gpsimd,) * 4, raw_scales[0], w2_scales[0])
 
-        dealt_words, dealt_scales = [], []
+        def load_list(name, source):
+            list_tile = keep.tile([P, S // GROUP], U16, name=name + "_list")
+            nc.sync.dma_start(list_tile[:], source)
+            return list_tile
+
+        rev_list = load_list("rev", rev)
+        load_scale_rows(nc.sync, raw_scales[1], w3_scales[0])
+        in2_list = load_list("in2", in2)
+        in1_list = load_list("in1", in1)
+        load_scale_rows(nc.gpsimd, raw_scales[0], w2_scales[0])
+
+        dealt_words = []
         for w in range(2):
-            tile = keep.tile([P, 2 * N], U8, name="dealt_words%d" % w, align_bytes=64)
+            dealt = keep.tile([P, 2 * N], U8, name="dealt_words%d" % w, align_bytes=64)
             nc.vector.tensor_copy(
-                tile[:].rearrange("p (t g m b) -> p g t m b", t=PACK, m=8, b=2),
-                raw_words[w][:].rearrange("p (g m t b) -> p g t m b", t=PACK, m=8, b=2),
+                dealt[:].rearrange("p (t g i b) -> p g t i b", t=PACK, i=8, b=2),
+                raw_words[w][:].rearrange("p (g i t b) -> p g t i b", t=PACK, i=8, b=2),
             )
-            dealt_words.append(tile)
+            dealt_words.append(dealt)
 
         x_picked_scales = keep.tile([P, S], U8, align_bytes=64)
         nc.vector.tensor_copy(x_picked_scales[:], x_scale_table[:].indirect(picked[:]))
@@ -97,33 +102,36 @@ def tile_picked_dmpnn8_none_po_kernel(
             target = grouped[:].rearrange("p (t m j) -> p m j t", t=2, j=PACK)
             for h in range(2):
                 source = w1_raw[h][:].rearrange("p j (m t) -> p m j t", t=PACK)
-                cast(target[:, 64 * h : 64 * (h + 1), :, :], source[:, :, :, 2 * u : 2 * u + 2])
-            feats = slice(2 * P * u, 2 * P * (u + 1))
-            nc.vector.quantize_mx(out=w1_codes[:, feats].bitcast(FP8X4), scales=w1_scales[:, feats], in_=grouped[:])
+                cast(target[:, h * (P // 2) : (h + 1) * (P // 2), :, :], source[:, :, :, 2 * u : 2 * u + 2])
+            places = slice(2 * P * u, 2 * P * (u + 1))
+            nc.vector.quantize_mx(out=w1_codes[:, places].bitcast(FP8X4), scales=w1_scales[:, places], in_=grouped[:])
 
-        x_picked = [keep.tile([P, HALF], U32, name="x_picked", tag="w1_grouped%d" % h, align_bytes=64) for h in range(2)]
+        x_picked = [
+            keep.tile([P, HALF], U32, name="x_picked", tag="w1_grouped%d" % h, align_bytes=64) for h in range(2)
+        ]
         y = [keep.tile([P, S], F32, name="y%d" % t, align_bytes=64) for t in range(PACK)]
         for h in range(2):
-            nc.vector.tensor_copy(
-                x_picked[h][:], x_table[:].indirect(entries(picked, h * HALF, HALF))
-            )
+            nc.vector.tensor_copy(x_picked[h][:], x_table[:].indirect(entries(picked, h * HALF, HALF)))
+
         both_scales = keep.tile([P, 2 * N], U8, tag="x_table", align_bytes=64)
+        dealt_scales = []
         for w in range(2):
             part = both_scales[:, w * N : (w + 1) * N]
             nc.vector.tensor_copy(
-                part.rearrange("p (t g m) -> p g t m", t=PACK, m=16),
-                raw_scales[w][:].rearrange("p (g m t) -> p g t m", t=PACK, m=16),
+                part.rearrange("p (t g i) -> p g t i", t=PACK, i=16),
+                raw_scales[w][:].rearrange("p (g i t) -> p g t i", t=PACK, i=16),
             )
             dealt_scales.append(part)
+
         for t in range(PACK):
-            feats = slice(t * P, (t + 1) * P)
+            places = slice(t * P, (t + 1) * P)
             for h in range(2):
                 cols = slice(h * HALF, (h + 1) * HALF)
                 bank = psum.tile([P, HALF], F32, name="y_bank", tag="bank%d" % t)
                 nc.tensor.matmul_mx(
                     out=bank[:],
-                    lhsT=w1_codes[:, feats].bitcast(FP8X4),
-                    lhsT_scale=w1_scales[:, feats],
+                    lhsT=w1_codes[:, places].bitcast(FP8X4),
+                    lhsT_scale=w1_scales[:, places],
                     rhs=x_picked[h][:].bitcast(FP8X4),
                     rhs_scale=x_picked_scales[:, cols],
                     start=True,
@@ -135,30 +143,26 @@ def tile_picked_dmpnn8_none_po_kernel(
         z_scales = keep.tile([P, S], U8, align_bytes=64)
         o_codes = keep.tile([P, S], U32, align_bytes=64)
         o_scales = keep.tile([P, S], U8, align_bytes=64)
-        out_rows = out_0.rearrange("(p t) j -> p t j", t=PACK)
+        o_grouped = [keep.tile([P, HALF, PACK], BF16, name="o_grouped%d" % h, align_bytes=64) for h in range(2)]
+        out_planes = out_0.rearrange("(p t) j -> p t j", t=PACK)
         out_words = out_1[0].rearrange("p c r -> p (c r)").bitcast(I32)
-
-        def weights(w, t):
-            return dict(
-                lhsT=dealt_words[w][:, 2 * P * t : 2 * P * (t + 1)].bitcast(FP4X4),
-                lhsT_scale=dealt_scales[w][:, P * t : P * (t + 1)],
-            )
-
-        def looked_up(t, name, start, width):
-            return y[t][:].indirect(entries(lists[name], start, width))
 
         def messages(start, width):
             cols = slice(start, start + width)
             z = keep.tile([P, PACK, width], F32, name="z", align_bytes=64)
             for planes in ((0, 1), (2, 3)) if start == 0 else ((0, 1, 2, 3),):
-                first = {t: keep.tile([P, width], F32, name="first%d" % t, align_bytes=64) for t in planes}
-                second = {t: keep.tile([P, width], F32, name="second%d" % t, align_bytes=64) for t in planes}
+                back = {t: keep.tile([P, width], F32, name="back%d" % t, align_bytes=64) for t in planes}
+                diff = {t: keep.tile([P, width], F32, name="diff%d" % t, align_bytes=64) for t in planes}
                 for t in planes:
-                    nc.vector.tensor_copy(first[t][:], looked_up(t, "rev", start, width))
+                    nc.vector.tensor_copy(back[t][:], y[t][:].indirect(entries(rev_list, start, width)))
                 for t in planes:
-                    nc.vector.tensor_tensor(second[t][:], looked_up(t, "in2", start, width), first[t][:], SUBTRACT)
+                    nc.vector.tensor_tensor(
+                        diff[t][:], y[t][:].indirect(entries(in2_list, start, width)), back[t][:], SUBTRACT
+                    )
                 for t in planes:
-                    nc.vector.tensor_tensor(z[:, t, :], looked_up(t, "in1", start, width), second[t][:], ADD)
+                    nc.vector.tensor_tensor(
+                        z[:, t, :], y[t][:].indirect(entries(in1_list, start, width)), diff[t][:], ADD
+                    )
             z_grouped = ring.tile([P, width, PACK], BF16, name="z_grouped", align_bytes=64)
             interleave(nc.vector.tensor_copy if cols.stop == S else nc.scalar.copy, z_grouped[:], z[:])
             nc.vector.quantize_mx(
@@ -167,28 +171,28 @@ def tile_picked_dmpnn8_none_po_kernel(
                 in_=z_grouped[:].rearrange("p c t -> p (c t)"),
             )
 
-        def first_pass(bank, t, c0):
+        def h0_pass(target, t, c0):
             h, within = divmod(c0, HALF)
             nc.tensor.matmul_mx(
-                out=bank,
+                out=target,
+                lhsT=dealt_words[0][:, 2 * P * t : 2 * P * (t + 1)].bitcast(FP4X4),
+                lhsT_scale=dealt_scales[0][:, P * t : P * (t + 1)],
                 rhs=x_picked[h][:, within : within + BLOCK].bitcast(FP8X4),
                 rhs_scale=x_picked_scales[:, c0 : c0 + BLOCK],
                 start=True,
                 stop=False,
-                **weights(0, t),
             )
 
-        def second_pass(bank, t, c0):
+        def z_pass(target, t, c0):
             nc.tensor.matmul_mx(
-                out=bank,
+                out=target,
+                lhsT=dealt_words[1][:, 2 * P * t : 2 * P * (t + 1)].bitcast(FP4X4),
+                lhsT_scale=dealt_scales[1][:, P * t : P * (t + 1)],
                 rhs=z_codes[:, c0 : c0 + BLOCK].bitcast(FP8X4),
                 rhs_scale=z_scales[:, c0 : c0 + BLOCK],
                 start=False,
                 stop=True,
-                **weights(1, t),
             )
-
-        o_grouped = [keep.tile([P, HALF, PACK], BF16, name="o_grouped%d" % h, align_bytes=64) for h in range(2)]
 
         def results(start, width):
             o = keep.tile([P, PACK, width], F32, name="o%d" % start, align_bytes=64)
@@ -198,19 +202,20 @@ def tile_picked_dmpnn8_none_po_kernel(
                 if c0 + BLOCK < S:
                     bank = psum.tile([P, PACK, BLOCK], F32, name="o_bank", tag="bank%d" % (c0 // BLOCK))
                     for t in range(PACK):
-                        first_pass(bank[:, t, :], t, c0)
-                        second_pass(bank[:, t, :], t, c0)
-                    nc.scalar.copy(rounded, bank[:].rearrange("p t c -> p c t"))
+                        h0_pass(bank[:, t, :], t, c0)
+                        z_pass(bank[:, t, :], t, c0)
                     nc.scalar.copy(o[:, :, c0 - start : c0 - start + BLOCK], bank[:])
+                    nc.scalar.copy(rounded, bank[:].rearrange("p t c -> p c t"))
                 else:
                     banks = [psum.tile([P, BLOCK], F32, name="o_bank", tag="bank%d" % t) for t in range(PACK)]
                     for t in range(PACK):
-                        first_pass(banks[t][:], t, c0)
+                        h0_pass(banks[t][:], t, c0)
                     for t in range(PACK):
-                        second_pass(banks[t][:], t, c0)
-                        nc.vector.tensor_copy(o[:, t, :], banks[t][:])
+                        z_pass(banks[t][:], t, c0)
+                        drain = nc.vector.tensor_copy if t % 2 else nc.scalar.copy
+                        drain(o[:, t, :], banks[t][:])
                     interleave(nc.vector.tensor_copy, rounded, o[:])
-            nc.sync.dma_start(out_rows[:, :, start : start + width], o[:])
+            nc.sync.dma_start(out_planes[:, :, start : start + width], o[:])
             if (start + width) % HALF == 0:
                 h = start // HALF
                 cols = slice(h * HALF, (h + 1) * HALF)
@@ -226,7 +231,8 @@ def tile_picked_dmpnn8_none_po_kernel(
             if n + 1 < len(CHUNKS):
                 messages(*CHUNKS[n + 1])
             results(*chunk)
-        for q in range(4):
+
+        for q in range(QUADRANTS):
             queue = nc.scalar if q % 2 else nc.sync
             queue.dma_start(
                 out_2[0, 4 * q : 4 * q + 4, :].bitcast(I32), o_scales[32 * q : 32 * q + 4, :].bitcast(I32)

@@ -44,8 +44,7 @@ def tile_picked_dmpnn8_none_po_kernel(
     nc = tc.nc
     with ExitStack() as ctx:
         keep = ctx.enter_context(tc.tile_pool(name="keep", bufs=1))
-        ring = ctx.enter_context(tc.tile_pool(name="ring", bufs=2))
-        psum = ctx.enter_context(tc.psum_pool(name="psum", bufs=2))
+        psum = ctx.enter_context(tc.psum_pool(name="psum", bufs=1))
 
         x_scale_table = keep.tile([P, T], U8, align_bytes=64)
         nc.gpsimd.memset(x_scale_table[:].bitcast(I32), 0)
@@ -55,84 +54,95 @@ def tile_picked_dmpnn8_none_po_kernel(
             nc.vector.memset(scale_tile[:].bitcast(I32), 0)
             raw_scales.append(scale_tile)
 
-        raw_words = []
-        for name, words in (("w2", w2_words), ("w3", w3_words)):
-            word_tile = keep.tile([P, 2 * N], U8, name=name + "_raw_words", align_bytes=64)
-            nc.sync.dma_start(word_tile[:].bitcast(I32), words[0].bitcast(I32))
-            raw_words.append(word_tile)
-        picked = keep.tile([P, S // GROUP], U16)
-        nc.sync.dma_start(picked[:], offs)
-        load_scale_rows(nc.scalar, x_scale_table, x_scales[0])
-        w1_rows = w1.rearrange("(p j) c -> p j c", j=PACK)
-        w1_raw = []
-        for h in range(2):
-            w1_half = keep.tile([P, PACK, H // 2], F32, name="w1_raw%d" % h, align_bytes=64)
-            nc.sync.dma_start(w1_half[:], w1_rows[:, :, h * (H // 2) : (h + 1) * (H // 2)])
-            w1_raw.append(w1_half)
-        x_table = keep.tile([P, T], U32, tag="x_table", align_bytes=64)
-        nc.sync.dma_start(x_table[:].bitcast(I32), x_words[0].rearrange("p c r -> p (c r)").bitcast(I32))
-
         def load_list(name, source):
             list_tile = keep.tile([P, S // GROUP], U16, name=name + "_list")
             nc.sync.dma_start(list_tile[:], source)
             return list_tile
 
-        rev_list = load_list("rev", rev)
+        def load_words(name, words):
+            word_tile = keep.tile([P, 2 * N], U8, name=name + "_raw_words", align_bytes=64)
+            nc.sync.dma_start(word_tile[:].bitcast(I32), words[0].bitcast(I32))
+            return word_tile
+
+        def deal_words(dealt, raw):
+            nc.vector.tensor_copy(
+                dealt.rearrange("p (t g i b) -> p g t i b", t=PACK, i=8, b=2),
+                raw[:].rearrange("p (g i t b) -> p g t i b", t=PACK, i=8, b=2),
+            )
+
+        def deal_scales(dealt, raw):
+            nc.vector.tensor_copy(
+                dealt.rearrange("p (t g i) -> p g t i", t=PACK, i=16),
+                raw[:].rearrange("p (g i t) -> p g t i", t=PACK, i=16),
+            )
+
+        picked = load_list("picked", offs)
+        w2_raw = load_words("w2", w2_words)
+        w1_rows = w1.rearrange("(p j) c -> p j c", j=PACK)
+        w1_raw = [keep.tile([P, PACK, H // 2], F32, name="w1_raw%d" % h, align_bytes=64) for h in range(2)]
+        x_table = keep.tile([P, T], U32, align_bytes=64)
+        nc.sync.dma_start(w1_raw[0][:], w1_rows[:, :, : H // 2])
+        load_scale_rows(nc.sync, x_scale_table, x_scales[0])
+        nc.sync.dma_start(x_table[:].bitcast(I32), x_words[0].rearrange("p c r -> p (c r)").bitcast(I32))
+        nc.sync.dma_start(w1_raw[1][:], w1_rows[:, :, H // 2 :])
+        w3_raw = load_words("w3", w3_words)
         load_scale_rows(nc.sync, raw_scales[1], w3_scales[0])
+        rev_list = load_list("rev", rev)
         in2_list = load_list("in2", in2)
         in1_list = load_list("in1", in1)
         load_scale_rows(nc.gpsimd, raw_scales[0], w2_scales[0])
 
-        dealt_words = []
-        for w in range(2):
-            dealt = keep.tile([P, 2 * N], U8, name="dealt_words%d" % w, align_bytes=64)
-            nc.vector.tensor_copy(
-                dealt[:].rearrange("p (t g i b) -> p g t i b", t=PACK, i=8, b=2),
-                raw_words[w][:].rearrange("p (g i t b) -> p g t i b", t=PACK, i=8, b=2),
-            )
-            dealt_words.append(dealt)
-
+        w2_dealt = keep.tile([P, 2 * N], U8, align_bytes=64)
+        deal_words(w2_dealt[:], w2_raw)
         x_picked_scales = keep.tile([P, S], U8, align_bytes=64)
         nc.vector.tensor_copy(x_picked_scales[:], x_scale_table[:].indirect(picked[:]))
 
         w1_codes = keep.tile([P, H], U32, align_bytes=64)
         w1_scales = keep.tile([P, H], U8, align_bytes=64)
-        for u, cast in enumerate((nc.scalar.copy, nc.vector.tensor_copy)):
-            grouped = keep.tile([P, 2 * H], BF16, name="w1_grouped", tag="w1_grouped%d" % u, align_bytes=64)
-            target = grouped[:].rearrange("p (t m j) -> p m j t", t=2, j=PACK)
-            for h in range(2):
-                source = w1_raw[h][:].rearrange("p j (m t) -> p m j t", t=PACK)
-                cast(target[:, h * (P // 2) : (h + 1) * (P // 2), :, :], source[:, :, :, 2 * u : 2 * u + 2])
-            places = slice(2 * P * u, 2 * P * (u + 1))
-            nc.vector.quantize_mx(out=w1_codes[:, places].bitcast(FP8X4), scales=w1_scales[:, places], in_=grouped[:])
-
-        x_picked = [
-            keep.tile([P, HALF], U32, name="x_picked", tag="w1_grouped%d" % h, align_bytes=64) for h in range(2)
+        grouped = [
+            keep.tile([P, 2 * H], BF16, name="w1_grouped", tag="w1_grouped%d" % u, align_bytes=64) for u in range(2)
         ]
-        y = [keep.tile([P, S], F32, name="y%d" % t, align_bytes=64) for t in range(PACK)]
-        for h in range(2):
-            nc.vector.tensor_copy(x_picked[h][:], x_table[:].indirect(entries(picked, h * HALF, HALF)))
 
-        both_scales = keep.tile([P, 2 * N], U8, tag="x_table", align_bytes=64)
-        dealt_scales = []
-        for w in range(2):
-            part = both_scales[:, w * N : (w + 1) * N]
-            nc.vector.tensor_copy(
-                part.rearrange("p (t g i) -> p g t i", t=PACK, i=16),
-                raw_scales[w][:].rearrange("p (g i t) -> p g t i", t=PACK, i=16),
+        def round_w1(h):
+            source = w1_raw[h][:].rearrange("p j (m t) -> p m j t", t=PACK)
+            for u, cast in enumerate((nc.vector.tensor_copy, nc.scalar.copy)):
+                target = grouped[u][:].rearrange("p (t m j) -> p m j t", t=2, j=PACK)
+                cast(target[:, h * (P // 2) : (h + 1) * (P // 2), :, :], source[:, :, :, 2 * u : 2 * u + 2])
+
+        round_w1(0)
+        x_picked = keep.tile([P, S], U32, align_bytes=64)
+        nc.vector.tensor_copy(x_picked[:], x_table[:].indirect(picked[:]))
+        round_w1(1)
+        for first, count in ((0, 1), (1, 1), (2, 2)):
+            places = slice(first * P, (first + count) * P)
+            u, within = divmod(first, 2)
+            nc.vector.quantize_mx(
+                out=w1_codes[:, places].bitcast(FP8X4),
+                scales=w1_scales[:, places],
+                in_=grouped[u][:, within * H : (within + count) * H],
             )
-            dealt_scales.append(part)
 
+        dealt = keep.tile([P, 4 * N], U8, tag="w1_grouped0", align_bytes=64)
+        dealt_words = [w2_dealt[:], dealt[:, : 2 * N]]
+        dealt_scales = [dealt[:, (2 + w) * N : (3 + w) * N] for w in range(2)]
+        deal_words(dealt_words[1], w3_raw)
+        deal_scales(dealt_scales[1], raw_scales[1])
+        deal_scales(dealt_scales[0], raw_scales[0])
+
+        y = [keep.tile([P, S], F32, name="y%d" % t, align_bytes=64) for t in range(PACK)]
+        banks_used = 0
         for t in range(PACK):
             places = slice(t * P, (t + 1) * P)
-            for h in range(2):
-                cols = slice(h * HALF, (h + 1) * HALF)
-                bank = psum.tile([P, HALF], F32, name="y_bank", tag="bank%d" % t)
+            width = HALF if t == 0 else S
+            for c0 in range(0, S, width):
+                cols = slice(c0, c0 + width)
+                bank = psum.tile([P, width], F32, name="y_bank", tag="bank%d" % banks_used)
+                banks_used = banks_used + 1
                 nc.tensor.matmul_mx(
                     out=bank[:],
                     lhsT=w1_codes[:, places].bitcast(FP8X4),
                     lhsT_scale=w1_scales[:, places],
-                    rhs=x_picked[h][:].bitcast(FP8X4),
+                    rhs=x_picked[:, cols].bitcast(FP8X4),
                     rhs_scale=x_picked_scales[:, cols],
                     start=True,
                     stop=True,
@@ -143,41 +153,48 @@ def tile_picked_dmpnn8_none_po_kernel(
         z_scales = keep.tile([P, S], U8, align_bytes=64)
         o_codes = keep.tile([P, S], U32, align_bytes=64)
         o_scales = keep.tile([P, S], U8, align_bytes=64)
-        o_grouped = [keep.tile([P, HALF, PACK], BF16, name="o_grouped%d" % h, align_bytes=64) for h in range(2)]
         out_planes = out_0.rearrange("(p t) j -> p t j", t=PACK)
         out_words = out_1[0].rearrange("p c r -> p (c r)").bitcast(I32)
 
+        back = {}
+
+        def reverse_messages(h, t, tag):
+            back[h, t] = keep.tile([P, HALF], F32, name="back", tag=tag, align_bytes=64)
+            nc.vector.tensor_copy(back[h, t][:], y[t][:].indirect(entries(rev_list, h * HALF, HALF)))
+
         def messages(start, width):
-            cols = slice(start, start + width)
-            z = keep.tile([P, PACK, width], F32, name="z", align_bytes=64)
-            for planes in ((0, 1), (2, 3)) if start == 0 else ((0, 1, 2, 3),):
-                back = {t: keep.tile([P, width], F32, name="back%d" % t, align_bytes=64) for t in planes}
-                diff = {t: keep.tile([P, width], F32, name="diff%d" % t, align_bytes=64) for t in planes}
-                for t in planes:
-                    nc.vector.tensor_copy(back[t][:], y[t][:].indirect(entries(rev_list, start, width)))
-                for t in planes:
-                    nc.vector.tensor_tensor(
-                        diff[t][:], y[t][:].indirect(entries(in2_list, start, width)), back[t][:], SUBTRACT
-                    )
-                for t in planes:
-                    nc.vector.tensor_tensor(
-                        z[:, t, :], y[t][:].indirect(entries(in1_list, start, width)), diff[t][:], ADD
-                    )
-            z_grouped = ring.tile([P, width, PACK], BF16, name="z_grouped", align_bytes=64)
-            interleave(nc.vector.tensor_copy if cols.stop == S else nc.scalar.copy, z_grouped[:], z[:])
-            nc.vector.quantize_mx(
-                out=z_codes[:, cols].bitcast(FP8X4),
-                scales=z_scales[:, cols],
-                in_=z_grouped[:].rearrange("p c t -> p (c t)"),
-            )
+            h, within = divmod(start, HALF)
+            diff = [keep.tile([P, width], F32, name="diff", tag="diff%d_%d" % (h, t), align_bytes=64) for t in range(PACK)]
+            z = keep.tile([P, PACK, width], F32, name="z%d" % start, align_bytes=64)
+            for t in range(PACK):
+                nc.vector.tensor_tensor(
+                    diff[t][:],
+                    y[t][:].indirect(entries(in2_list, start, width)),
+                    back[h, t][:, within : within + width],
+                    SUBTRACT,
+                )
+            for t in range(PACK):
+                nc.vector.tensor_tensor(
+                    z[:, t, :], y[t][:].indirect(entries(in1_list, start, width)), diff[t][:], ADD
+                )
+            for c0 in range(start, start + width, BLOCK):
+                cols = slice(c0, c0 + BLOCK)
+                z_grouped = keep.tile([P, BLOCK, PACK], BF16, name="z_grouped%d" % c0, align_bytes=64)
+                copy = nc.vector.tensor_copy if cols.stop == S else nc.scalar.copy
+                interleave(copy, z_grouped[:], z[:, :, c0 - start : c0 - start + BLOCK])
+                nc.vector.quantize_mx(
+                    out=z_codes[:, cols].bitcast(FP8X4),
+                    scales=z_scales[:, cols],
+                    in_=z_grouped[:].rearrange("p c t -> p (c t)"),
+                )
+            return z
 
         def h0_pass(target, t, c0):
-            h, within = divmod(c0, HALF)
             nc.tensor.matmul_mx(
                 out=target,
                 lhsT=dealt_words[0][:, 2 * P * t : 2 * P * (t + 1)].bitcast(FP4X4),
                 lhsT_scale=dealt_scales[0][:, P * t : P * (t + 1)],
-                rhs=x_picked[h][:, within : within + BLOCK].bitcast(FP8X4),
+                rhs=x_picked[:, c0 : c0 + BLOCK].bitcast(FP8X4),
                 rhs_scale=x_picked_scales[:, c0 : c0 + BLOCK],
                 start=True,
                 stop=False,
@@ -194,43 +211,46 @@ def tile_picked_dmpnn8_none_po_kernel(
                 stop=True,
             )
 
-        def results(start, width):
-            o = keep.tile([P, PACK, width], F32, name="o%d" % start, align_bytes=64)
-            for c0 in range(start, start + width, BLOCK):
-                h, within = divmod(c0, HALF)
-                rounded = o_grouped[h][:, within : within + BLOCK, :]
-                if c0 + BLOCK < S:
-                    bank = psum.tile([P, PACK, BLOCK], F32, name="o_bank", tag="bank%d" % (c0 // BLOCK))
-                    for t in range(PACK):
-                        h0_pass(bank[:, t, :], t, c0)
-                        z_pass(bank[:, t, :], t, c0)
-                    nc.scalar.copy(o[:, :, c0 - start : c0 - start + BLOCK], bank[:])
-                    nc.scalar.copy(rounded, bank[:].rearrange("p t c -> p c t"))
-                else:
-                    banks = [psum.tile([P, BLOCK], F32, name="o_bank", tag="bank%d" % t) for t in range(PACK)]
-                    for t in range(PACK):
-                        h0_pass(banks[t][:], t, c0)
-                    for t in range(PACK):
-                        z_pass(banks[t][:], t, c0)
-                        drain = nc.vector.tensor_copy if t % 2 else nc.scalar.copy
-                        drain(o[:, t, :], banks[t][:])
-                    interleave(nc.vector.tensor_copy, rounded, o[:])
-            nc.sync.dma_start(out_planes[:, :, start : start + width], o[:])
-            if (start + width) % HALF == 0:
-                h = start // HALF
-                cols = slice(h * HALF, (h + 1) * HALF)
-                nc.vector.quantize_mx(
-                    out=o_codes[:, cols].bitcast(FP8X4),
-                    scales=o_scales[:, cols],
-                    in_=o_grouped[h][:].rearrange("p c t -> p (c t)"),
-                )
-                nc.sync.dma_start(out_words[:, cols], o_codes[:, cols].bitcast(I32))
+        def results(c0):
+            cols = slice(c0, c0 + BLOCK)
+            block = c0 // BLOCK
+            both = keep.tile([P, 6 * BLOCK], F32, name="z%d" % HALF if block == 1 else "o%d" % c0, align_bytes=64)
+            o = both[:, : PACK * BLOCK].rearrange("p (t c) -> p t c", t=PACK)
+            rounded = both[:, PACK * BLOCK :].bitcast(BF16)
+            o_grouped = rounded.rearrange("p (c t) -> p c t", t=PACK)
+            if cols.stop < S:
+                bank = psum.tile([P, PACK, BLOCK], F32, name="o_bank", tag="bank%d" % (banks_used + block))
+                for t in range(PACK):
+                    h0_pass(bank[:, t, :], t, c0)
+                    z_pass(bank[:, t, :], t, c0)
+                nc.scalar.copy(o, bank[:])
+                copy = nc.vector.tensor_copy if block == 2 else nc.scalar.copy
+                copy(o_grouped, bank[:].rearrange("p t c -> p c t"))
+            else:
+                banks = [psum.tile([P, BLOCK], F32, name="o_bank", tag="bank%d" % t) for t in range(PACK)]
+                for t in range(PACK):
+                    h0_pass(banks[t][:], t, c0)
+                for t in range(PACK):
+                    z_pass(banks[t][:], t, c0)
+                    nc.scalar.copy(o[:, t, :], banks[t][:])
+                interleave(nc.vector.tensor_copy, o_grouped, o)
+            nc.sync.dma_start(out_planes[:, :, cols], o)
+            nc.vector.quantize_mx(out=o_codes[:, cols].bitcast(FP8X4), scales=o_scales[:, cols], in_=rounded)
+            if block % 2:
+                half = slice(cols.stop - HALF, cols.stop)
+                nc.sync.dma_start(out_words[:, half], o_codes[:, half].bitcast(I32))
 
+        for t in range(PACK):
+            reverse_messages(0, t, "back0_%d" % t)
+            if t < 2:
+                reverse_messages(1, t, "back1_%d" % t)
         messages(*CHUNKS[0])
-        for n, chunk in enumerate(CHUNKS):
-            if n + 1 < len(CHUNKS):
-                messages(*CHUNKS[n + 1])
-            results(*chunk)
+        for t in range(2, PACK):
+            reverse_messages(1, t, "diff0_%d" % t)
+        messages(*CHUNKS[1])
+        z_last = messages(*CHUNKS[2])
+        for c0 in range(0, S, BLOCK):
+            results(c0)
 
         for q in range(QUADRANTS):
             queue = nc.scalar if q % 2 else nc.sync

@@ -26,8 +26,8 @@ FLOPS = 2 * K * H * S + 2 * K * N * S + 2 * H * N * S
 
 
 def load_scale_rows(queue, scale_tile, rows):
-    for q in range(QUADRANTS):
-        queue.dma_start(scale_tile[32 * q : 32 * q + 4, :].bitcast(I32), rows[4 * q : 4 * q + 4, :].bitcast(I32))
+    for r in range(4):
+        queue.dma_start(scale_tile[r:P:32, :].bitcast(I32), rows[r:16:4, :].bitcast(I32))
 
 
 def entries(list_tile, start, count):
@@ -236,8 +236,8 @@ def tile_picked_dmpnn8_none_po_kernel(
                 interleave(nc.vector.tensor_copy, o_grouped, o)
             nc.sync.dma_start(out_planes[:, :, cols], o)
             nc.vector.quantize_mx(out=o_codes[:, cols].bitcast(FP8X4), scales=o_scales[:, cols], in_=rounded)
-            if block % 2:
-                half = slice(cols.stop - HALF, cols.stop)
+            if block > 0:
+                half = slice(0 if block == 1 else c0, cols.stop)
                 nc.sync.dma_start(out_words[:, half], o_codes[:, half].bitcast(I32))
 
         for t in range(PACK):
@@ -252,8 +252,6 @@ def tile_picked_dmpnn8_none_po_kernel(
         for c0 in range(0, S, BLOCK):
             results(c0)
 
-        for q in range(QUADRANTS):
-            queue = nc.scalar if q % 2 else nc.sync
-            queue.dma_start(
-                out_2[0, 4 * q : 4 * q + 4, :].bitcast(I32), o_scales[32 * q : 32 * q + 4, :].bitcast(I32)
-            )
+        for r in range(4):
+            queue = nc.scalar if r % 2 else nc.sync
+            queue.dma_start(out_2[0, r:16:4, :].bitcast(I32), o_scales[r:P:32, :].bitcast(I32))

@@ -46,22 +46,23 @@ def tile_picked_dmpnn8_none_po_kernel(
         keep = ctx.enter_context(tc.tile_pool(name="keep", bufs=1))
         psum = ctx.enter_context(tc.psum_pool(name="psum", bufs=1))
 
-        x_scale_table = keep.tile([P, T], U8, align_bytes=64)
-        nc.gpsimd.memset(x_scale_table[:].bitcast(I32), 0)
-        raw_scales = []
-        for name in ("w2", "w3"):
-            scale_tile = keep.tile([P, N], U8, name=name + "_raw_scales", align_bytes=64)
-            nc.vector.memset(scale_tile[:].bitcast(I32), 0)
-            raw_scales.append(scale_tile)
+        x_scale_table = keep.tile([P, T], U8, tag="x_scale_table", align_bytes=64)
+        nc.vector.memset(x_scale_table[:].bitcast(I32), 0)
+        raw_scales = keep.tile([P, 2 * N], U8, align_bytes=64)
+        nc.vector.memset(raw_scales[:].bitcast(I32), 0)
+
+        y_wide = [keep.tile([P, 2 * S], F32, name="y_wide%d" % t, align_bytes=64) for t in range(PACK)]
+        for t in range(PACK):
+            nc.vector.memset(y_wide[t][:, S:], 0.0)
 
         def load_list(name, source):
             list_tile = keep.tile([P, S // GROUP], U16, name=name + "_list")
             nc.sync.dma_start(list_tile[:], source)
             return list_tile
 
-        def load_words(name, words):
+        def load_words(queue, name, words):
             word_tile = keep.tile([P, 2 * N], U8, name=name + "_raw_words", align_bytes=64)
-            nc.sync.dma_start(word_tile[:].bitcast(I32), words[0].bitcast(I32))
+            queue.dma_start(word_tile[:].bitcast(I32), words[0].bitcast(I32))
             return word_tile
 
         def deal_words(dealt, raw):
@@ -70,49 +71,46 @@ def tile_picked_dmpnn8_none_po_kernel(
                 raw[:].rearrange("p (g i t b) -> p g t i b", t=PACK, i=8, b=2),
             )
 
-        def deal_scales(dealt, raw):
-            nc.vector.tensor_copy(
-                dealt.rearrange("p (t g i) -> p g t i", t=PACK, i=16),
-                raw[:].rearrange("p (g i t) -> p g t i", t=PACK, i=16),
-            )
-
-        picked = load_list("picked", offs)
-        w2_raw = load_words("w2", w2_words)
+        w3_raw = load_words(nc.scalar, "w3", w3_words)
         w1_rows = w1.rearrange("(p j) c -> p j c", j=PACK)
-        w1_raw = [keep.tile([P, PACK, H // 2], F32, name="w1_raw%d" % h, align_bytes=64) for h in range(2)]
+        w1_raw = [keep.tile([P, 2, H], F32, name="w1_raw%d" % h, align_bytes=64) for h in range(2)]
         x_table = keep.tile([P, T], U32, align_bytes=64)
-        nc.sync.dma_start(w1_raw[0][:], w1_rows[:, :, : H // 2])
+        nc.sync.dma_start(w1_raw[0][:], w1_rows[:, 0:2, :])
+        picked = load_list("picked", offs)
         load_scale_rows(nc.sync, x_scale_table, x_scales[0])
         nc.sync.dma_start(x_table[:].bitcast(I32), x_words[0].rearrange("p c r -> p (c r)").bitcast(I32))
-        nc.sync.dma_start(w1_raw[1][:], w1_rows[:, :, H // 2 :])
-        w3_raw = load_words("w3", w3_words)
-        load_scale_rows(nc.sync, raw_scales[1], w3_scales[0])
+        nc.sync.dma_start(w1_raw[1][:], w1_rows[:, 2:4, :])
+        w2_raw = load_words(nc.sync, "w2", w2_words)
+        for w, scales in enumerate((w2_scales, w3_scales)):
+            nc.sync.dma_start(raw_scales[0:P:8, w * N : (w + 1) * N].bitcast(I32), scales[0].bitcast(I32))
         rev_list = load_list("rev", rev)
         in2_list = load_list("in2", in2)
         in1_list = load_list("in1", in1)
-        load_scale_rows(nc.gpsimd, raw_scales[0], w2_scales[0])
 
-        w2_dealt = keep.tile([P, 2 * N], U8, align_bytes=64)
-        deal_words(w2_dealt[:], w2_raw)
+        w3_dealt = keep.tile([P, 2 * N], U8, align_bytes=64)
+        deal_words(w3_dealt[:], w3_raw)
         x_picked_scales = keep.tile([P, S], U8, align_bytes=64)
         nc.vector.tensor_copy(x_picked_scales[:], x_scale_table[:].indirect(picked[:]))
 
-        w1_codes = keep.tile([P, H], U32, align_bytes=64)
+        w1_codes = keep.tile([P, H], U32, tag="w1_codes", align_bytes=64)
         w1_scales = keep.tile([P, H], U8, align_bytes=64)
         grouped = [
             keep.tile([P, 2 * H], BF16, name="w1_grouped", tag="w1_grouped%d" % u, align_bytes=64) for u in range(2)
         ]
 
-        def round_w1(h):
-            source = w1_raw[h][:].rearrange("p j (m t) -> p m j t", t=PACK)
-            for u, cast in enumerate((nc.vector.tensor_copy, nc.scalar.copy)):
-                target = grouped[u][:].rearrange("p (t m j) -> p m j t", t=2, j=PACK)
-                cast(target[:, h * (P // 2) : (h + 1) * (P // 2), :, :], source[:, :, :, 2 * u : 2 * u + 2])
+        def round_w1(cast, h, first, count):
+            u, within = divmod(first, 2)
+            source = w1_raw[h][:].rearrange("p j (m t) -> p m t j", t=PACK)
+            target = grouped[u][:].rearrange("p (t m j) -> p m t j", t=2, j=PACK)
+            cast(target[:, :, within : within + count, 2 * h : 2 * h + 2], source[:, :, first : first + count, :])
 
-        round_w1(0)
+        round_w1(nc.vector.tensor_copy, 0, 0, 2)
+        round_w1(nc.scalar.copy, 0, 2, 2)
         x_picked = keep.tile([P, S], U32, align_bytes=64)
         nc.vector.tensor_copy(x_picked[:], x_table[:].indirect(picked[:]))
-        round_w1(1)
+        round_w1(nc.vector.tensor_copy, 1, 0, 1)
+        round_w1(nc.vector.tensor_copy, 1, 1, 1)
+        round_w1(nc.scalar.copy, 1, 2, 2)
         for first, count in ((0, 1), (1, 1), (2, 2)):
             places = slice(first * P, (first + count) * P)
             u, within = divmod(first, 2)
@@ -122,12 +120,17 @@ def tile_picked_dmpnn8_none_po_kernel(
                 in_=grouped[u][:, within * H : (within + count) * H],
             )
 
-        dealt = keep.tile([P, 4 * N], U8, tag="w1_grouped0", align_bytes=64)
-        dealt_words = [w2_dealt[:], dealt[:, : 2 * N]]
-        dealt_scales = [dealt[:, (2 + w) * N : (3 + w) * N] for w in range(2)]
-        deal_words(dealt_words[1], w3_raw)
-        deal_scales(dealt_scales[1], raw_scales[1])
-        deal_scales(dealt_scales[0], raw_scales[0])
+        late = keep.tile([P, 4 * N], U8, tag="w1_grouped0", align_bytes=64)
+        w2_dealt, w_scales = late[:, : 2 * N], late[:, 2 * N :]
+        deal_words(w2_dealt, w2_raw)
+        nc.vector.tensor_copy(
+            w_scales.rearrange("p (w t g i) -> p w g t i", w=2, t=PACK, i=16),
+            raw_scales[:].rearrange("p (w g i t) -> p w g t i", w=2, t=PACK, i=16),
+        )
+        for r in range(1, 4):
+            nc.sync.dma_start(late[r:P:32, 2 * N :].bitcast(I32), late[8 * r : P : 32, 2 * N :].bitcast(I32))
+        dealt_words = [w2_dealt, w3_dealt[:]]
+        dealt_scales = [w_scales[:, w * N : (w + 1) * N] for w in range(2)]
 
         y = [keep.tile([P, S], F32, name="y%d" % t, align_bytes=64) for t in range(PACK)]
         banks_used = 0
@@ -147,7 +150,10 @@ def tile_picked_dmpnn8_none_po_kernel(
                     start=True,
                     stop=True,
                 )
-                nc.scalar.copy(y[t][:, cols], bank[:])
+                nc.scalar.copy(y_wide[t][:, cols], bank[:])
+
+        for t in range(PACK):
+            nc.scalar.copy(y[t][:], y_wide[t][:, :S])
 
         z_codes = keep.tile([P, S], U32, align_bytes=64)
         z_scales = keep.tile([P, S], U8, align_bytes=64)
@@ -156,32 +162,42 @@ def tile_picked_dmpnn8_none_po_kernel(
         out_planes = out_0.rearrange("(p t) j -> p t j", t=PACK)
         out_words = out_1[0].rearrange("p c r -> p (c r)").bitcast(I32)
 
-        back = {}
+        back = [keep.tile([P, S], F32, name="back%d" % t, align_bytes=64) for t in range(PACK)]
+        diff = keep.tile([P, PACK, S - BLOCK], F32, tag="w1_codes", align_bytes=64)
 
-        def reverse_messages(h, t, tag):
-            back[h, t] = keep.tile([P, HALF], F32, name="back", tag=tag, align_bytes=64)
-            nc.vector.tensor_copy(back[h, t][:], y[t][:].indirect(entries(rev_list, h * HALF, HALF)))
+        def interleave_by_pairs(dst, src):
+            for u in range(2):
+                pair = slice(2 * u, 2 * u + 2)
+                nc.vector.tensor_copy(dst[:, :, pair], src[:, pair, :].rearrange("p t c -> p c t"))
 
-        def messages(start, width):
-            h, within = divmod(start, HALF)
-            diff = [keep.tile([P, width], F32, name="diff", tag="diff%d_%d" % (h, t), align_bytes=64) for t in range(PACK)]
-            z = keep.tile([P, PACK, width], F32, name="z%d" % start, align_bytes=64)
+        def window(t, width):
+            return y[t][:] if width == BLOCK else y_wide[t][:]
+
+        def subtract_back(start, width, diff):
             for t in range(PACK):
                 nc.vector.tensor_tensor(
-                    diff[t][:],
-                    y[t][:].indirect(entries(in2_list, start, width)),
-                    back[h, t][:, within : within + width],
+                    diff[:, t, :width],
+                    window(t, width).indirect(entries(in2_list, start, width)),
+                    back[t][:, start : start + width],
                     SUBTRACT,
                 )
+
+        def messages(start, width, diff, place):
+            z = keep.tile([P, PACK, width], F32, name="z", tag="z%d" % (start // HALF), align_bytes=64)
             for t in range(PACK):
                 nc.vector.tensor_tensor(
-                    z[:, t, :], y[t][:].indirect(entries(in1_list, start, width)), diff[t][:], ADD
+                    z[:, t, :],
+                    window(t, width).indirect(entries(in1_list, start, width)),
+                    diff[:, t, place : place + width],
+                    ADD,
                 )
             for c0 in range(start, start + width, BLOCK):
                 cols = slice(c0, c0 + BLOCK)
                 z_grouped = keep.tile([P, BLOCK, PACK], BF16, name="z_grouped%d" % c0, align_bytes=64)
-                copy = nc.vector.tensor_copy if cols.stop == S else nc.scalar.copy
-                interleave(copy, z_grouped[:], z[:, :, c0 - start : c0 - start + BLOCK])
+                if cols.stop == S:
+                    interleave_by_pairs(z_grouped[:], z[:])
+                else:
+                    interleave(nc.scalar.copy, z_grouped[:], z[:, :, c0 - start : c0 - start + BLOCK])
                 nc.vector.quantize_mx(
                     out=z_codes[:, cols].bitcast(FP8X4),
                     scales=z_scales[:, cols],
@@ -214,7 +230,7 @@ def tile_picked_dmpnn8_none_po_kernel(
         def results(c0):
             cols = slice(c0, c0 + BLOCK)
             block = c0 // BLOCK
-            both = keep.tile([P, 6 * BLOCK], F32, name="z%d" % HALF if block == 1 else "o%d" % c0, align_bytes=64)
+            both = keep.tile([P, 6 * BLOCK], F32, name="o%d" % c0, align_bytes=64)
             o = both[:, : PACK * BLOCK].rearrange("p (t c) -> p t c", t=PACK)
             rounded = both[:, PACK * BLOCK :].bitcast(BF16)
             o_grouped = rounded.rearrange("p (c t) -> p c t", t=PACK)
@@ -233,22 +249,20 @@ def tile_picked_dmpnn8_none_po_kernel(
                 for t in range(PACK):
                     z_pass(banks[t][:], t, c0)
                     nc.scalar.copy(o[:, t, :], banks[t][:])
-                interleave(nc.vector.tensor_copy, o_grouped, o)
-            nc.sync.dma_start(out_planes[:, :, cols], o)
+                interleave_by_pairs(o_grouped, o)
+            (nc.scalar if cols.stop == S else nc.sync).dma_start(out_planes[:, :, cols], o)
             nc.vector.quantize_mx(out=o_codes[:, cols].bitcast(FP8X4), scales=o_scales[:, cols], in_=rounded)
             if block > 0:
                 half = slice(0 if block == 1 else c0, cols.stop)
                 nc.sync.dma_start(out_words[:, half], o_codes[:, half].bitcast(I32))
 
         for t in range(PACK):
-            reverse_messages(0, t, "back0_%d" % t)
-            if t < 2:
-                reverse_messages(1, t, "back1_%d" % t)
-        messages(*CHUNKS[0])
-        for t in range(2, PACK):
-            reverse_messages(1, t, "diff0_%d" % t)
-        messages(*CHUNKS[1])
-        z_last = messages(*CHUNKS[2])
+            nc.vector.tensor_copy(back[t][:], y_wide[t][:].indirect(rev_list[:]))
+        subtract_back(0, S - BLOCK, diff)
+        z_first = messages(0, HALF, diff, 0)
+        messages(HALF, BLOCK, diff, HALF)
+        subtract_back(S - BLOCK, BLOCK, z_first)
+        z_last = messages(S - BLOCK, BLOCK, z_first, 0)
         for c0 in range(0, S, BLOCK):
             results(c0)
 

@@ -48,12 +48,15 @@ def tile_picked_dmpnn8_none_po_kernel(
 
         x_scale_table = keep.tile([P, T], U8, tag="x_scale_table", align_bytes=64)
         nc.vector.memset(x_scale_table[:].bitcast(I32), 0)
-        raw_scales = keep.tile([P, 2 * N], U8, align_bytes=64)
+        raw_scales = keep.tile([P, N], U8, tag="raw_scales", align_bytes=64)
         nc.vector.memset(raw_scales[:].bitcast(I32), 0)
+        w3_plane = keep.tile([P, N], U8, align_bytes=64)
+        nc.vector.memset(w3_plane[:].bitcast(I32), 0)
 
         y_wide = [keep.tile([P, 2 * S], F32, name="y_wide%d" % t, align_bytes=64) for t in range(PACK)]
-        for t in range(PACK):
-            nc.vector.memset(y_wide[t][:, S:], 0.0)
+        nc.vector.memset(y_wide[0][:, S:], 0.0)
+        for t in range(1, PACK):
+            nc.scalar.copy(y_wide[t][:, S:], y_wide[0][:, S:])
 
         def load_list(name, source):
             list_tile = keep.tile([P, S // GROUP], U16, name=name + "_list")
@@ -67,28 +70,26 @@ def tile_picked_dmpnn8_none_po_kernel(
 
         def deal_words(dealt, raw):
             nc.vector.tensor_copy(
-                dealt.rearrange("p (t g i b) -> p g t i b", t=PACK, i=8, b=2),
-                raw[:].rearrange("p (g i t b) -> p g t i b", t=PACK, i=8, b=2),
+                dealt.bitcast(U16).rearrange("p (t g i) -> p g t i", t=PACK, i=8),
+                raw[:].bitcast(U16).rearrange("p (g i t) -> p g t i", t=PACK, i=8),
             )
 
-        w3_raw = load_words(nc.scalar, "w3", w3_words)
         w1_rows = w1.rearrange("(p j) c -> p j c", j=PACK)
         w1_raw = [keep.tile([P, 2, H], F32, name="w1_raw%d" % h, align_bytes=64) for h in range(2)]
-        x_table = keep.tile([P, T], U32, align_bytes=64)
+        x_table = keep.tile([P, T], U32, tag="x_table", align_bytes=64)
         nc.sync.dma_start(w1_raw[0][:], w1_rows[:, 0:2, :])
         picked = load_list("picked", offs)
         load_scale_rows(nc.sync, x_scale_table, x_scales[0])
         nc.sync.dma_start(x_table[:].bitcast(I32), x_words[0].rearrange("p c r -> p (c r)").bitcast(I32))
         nc.sync.dma_start(w1_raw[1][:], w1_rows[:, 2:4, :])
         w2_raw = load_words(nc.sync, "w2", w2_words)
+        w3_raw = load_words(nc.sync, "w3", w3_words)
         for w, scales in enumerate((w2_scales, w3_scales)):
-            nc.sync.dma_start(raw_scales[0:P:8, w * N : (w + 1) * N].bitcast(I32), scales[0].bitcast(I32))
+            nc.sync.dma_start(raw_scales[4 * w : P : 8, :].bitcast(I32), scales[0].bitcast(I32))
         rev_list = load_list("rev", rev)
         in2_list = load_list("in2", in2)
         in1_list = load_list("in1", in1)
 
-        w3_dealt = keep.tile([P, 2 * N], U8, align_bytes=64)
-        deal_words(w3_dealt[:], w3_raw)
         x_picked_scales = keep.tile([P, S], U8, align_bytes=64)
         nc.vector.tensor_copy(x_picked_scales[:], x_scale_table[:].indirect(picked[:]))
 
@@ -120,24 +121,26 @@ def tile_picked_dmpnn8_none_po_kernel(
                 in_=grouped[u][:, within * H : (within + count) * H],
             )
 
-        late = keep.tile([P, 4 * N], U8, tag="w1_grouped0", align_bytes=64)
-        w2_dealt, w_scales = late[:, : 2 * N], late[:, 2 * N :]
+        late = keep.tile([P, 5 * N], U8, tag="w1_grouped0", align_bytes=64)
+        w2_dealt, w3_dealt, w_scales = late[:, : 2 * N], late[:, 2 * N : 4 * N], late[:, 4 * N :]
         deal_words(w2_dealt, w2_raw)
+        deal_words(w3_dealt, w3_raw)
         nc.vector.tensor_copy(
-            w_scales.rearrange("p (w t g i) -> p w g t i", w=2, t=PACK, i=16),
-            raw_scales[:].rearrange("p (w g i t) -> p w g t i", w=2, t=PACK, i=16),
+            w_scales.rearrange("p (t g i) -> p g t i", t=PACK, i=16),
+            raw_scales[:].rearrange("p (g i t) -> p g t i", t=PACK, i=16),
         )
         for r in range(1, 4):
-            nc.sync.dma_start(late[r:P:32, 2 * N :].bitcast(I32), late[8 * r : P : 32, 2 * N :].bitcast(I32))
-        dealt_words = [w2_dealt, w3_dealt[:]]
-        dealt_scales = [w_scales[:, w * N : (w + 1) * N] for w in range(2)]
+            nc.sync.dma_start(late[r:P:32, 4 * N :].bitcast(I32), late[8 * r : P : 32, 4 * N :].bitcast(I32))
+        for r in range(4):
+            nc.sync.dma_start(w3_plane[r:P:32, :].bitcast(I32), late[8 * r + 4 : P : 32, 4 * N :].bitcast(I32))
+        dealt_words = [w2_dealt, w3_dealt]
+        dealt_scales = [w_scales, w3_plane[:]]
 
         y = [keep.tile([P, S], F32, name="y%d" % t, align_bytes=64) for t in range(PACK)]
         banks_used = 0
         for t in range(PACK):
             places = slice(t * P, (t + 1) * P)
-            width = HALF if t == 0 else S
-            for c0 in range(0, S, width):
+            for c0, width in ((0, HALF), (HALF, HALF)) if t == 0 else ((0, S),):
                 cols = slice(c0, c0 + width)
                 bank = psum.tile([P, width], F32, name="y_bank", tag="bank%d" % banks_used)
                 banks_used = banks_used + 1
@@ -162,7 +165,10 @@ def tile_picked_dmpnn8_none_po_kernel(
         out_planes = out_0.rearrange("(p t) j -> p t j", t=PACK)
         out_words = out_1[0].rearrange("p c r -> p (c r)").bitcast(I32)
 
-        back = [keep.tile([P, S], F32, name="back%d" % t, align_bytes=64) for t in range(PACK)]
+        back = [
+            keep.tile([P, S], F32, name="back", tag="back%d" % t, align_bytes=64)
+            for t in range(PACK)
+        ]
         diff = keep.tile([P, PACK, S - BLOCK], F32, tag="w1_codes", align_bytes=64)
 
         def interleave_by_pairs(dst, src):
@@ -235,7 +241,7 @@ def tile_picked_dmpnn8_none_po_kernel(
             rounded = both[:, PACK * BLOCK :].bitcast(BF16)
             o_grouped = rounded.rearrange("p (c t) -> p c t", t=PACK)
             if cols.stop < S:
-                bank = psum.tile([P, PACK, BLOCK], F32, name="o_bank", tag="bank%d" % (banks_used + block))
+                bank = psum.tile([P, PACK, BLOCK], F32, name="o_bank", tag="bank%d" % (7 - block))
                 for t in range(PACK):
                     h0_pass(bank[:, t, :], t, c0)
                     z_pass(bank[:, t, :], t, c0)
@@ -252,8 +258,8 @@ def tile_picked_dmpnn8_none_po_kernel(
                 interleave_by_pairs(o_grouped, o)
             (nc.scalar if cols.stop == S else nc.sync).dma_start(out_planes[:, :, cols], o)
             nc.vector.quantize_mx(out=o_codes[:, cols].bitcast(FP8X4), scales=o_scales[:, cols], in_=rounded)
-            if block > 0:
-                half = slice(0 if block == 1 else c0, cols.stop)
+            if block % 2:
+                half = slice(c0 - BLOCK, cols.stop)
                 nc.sync.dma_start(out_words[:, half], o_codes[:, half].bitcast(I32))
 
         for t in range(PACK):

@@ -20,7 +20,7 @@ GROUP = 16
 K, T, S, H, N = 512, 2048, 512, 512, 512
 HALF = S // 2
 BLOCK = 128
-CHUNKS = ((0, 256), (256, 128), (384, 128))
+EARLY = S - BLOCK
 
 FLOPS = 2 * K * H * S + 2 * K * N * S + 2 * H * N * S
 
@@ -69,9 +69,9 @@ def tile_picked_dmpnn8_none_po_kernel(
             return word_tile
 
         def deal_words(dealt, raw):
-            nc.vector.tensor_copy(
-                dealt.bitcast(U16).rearrange("p (t g i) -> p g t i", t=PACK, i=8),
-                raw[:].bitcast(U16).rearrange("p (g i t) -> p g t i", t=PACK, i=8),
+            nc.gpsimd.tensor_copy(
+                dealt.bitcast(U16).rearrange("p (t m) -> p t m", t=PACK),
+                raw[:].bitcast(U16).rearrange("p (m t) -> p t m", t=PACK),
             )
 
         w1_rows = w1.rearrange("(p j) c -> p j c", j=PACK)
@@ -99,17 +99,21 @@ def tile_picked_dmpnn8_none_po_kernel(
             keep.tile([P, 2 * H], BF16, name="w1_grouped", tag="w1_grouped%d" % u, align_bytes=64) for u in range(2)
         ]
 
-        def round_w1(cast, h, first, count):
+        def round_w1(cast, h, first, count, columns=slice(0, P)):
             u, within = divmod(first, 2)
             source = w1_raw[h][:].rearrange("p j (m t) -> p m t j", t=PACK)
             target = grouped[u][:].rearrange("p (t m j) -> p m t j", t=2, j=PACK)
-            cast(target[:, :, within : within + count, 2 * h : 2 * h + 2], source[:, :, first : first + count, :])
+            cast(
+                target[:, columns, within : within + count, 2 * h : 2 * h + 2],
+                source[:, columns, first : first + count, :],
+            )
 
         round_w1(nc.vector.tensor_copy, 0, 0, 2)
         round_w1(nc.scalar.copy, 0, 2, 2)
         x_picked = keep.tile([P, S], U32, align_bytes=64)
         nc.vector.tensor_copy(x_picked[:], x_table[:].indirect(picked[:]))
-        round_w1(nc.vector.tensor_copy, 1, 0, 1)
+        round_w1(nc.vector.tensor_copy, 1, 0, 1, slice(0, P // 2))
+        round_w1(nc.scalar.copy, 1, 0, 1, slice(P // 2, P))
         round_w1(nc.vector.tensor_copy, 1, 1, 1)
         round_w1(nc.scalar.copy, 1, 2, 2)
         for first, count in ((0, 1), (1, 1), (2, 2)):
@@ -121,13 +125,13 @@ def tile_picked_dmpnn8_none_po_kernel(
                 in_=grouped[u][:, within * H : (within + count) * H],
             )
 
-        late = keep.tile([P, 5 * N], U8, tag="w1_grouped0", align_bytes=64)
+        late = keep.tile([P, 5 * N], U8, tag="w1_grouped1", align_bytes=64)
         w2_dealt, w3_dealt, w_scales = late[:, : 2 * N], late[:, 2 * N : 4 * N], late[:, 4 * N :]
         deal_words(w2_dealt, w2_raw)
         deal_words(w3_dealt, w3_raw)
-        nc.vector.tensor_copy(
-            w_scales.rearrange("p (t g i) -> p g t i", t=PACK, i=16),
-            raw_scales[:].rearrange("p (g i t) -> p g t i", t=PACK, i=16),
+        nc.gpsimd.tensor_copy(
+            w_scales.rearrange("p (t m) -> p t m", t=PACK),
+            raw_scales[:].rearrange("p (m t) -> p t m", t=PACK),
         )
         for r in range(1, 4):
             nc.sync.dma_start(late[r:P:32, 4 * N :].bitcast(I32), late[8 * r : P : 32, 4 * N :].bitcast(I32))
@@ -140,7 +144,7 @@ def tile_picked_dmpnn8_none_po_kernel(
         banks_used = 0
         for t in range(PACK):
             places = slice(t * P, (t + 1) * P)
-            for c0, width in ((0, HALF), (HALF, HALF)) if t == 0 else ((0, S),):
+            for c0, width in ((0, HALF), (HALF, BLOCK), (HALF + BLOCK, BLOCK)) if t == 0 else ((0, S),):
                 cols = slice(c0, c0 + width)
                 bank = psum.tile([P, width], F32, name="y_bank", tag="bank%d" % banks_used)
                 banks_used = banks_used + 1
@@ -153,9 +157,10 @@ def tile_picked_dmpnn8_none_po_kernel(
                     start=True,
                     stop=True,
                 )
-                nc.scalar.copy(y_wide[t][:, cols], bank[:])
+                drain = nc.vector.tensor_copy if c0 == S - BLOCK else nc.scalar.copy
+                drain(y_wide[t][:, cols], bank[:])
 
-        for t in range(PACK):
+        for t in reversed(range(PACK)):
             nc.scalar.copy(y[t][:], y_wide[t][:, :S])
 
         z_codes = keep.tile([P, S], U32, align_bytes=64)
@@ -165,113 +170,108 @@ def tile_picked_dmpnn8_none_po_kernel(
         out_planes = out_0.rearrange("(p t) j -> p t j", t=PACK)
         out_words = out_1[0].rearrange("p c r -> p (c r)").bitcast(I32)
 
-        back = [
-            keep.tile([P, S], F32, name="back", tag="back%d" % t, align_bytes=64)
-            for t in range(PACK)
-        ]
-        diff = keep.tile([P, PACK, S - BLOCK], F32, tag="w1_codes", align_bytes=64)
-
-        def interleave_by_pairs(dst, src):
-            for u in range(2):
-                pair = slice(2 * u, 2 * u + 2)
-                nc.vector.tensor_copy(dst[:, :, pair], src[:, pair, :].rearrange("p t c -> p c t"))
-
-        def window(t, width):
-            return y[t][:] if width == BLOCK else y_wide[t][:]
-
-        def subtract_back(start, width, diff):
-            for t in range(PACK):
-                nc.vector.tensor_tensor(
-                    diff[:, t, :width],
-                    window(t, width).indirect(entries(in2_list, start, width)),
-                    back[t][:, start : start + width],
-                    SUBTRACT,
-                )
-
-        def messages(start, width, diff, place):
-            z = keep.tile([P, PACK, width], F32, name="z", tag="z%d" % (start // HALF), align_bytes=64)
-            for t in range(PACK):
-                nc.vector.tensor_tensor(
-                    z[:, t, :],
-                    window(t, width).indirect(entries(in1_list, start, width)),
-                    diff[:, t, place : place + width],
-                    ADD,
-                )
-            for c0 in range(start, start + width, BLOCK):
-                cols = slice(c0, c0 + BLOCK)
-                z_grouped = keep.tile([P, BLOCK, PACK], BF16, name="z_grouped%d" % c0, align_bytes=64)
-                if cols.stop == S:
-                    interleave_by_pairs(z_grouped[:], z[:])
-                else:
-                    interleave(nc.scalar.copy, z_grouped[:], z[:, :, c0 - start : c0 - start + BLOCK])
-                nc.vector.quantize_mx(
-                    out=z_codes[:, cols].bitcast(FP8X4),
-                    scales=z_scales[:, cols],
-                    in_=z_grouped[:].rearrange("p c t -> p (c t)"),
-                )
-            return z
-
-        def h0_pass(target, t, c0):
+        def weight_pass(w, target, t, moving, moving_scales, c0, start, stop):
             nc.tensor.matmul_mx(
                 out=target,
-                lhsT=dealt_words[0][:, 2 * P * t : 2 * P * (t + 1)].bitcast(FP4X4),
-                lhsT_scale=dealt_scales[0][:, P * t : P * (t + 1)],
-                rhs=x_picked[:, c0 : c0 + BLOCK].bitcast(FP8X4),
-                rhs_scale=x_picked_scales[:, c0 : c0 + BLOCK],
-                start=True,
-                stop=False,
+                lhsT=dealt_words[w][:, 2 * P * t : 2 * P * (t + 1)].bitcast(FP4X4),
+                lhsT_scale=dealt_scales[w][:, P * t : P * (t + 1)],
+                rhs=moving[:, c0 : c0 + BLOCK].bitcast(FP8X4),
+                rhs_scale=moving_scales[:, c0 : c0 + BLOCK],
+                start=start,
+                stop=stop,
             )
 
-        def z_pass(target, t, c0):
-            nc.tensor.matmul_mx(
-                out=target,
-                lhsT=dealt_words[1][:, 2 * P * t : 2 * P * (t + 1)].bitcast(FP4X4),
-                lhsT_scale=dealt_scales[1][:, P * t : P * (t + 1)],
-                rhs=z_codes[:, c0 : c0 + BLOCK].bitcast(FP8X4),
-                rhs_scale=z_scales[:, c0 : c0 + BLOCK],
-                start=False,
-                stop=True,
-            )
+        early_banks = [psum.tile([P, PACK, BLOCK], F32, name="o_bank", tag="bank%d" % b) for b in (6, 7, 4)]
+        for b in range(2):
+            for t in range(PACK):
+                weight_pass(0, early_banks[b][:, t, :], t, x_picked, x_picked_scales, b * BLOCK, t == 0, False)
+        last_banks = [psum.tile([P, BLOCK], F32, name="o_bank", tag="bank%d" % t) for t in range(PACK)]
+        for t in range(PACK):
+            weight_pass(0, last_banks[t][:], t, x_picked, x_picked_scales, EARLY, True, False)
 
-        def results(c0):
-            cols = slice(c0, c0 + BLOCK)
-            block = c0 // BLOCK
-            both = keep.tile([P, 6 * BLOCK], F32, name="o%d" % c0, align_bytes=64)
-            o = both[:, : PACK * BLOCK].rearrange("p (t c) -> p t c", t=PACK)
-            rounded = both[:, PACK * BLOCK :].bitcast(BF16)
-            o_grouped = rounded.rearrange("p (c t) -> p c t", t=PACK)
-            if cols.stop < S:
-                bank = psum.tile([P, PACK, BLOCK], F32, name="o_bank", tag="bank%d" % (7 - block))
-                for t in range(PACK):
-                    h0_pass(bank[:, t, :], t, c0)
-                    z_pass(bank[:, t, :], t, c0)
-                nc.scalar.copy(o, bank[:])
-                copy = nc.vector.tensor_copy if block == 2 else nc.scalar.copy
-                copy(o_grouped, bank[:].rearrange("p t c -> p c t"))
-            else:
-                banks = [psum.tile([P, BLOCK], F32, name="o_bank", tag="bank%d" % t) for t in range(PACK)]
-                for t in range(PACK):
-                    h0_pass(banks[t][:], t, c0)
-                for t in range(PACK):
-                    z_pass(banks[t][:], t, c0)
-                    nc.scalar.copy(o[:, t, :], banks[t][:])
-                interleave_by_pairs(o_grouped, o)
-            (nc.scalar if cols.stop == S else nc.sync).dma_start(out_planes[:, :, cols], o)
-            nc.vector.quantize_mx(out=o_codes[:, cols].bitcast(FP8X4), scales=o_scales[:, cols], in_=rounded)
-            if block % 2:
-                half = slice(c0 - BLOCK, cols.stop)
-                nc.sync.dma_start(out_words[:, half], o_codes[:, half].bitcast(I32))
+        back = [keep.tile([P, S], F32, name="back%d" % t, align_bytes=64) for t in range(PACK)]
+        diff = keep.tile([P, PACK, EARLY], F32, tag="w1_codes", align_bytes=64)
+        z_first = keep.tile([P, PACK, HALF], F32, align_bytes=64)
+        z_third = diff[:, :, :BLOCK]
+        z_first_grouped = [keep.tile([P, BLOCK, PACK], BF16, name="z_grouped%d" % b, align_bytes=64) for b in range(2)]
+        z_third_grouped = keep.tile([P, BLOCK, PACK], BF16, align_bytes=64)
+        z_last_grouped = keep.tile([P, BLOCK, PACK], BF16, align_bytes=64)
+
+        def fetch(target, windows, t, list_tile, start, other, op):
+            count = target.shape[-1]
+            nc.vector.tensor_tensor(target, windows[t][:].indirect(entries(list_tile, start, count)), other, op)
+
+        def quantise_z(grouped_z, cols):
+            nc.vector.quantize_mx(
+                out=z_codes[:, cols].bitcast(FP8X4),
+                scales=z_scales[:, cols],
+                in_=grouped_z[:].rearrange("p c t -> p (c t)"),
+            )
 
         for t in range(PACK):
             nc.vector.tensor_copy(back[t][:], y_wide[t][:].indirect(rev_list[:]))
-        subtract_back(0, S - BLOCK, diff)
-        z_first = messages(0, HALF, diff, 0)
-        messages(HALF, BLOCK, diff, HALF)
-        subtract_back(S - BLOCK, BLOCK, z_first)
-        z_last = messages(S - BLOCK, BLOCK, z_first, 0)
-        for c0 in range(0, S, BLOCK):
-            results(c0)
+        for t in range(PACK):
+            fetch(diff[:, t, :], y_wide, t, in2_list, 0, back[t][:, :EARLY], SUBTRACT)
+        for t in range(PACK):
+            fetch(z_first[:, t, :], y_wide, t, in1_list, 0, diff[:, t, :HALF], ADD)
+        for t in range(PACK):
+            fetch(z_third[:, t, :], y, t, in1_list, HALF, diff[:, t, HALF:], ADD)
+        for b in range(2):
+            cols = slice(b * BLOCK, (b + 1) * BLOCK)
+            interleave(nc.scalar.copy, z_first_grouped[b][:], z_first[:, :, cols])
+            quantise_z(z_first_grouped[b], cols)
+        interleave(nc.scalar.copy, z_third_grouped[:], z_third)
+        quantise_z(z_third_grouped, slice(HALF, EARLY))
 
+        last_diff = [z_first[:, t, :BLOCK] for t in range(PACK)]
+        last_pairs = [z_third[:, 0:2, :], z_third[:, 2:4, :]]
+        for t in range(PACK):
+            fetch(last_diff[t], y, t, in2_list, EARLY, back[t][:, EARLY:], SUBTRACT)
+        for t in range(PACK):
+            fetch(last_pairs[t // 2][:, t % 2, :], y, t, in1_list, EARLY, last_diff[t], ADD)
+        for u in range(2):
+            nc.vector.tensor_copy(z_last_grouped[:, :, 2 * u : 2 * u + 2], last_pairs[u].rearrange("p t c -> p c t"))
+        quantise_z(z_last_grouped, slice(EARLY, S))
+
+        o_early = keep.tile([P, PACK, EARLY], F32, align_bytes=64)
+        o_last = keep.tile([P, PACK, BLOCK], F32, align_bytes=64)
+        o_first_grouped = keep.tile([P, HALF, PACK], BF16, align_bytes=64)
+        o_third_grouped = keep.tile([P, BLOCK, PACK], BF16, align_bytes=64)
+        o_last_grouped = keep.tile([P, BLOCK, PACK], BF16, align_bytes=64)
+
+        def quantise_o(grouped_o, cols):
+            nc.vector.quantize_mx(
+                out=o_codes[:, cols].bitcast(FP8X4),
+                scales=o_scales[:, cols],
+                in_=grouped_o[:].rearrange("p c t -> p (c t)"),
+            )
+
+        for b in range(2):
+            for t in range(PACK):
+                weight_pass(1, early_banks[b][:, t, :], t, z_codes, z_scales, b * BLOCK, False, t == PACK - 1)
+            cols = slice(b * BLOCK, (b + 1) * BLOCK)
+            nc.scalar.copy(o_early[:, :, cols], early_banks[b][:])
+            nc.scalar.copy(o_first_grouped[:, cols, :], early_banks[b][:].rearrange("p t c -> p c t"))
+        nc.sync.dma_start(out_planes[:, :, :HALF], o_early[:, :, :HALF])
+        quantise_o(o_first_grouped, slice(0, HALF))
+        nc.sync.dma_start(out_words[:, :HALF], o_codes[:, :HALF].bitcast(I32))
+        for t in range(PACK):
+            weight_pass(0, early_banks[2][:, t, :], t, x_picked, x_picked_scales, HALF, True, False)
+            weight_pass(1, early_banks[2][:, t, :], t, z_codes, z_scales, HALF, False, True)
+        nc.scalar.copy(o_early[:, :, HALF:], early_banks[2][:])
+        nc.sync.dma_start(out_planes[:, :, HALF:EARLY], o_early[:, :, HALF:])
+        nc.vector.tensor_copy(o_third_grouped[:], early_banks[2][:].rearrange("p t c -> p c t"))
+        quantise_o(o_third_grouped, slice(HALF, EARLY))
+
+        for t in range(PACK):
+            weight_pass(1, last_banks[t][:], t, z_codes, z_scales, EARLY, False, True)
+            nc.scalar.copy(o_last[:, t, :], last_banks[t][:])
+        nc.scalar.dma_start(out_planes[:, :, EARLY:], o_last[:])
+        for u in range(2):
+            pair = slice(2 * u, 2 * u + 2)
+            nc.vector.tensor_copy(o_last_grouped[:, :, pair], o_last[:, pair, :].rearrange("p t c -> p c t"))
+        quantise_o(o_last_grouped, slice(EARLY, S))
+        nc.sync.dma_start(out_words[:, HALF:], o_codes[:, HALF:].bitcast(I32))
         for r in range(4):
             queue = nc.scalar if r % 2 else nc.sync
             queue.dma_start(out_2[0, r:16:4, :].bitcast(I32), o_scales[r:P:32, :].bitcast(I32))

@@ -235,7 +235,7 @@ def tile_picked_dmpnn8_none_po_kernel(
 
         o_early = keep.tile([P, PACK, EARLY], F32, align_bytes=64)
         o_last = keep.tile([P, PACK, BLOCK], F32, align_bytes=64)
-        o_first_grouped = keep.tile([P, HALF, PACK], BF16, align_bytes=64)
+        o_first_grouped = [keep.tile([P, BLOCK, PACK], BF16, name="o_grouped%d" % b, align_bytes=64) for b in range(2)]
         o_third_grouped = keep.tile([P, BLOCK, PACK], BF16, align_bytes=64)
         o_last_grouped = keep.tile([P, BLOCK, PACK], BF16, align_bytes=64)
 
@@ -251,9 +251,9 @@ def tile_picked_dmpnn8_none_po_kernel(
                 weight_pass(1, early_banks[b][:, t, :], t, z_codes, z_scales, b * BLOCK, False, t == PACK - 1)
             cols = slice(b * BLOCK, (b + 1) * BLOCK)
             nc.scalar.copy(o_early[:, :, cols], early_banks[b][:])
-            nc.scalar.copy(o_first_grouped[:, cols, :], early_banks[b][:].rearrange("p t c -> p c t"))
-        nc.sync.dma_start(out_planes[:, :, :HALF], o_early[:, :, :HALF])
-        quantise_o(o_first_grouped, slice(0, HALF))
+            nc.sync.dma_start(out_planes[:, :, cols], o_early[:, :, cols])
+            nc.scalar.copy(o_first_grouped[b][:], early_banks[b][:].rearrange("p t c -> p c t"))
+            quantise_o(o_first_grouped[b], cols)
         nc.sync.dma_start(out_words[:, :HALF], o_codes[:, :HALF].bitcast(I32))
         for t in range(PACK):
             weight_pass(0, early_banks[2][:, t, :], t, x_picked, x_picked_scales, HALF, True, False)

@@ -25,11 +25,6 @@ EARLY = S - BLOCK
 FLOPS = 2 * K * H * S + 2 * K * N * S + 2 * H * N * S
 
 
-def load_scale_rows(queue, scale_tile, rows):
-    for r in range(4):
-        queue.dma_start(scale_tile[r:P:32, :].bitcast(I32), rows[r:16:4, :].bitcast(I32))
-
-
 def entries(list_tile, start, count):
     return list_tile[:, start // GROUP : (start + count) // GROUP]
 
@@ -48,8 +43,6 @@ def tile_picked_dmpnn8_none_po_kernel(
 
         x_scale_table = keep.tile([P, T], U8, tag="x_scale_table", align_bytes=64)
         nc.vector.memset(x_scale_table[:].bitcast(I32), 0)
-        raw_scales = keep.tile([P, N], U8, tag="raw_scales", align_bytes=64)
-        nc.vector.memset(raw_scales[:].bitcast(I32), 0)
         w3_plane = keep.tile([P, N], U8, align_bytes=64)
         nc.vector.memset(w3_plane[:].bitcast(I32), 0)
 
@@ -63,15 +56,10 @@ def tile_picked_dmpnn8_none_po_kernel(
             nc.sync.dma_start(list_tile[:], source)
             return list_tile
 
-        def load_words(queue, name, words):
-            word_tile = keep.tile([P, 2 * N], U8, name=name + "_raw_words", align_bytes=64)
-            queue.dma_start(word_tile[:].bitcast(I32), words[0].bitcast(I32))
-            return word_tile
-
         def deal_words(dealt, raw):
             nc.gpsimd.tensor_copy(
                 dealt.bitcast(U16).rearrange("p (t m) -> p t m", t=PACK),
-                raw[:].bitcast(U16).rearrange("p (m t) -> p t m", t=PACK),
+                raw.bitcast(U16).rearrange("p (m t) -> p t m", t=PACK),
             )
 
         w1_rows = w1.rearrange("(p j) c -> p j c", j=PACK)
@@ -79,19 +67,17 @@ def tile_picked_dmpnn8_none_po_kernel(
         x_table = keep.tile([P, T], U32, tag="x_table", align_bytes=64)
         nc.sync.dma_start(w1_raw[0][:], w1_rows[:, 0:2, :])
         picked = load_list("picked", offs)
-        load_scale_rows(nc.sync, x_scale_table, x_scales[0])
+        nc.sync.dma_start(x_scale_table[0:P:8, :].bitcast(I32), x_scales[0].bitcast(I32))
         nc.sync.dma_start(x_table[:].bitcast(I32), x_words[0].rearrange("p c r -> p (c r)").bitcast(I32))
         nc.sync.dma_start(w1_raw[1][:], w1_rows[:, 2:4, :])
-        w2_raw = load_words(nc.sync, "w2", w2_words)
-        w3_raw = load_words(nc.sync, "w3", w3_words)
-        for w, scales in enumerate((w2_scales, w3_scales)):
-            nc.sync.dma_start(raw_scales[4 * w : P : 8, :].bitcast(I32), scales[0].bitcast(I32))
         rev_list = load_list("rev", rev)
         in2_list = load_list("in2", in2)
         in1_list = load_list("in1", in1)
 
+        x_spread_scales = keep.tile([P, S], U8, tag="spread_scales", align_bytes=64)
+        nc.vector.tensor_copy(x_spread_scales[:], x_scale_table[:].indirect(picked[:]))
         x_picked_scales = keep.tile([P, S], U8, align_bytes=64)
-        nc.vector.tensor_copy(x_picked_scales[:], x_scale_table[:].indirect(picked[:]))
+        nc.vector.tensor_copy(x_picked_scales[:].bitcast(I32), x_spread_scales[:].bitcast(I32))
 
         w1_codes = keep.tile([P, H], U32, tag="w1_codes", align_bytes=64)
         w1_scales = keep.tile([P, H], U8, align_bytes=64)
@@ -110,6 +96,8 @@ def tile_picked_dmpnn8_none_po_kernel(
 
         round_w1(nc.vector.tensor_copy, 0, 0, 2)
         round_w1(nc.scalar.copy, 0, 2, 2)
+        for r in range(1, 4):
+            nc.scalar.dma_start(x_picked_scales[r:P:32, :].bitcast(I32), x_spread_scales[8 * r : P : 32, :].bitcast(I32))
         x_picked = keep.tile([P, S], U32, align_bytes=64)
         nc.vector.tensor_copy(x_picked[:], x_table[:].indirect(picked[:]))
         round_w1(nc.vector.tensor_copy, 1, 0, 1, slice(0, P // 2))
@@ -125,10 +113,18 @@ def tile_picked_dmpnn8_none_po_kernel(
                 in_=grouped[u][:, within * H : (within + count) * H],
             )
 
+        raw_words = keep.tile([P, 4 * N], U8, tag="x_table", align_bytes=64)
+        for w, words in enumerate((w2_words, w3_words)):
+            nc.sync.dma_start(raw_words[:, 2 * N * w : 2 * N * (w + 1)].bitcast(I32), words[0].bitcast(I32))
+        raw_scales = keep.tile([P, N], U8, tag="spread_scales", align_bytes=64)
+        nc.gpsimd.memset(raw_scales[:].bitcast(I32), 0)
+        for w, scales in enumerate((w2_scales, w3_scales)):
+            nc.sync.dma_start(raw_scales[4 * w : P : 8, :].bitcast(I32), scales[0].bitcast(I32))
+
         late = keep.tile([P, 5 * N], U8, tag="w1_grouped1", align_bytes=64)
         w2_dealt, w3_dealt, w_scales = late[:, : 2 * N], late[:, 2 * N : 4 * N], late[:, 4 * N :]
-        deal_words(w2_dealt, w2_raw)
-        deal_words(w3_dealt, w3_raw)
+        deal_words(w2_dealt, raw_words[:, : 2 * N])
+        deal_words(w3_dealt, raw_words[:, 2 * N :])
         nc.gpsimd.tensor_copy(
             w_scales.rearrange("p (t m) -> p t m", t=PACK),
             raw_scales[:].rearrange("p (m t) -> p t m", t=PACK),
@@ -190,7 +186,7 @@ def tile_picked_dmpnn8_none_po_kernel(
             weight_pass(0, last_banks[t][:], t, x_picked, x_picked_scales, EARLY, True, False)
 
         back = [keep.tile([P, S], F32, name="back%d" % t, align_bytes=64) for t in range(PACK)]
-        diff = keep.tile([P, PACK, EARLY], F32, tag="w1_codes", align_bytes=64)
+        diff = keep.tile([P, PACK, EARLY], F32, tag="x_table", align_bytes=64)
         z_first = keep.tile([P, PACK, HALF], F32, align_bytes=64)
         z_third = diff[:, :, :BLOCK]
         z_first_grouped = [keep.tile([P, BLOCK, PACK], BF16, name="z_grouped%d" % b, align_bytes=64) for b in range(2)]

@@ -47,9 +47,9 @@ def tile_picked_dmpnn8_none_po_kernel(
         nc.vector.memset(w3_plane[:].bitcast(I32), 0)
 
         y_wide = [keep.tile([P, 2 * S], F32, name="y_wide%d" % t, align_bytes=64) for t in range(PACK)]
-        nc.vector.memset(y_wide[0][:, S:], 0.0)
-        for t in range(1, PACK):
-            nc.scalar.copy(y_wide[t][:, S:], y_wide[0][:, S:])
+        for t in range(PACK - 1):
+            nc.vector.memset(y_wide[t][:, S:], 0.0)
+        nc.scalar.copy(y_wide[3][:, S:], y_wide[0][:, S:])
 
         def load_list(name, source):
             list_tile = keep.tile([P, S // GROUP], U16, name=name + "_list")
@@ -82,7 +82,8 @@ def tile_picked_dmpnn8_none_po_kernel(
         w1_codes = keep.tile([P, H], U32, tag="w1_codes", align_bytes=64)
         w1_scales = keep.tile([P, H], U8, align_bytes=64)
         grouped = [
-            keep.tile([P, 2 * H], BF16, name="w1_grouped", tag="w1_grouped%d" % u, align_bytes=64) for u in range(2)
+            keep.tile([P, 2 * H], BF16, name="w1_grouped", tag=tag, align_bytes=64)
+            for tag in ("x_scale_table", "w1_grouped1")
         ]
 
         def round_w1(cast, h, first, count, columns=slice(0, P)):

@@ -154,7 +154,7 @@ def tile_picked_dmpnn8_none_po_kernel(
                     start=True,
                     stop=True,
                 )
-                drain = nc.vector.tensor_copy if c0 == S - BLOCK else nc.scalar.copy
+                drain = nc.vector.tensor_copy if width == HALF else nc.scalar.copy
                 drain(y_wide[t][:, cols], bank[:])
 
         for t in reversed(range(PACK)):

@@ -117,8 +117,8 @@ def tile_picked_dmpnn8_none_po_kernel(
         raw_words = keep.tile([P, 4 * N], U8, tag="x_table", align_bytes=64)
         for w, words in enumerate((w2_words, w3_words)):
             nc.sync.dma_start(raw_words[:, 2 * N * w : 2 * N * (w + 1)].bitcast(I32), words[0].bitcast(I32))
-        raw_scales = keep.tile([P, N], U8, tag="spread_scales", align_bytes=64)
-        nc.gpsimd.memset(raw_scales[:].bitcast(I32), 0)
+        raw_scales = keep.tile([P, N], U8, tag="x_scale_table", align_bytes=64)
+        nc.vector.memset(raw_scales[:].bitcast(I32), 0)
         for w, scales in enumerate((w2_scales, w3_scales)):
             nc.sync.dma_start(raw_scales[4 * w : P : 8, :].bitcast(I32), scales[0].bitcast(I32))
 
@@ -270,5 +270,5 @@ def tile_picked_dmpnn8_none_po_kernel(
         quantise_o(o_last_grouped, slice(EARLY, S))
         nc.sync.dma_start(out_words[:, HALF:], o_codes[:, HALF:].bitcast(I32))
         for r in range(4):
-            queue = nc.scalar if r % 2 else nc.sync
+            queue = nc.sync if r % 2 else nc.scalar
             queue.dma_start(out_2[0, r:16:4, :].bitcast(I32), o_scales[r:P:32, :].bitcast(I32))

@@ -12,6 +12,7 @@ FP8X4 = mybir.dt.float8_e4m3fn_x4
 FP4X4 = mybir.dt.float4_e2m1fn_x4
 ADD = mybir.AluOpType.add
 SUBTRACT = mybir.AluOpType.subtract
+COPY = mybir.ActivationFunctionType.Copy
 
 P = 128
 PACK = 4
@@ -39,6 +40,7 @@ def tile_picked_dmpnn8_none_po_kernel(
     nc = tc.nc
     with ExitStack() as ctx:
         keep = ctx.enter_context(tc.tile_pool(name="keep", bufs=1))
+        spent = ctx.enter_context(tc.tile_pool(name="spent", bufs=1))
         psum = ctx.enter_context(tc.psum_pool(name="psum", bufs=1))
 
         x_scale_table = keep.tile([P, T], U8, tag="x_scale_table", align_bytes=64)
@@ -46,18 +48,16 @@ def tile_picked_dmpnn8_none_po_kernel(
         w3_plane = keep.tile([P, N], U8, align_bytes=64)
         nc.vector.memset(w3_plane[:].bitcast(I32), 0)
 
-        y_wide = [keep.tile([P, 2 * S], F32, name="y_wide%d" % t, align_bytes=64) for t in range(PACK)]
-        for t in range(PACK - 1):
-            nc.vector.memset(y_wide[t][:, S:], 0.0)
-        nc.scalar.copy(y_wide[3][:, S:], y_wide[0][:, S:])
+        raw_scales = keep.tile([P, N], U8, align_bytes=64)
+        nc.vector.memset(raw_scales[:].bitcast(I32), 0)
 
         def load_list(name, source):
             list_tile = keep.tile([P, S // GROUP], U16, name=name + "_list")
             nc.sync.dma_start(list_tile[:], source)
             return list_tile
 
-        def deal_words(dealt, raw):
-            nc.gpsimd.tensor_copy(
+        def deal_words(copy, dealt, raw):
+            copy(
                 dealt.bitcast(U16).rearrange("p (t m) -> p t m", t=PACK),
                 raw.bitcast(U16).rearrange("p (m t) -> p t m", t=PACK),
             )
@@ -67,12 +67,17 @@ def tile_picked_dmpnn8_none_po_kernel(
         x_table = keep.tile([P, T], U32, tag="x_table", align_bytes=64)
         nc.sync.dma_start(w1_raw[0][:], w1_rows[:, 0:2, :])
         picked = load_list("picked", offs)
-        nc.sync.dma_start(x_scale_table[0:P:8, :].bitcast(I32), x_scales[0].bitcast(I32))
-        nc.sync.dma_start(x_table[:].bitcast(I32), x_words[0].rearrange("p c r -> p (c r)").bitcast(I32))
-        nc.sync.dma_start(w1_raw[1][:], w1_rows[:, 2:4, :])
-        rev_list = load_list("rev", rev)
         in2_list = load_list("in2", in2)
         in1_list = load_list("in1", in1)
+        nc.sync.dma_start(x_scale_table[0:P:8, :].bitcast(I32), x_scales[0].bitcast(I32))
+        nc.sync.dma_start(x_table[:].bitcast(I32), x_words[0].rearrange("p c r -> p (c r)").bitcast(I32))
+        rev_list = load_list("rev", rev)
+        nc.sync.dma_start(w1_raw[1][:], w1_rows[:, 2:4, :])
+        raw_words = [keep.tile([P, 2 * N], U8, name="raw_words%d" % w, align_bytes=64) for w in range(2)]
+        for w, words in enumerate((w2_words, w3_words)):
+            nc.sync.dma_start(raw_words[w][:].bitcast(I32), words[0].bitcast(I32))
+        for w, scales in enumerate((w2_scales, w3_scales)):
+            nc.sync.dma_start(raw_scales[4 * w : P : 8, :].bitcast(I32), scales[0].bitcast(I32))
 
         x_spread_scales = keep.tile([P, S], U8, tag="spread_scales", align_bytes=64)
         nc.vector.tensor_copy(x_spread_scales[:], x_scale_table[:].indirect(picked[:]))
@@ -82,21 +87,21 @@ def tile_picked_dmpnn8_none_po_kernel(
         w1_codes = keep.tile([P, H], U32, tag="w1_codes", align_bytes=64)
         w1_scales = keep.tile([P, H], U8, align_bytes=64)
         grouped = [
-            keep.tile([P, 2 * H], BF16, name="w1_grouped", tag=tag, align_bytes=64)
-            for tag in ("x_scale_table", "w1_grouped1")
+            keep.tile([P, 2 * H], BF16, name="w1_grouped0", tag="x_scale_table", align_bytes=64),
+            spent.tile([P, 3 * H], BF16, name="w1_grouped1", offset=0, align_bytes=64),
         ]
 
         def round_w1(cast, h, first, count, columns=slice(0, P)):
             u, within = divmod(first, 2)
             source = w1_raw[h][:].rearrange("p j (m t) -> p m t j", t=PACK)
-            target = grouped[u][:].rearrange("p (t m j) -> p m t j", t=2, j=PACK)
+            target = grouped[u][:, : 2 * H].rearrange("p (t m j) -> p m t j", t=2, j=PACK)
             cast(
                 target[:, columns, within : within + count, 2 * h : 2 * h + 2],
                 source[:, columns, first : first + count, :],
             )
 
         round_w1(nc.vector.tensor_copy, 0, 0, 2)
-        round_w1(nc.scalar.copy, 0, 2, 2)
+        round_w1(lambda dst, src: nc.scalar.activation(dst, src, COPY), 0, 2, 2)
         for r in range(1, 4):
             nc.scalar.dma_start(x_picked_scales[r:P:32, :].bitcast(I32), x_spread_scales[8 * r : P : 32, :].bitcast(I32))
         x_picked = keep.tile([P, S], U32, align_bytes=64)
@@ -114,37 +119,22 @@ def tile_picked_dmpnn8_none_po_kernel(
                 in_=grouped[u][:, within * H : (within + count) * H],
             )
 
-        raw_words = keep.tile([P, 4 * N], U8, tag="x_table", align_bytes=64)
-        for w, words in enumerate((w2_words, w3_words)):
-            nc.sync.dma_start(raw_words[:, 2 * N * w : 2 * N * (w + 1)].bitcast(I32), words[0].bitcast(I32))
-        raw_scales = keep.tile([P, N], U8, tag="x_scale_table", align_bytes=64)
-        nc.vector.memset(raw_scales[:].bitcast(I32), 0)
-        for w, scales in enumerate((w2_scales, w3_scales)):
-            nc.sync.dma_start(raw_scales[4 * w : P : 8, :].bitcast(I32), scales[0].bitcast(I32))
-
-        late = keep.tile([P, 5 * N], U8, tag="w1_grouped1", align_bytes=64)
-        w2_dealt, w3_dealt, w_scales = late[:, : 2 * N], late[:, 2 * N : 4 * N], late[:, 4 * N :]
-        deal_words(w2_dealt, raw_words[:, : 2 * N])
-        deal_words(w3_dealt, raw_words[:, 2 * N :])
-        nc.gpsimd.tensor_copy(
-            w_scales.rearrange("p (t m) -> p t m", t=PACK),
-            raw_scales[:].rearrange("p (m t) -> p t m", t=PACK),
-        )
-        for r in range(1, 4):
-            nc.sync.dma_start(late[r:P:32, 4 * N :].bitcast(I32), late[8 * r : P : 32, 4 * N :].bitcast(I32))
-        for r in range(4):
-            nc.sync.dma_start(w3_plane[r:P:32, :].bitcast(I32), late[8 * r + 4 : P : 32, 4 * N :].bitcast(I32))
+        w2_dealt = spent.tile([P, 2 * N], U8, offset=0, align_bytes=64)
+        w3_dealt = spent.tile([P, 2 * N], U8, offset=2 * N, align_bytes=64)
+        w_scales = spent.tile([P, N], U8, offset=4 * N, align_bytes=64)
+        deal_words(nc.gpsimd.tensor_copy, w2_dealt[:], raw_words[0][:])
+        deal_words(nc.gpsimd.tensor_copy, w3_dealt[:], raw_words[1][:])
         dealt_words = [w2_dealt, w3_dealt]
-        dealt_scales = [w_scales, w3_plane[:]]
+        dealt_scales = [w_scales, w3_plane]
 
         y = [keep.tile([P, S], F32, name="y%d" % t, align_bytes=64) for t in range(PACK)]
-        banks_used = 0
+        y_banks = []
         for t in range(PACK):
             places = slice(t * P, (t + 1) * P)
             for c0, width in ((0, HALF), (HALF, BLOCK), (HALF + BLOCK, BLOCK)) if t == 0 else ((0, S),):
                 cols = slice(c0, c0 + width)
-                bank = psum.tile([P, width], F32, name="y_bank", tag="bank%d" % banks_used)
-                banks_used = banks_used + 1
+                bank = psum.tile([P, width], F32, name="y_bank", tag="bank%d" % len(y_banks))
+                y_banks.append(bank)
                 nc.tensor.matmul_mx(
                     out=bank[:],
                     lhsT=w1_codes[:, places].bitcast(FP8X4),
@@ -154,11 +144,18 @@ def tile_picked_dmpnn8_none_po_kernel(
                     start=True,
                     stop=True,
                 )
-                drain = nc.vector.tensor_copy if width == HALF else nc.scalar.copy
-                drain(y_wide[t][:, cols], bank[:])
+                if t == 0:
+                    drain = nc.vector.tensor_copy if width == HALF else nc.scalar.copy
+                    drain(y[t][:, cols], bank[:])
 
-        for t in reversed(range(PACK)):
-            nc.scalar.copy(y[t][:], y_wide[t][:, :S])
+        nc.vector.tensor_copy(
+            w_scales[:].rearrange("p (t m) -> p t m", t=PACK),
+            raw_scales[:].rearrange("p (m t) -> p t m", t=PACK),
+        )
+        for r in range(1, 4):
+            nc.sync.dma_start(w_scales[r:P:32, :].bitcast(I32), w_scales[8 * r : P : 32, :].bitcast(I32))
+        for r in range(4):
+            nc.sync.dma_start(w3_plane[r:P:32, :].bitcast(I32), w_scales[8 * r + 4 : P : 32, :].bitcast(I32))
 
         z_codes = keep.tile([P, S], U32, align_bytes=64)
         z_scales = keep.tile([P, S], U8, align_bytes=64)
@@ -178,25 +175,21 @@ def tile_picked_dmpnn8_none_po_kernel(
                 stop=stop,
             )
 
-        early_banks = [psum.tile([P, PACK, BLOCK], F32, name="o_bank", tag="bank%d" % b) for b in (6, 7, 4)]
-        for b in range(2):
-            for t in range(PACK):
-                weight_pass(0, early_banks[b][:, t, :], t, x_picked, x_picked_scales, b * BLOCK, t == 0, False)
-        last_banks = [psum.tile([P, BLOCK], F32, name="o_bank", tag="bank%d" % t) for t in range(PACK)]
-        for t in range(PACK):
-            weight_pass(0, last_banks[t][:], t, x_picked, x_picked_scales, EARLY, True, False)
-
-        back = [keep.tile([P, S], F32, name="back%d" % t, align_bytes=64) for t in range(PACK)]
-        diff = keep.tile([P, PACK, EARLY], F32, tag="x_table", align_bytes=64)
+        back_first = [
+            keep.tile([P, HALF], F32, name="back", tag="back%d" % t, align_bytes=64) for t in range(PACK)
+        ]
+        diff_first = [keep.tile([P, HALF], F32, name="diff%d" % t, align_bytes=64) for t in range(PACK)]
         z_first = keep.tile([P, PACK, HALF], F32, align_bytes=64)
-        z_third = diff[:, :, :BLOCK]
-        z_first_grouped = [keep.tile([P, BLOCK, PACK], BF16, name="z_grouped%d" % b, align_bytes=64) for b in range(2)]
-        z_third_grouped = keep.tile([P, BLOCK, PACK], BF16, align_bytes=64)
-        z_last_grouped = keep.tile([P, BLOCK, PACK], BF16, align_bytes=64)
+        z_grouped = [keep.tile([P, BLOCK, PACK], BF16, name="z_grouped%d" % b, align_bytes=64) for b in range(4)]
+        sums = [keep.tile([P, PACK, BLOCK], F32, name="sums%d" % b, align_bytes=64) for b in range(2)]
 
-        def fetch(target, windows, t, list_tile, start, other, op):
+        def fetch_plain(target, t, list_tile, start):
             count = target.shape[-1]
-            nc.vector.tensor_tensor(target, windows[t][:].indirect(entries(list_tile, start, count)), other, op)
+            nc.scalar.activation(target, y[t][:].indirect(entries(list_tile, start, count)), COPY)
+
+        def fetch(target, t, list_tile, start, other, op):
+            count = target.shape[-1]
+            nc.vector.tensor_tensor(target, y[t][:].indirect(entries(list_tile, start, count)), other, op)
 
         def quantise_z(grouped_z, cols):
             nc.vector.quantize_mx(
@@ -205,30 +198,47 @@ def tile_picked_dmpnn8_none_po_kernel(
                 in_=grouped_z[:].rearrange("p c t -> p (c t)"),
             )
 
+        fetch_plain(back_first[0][:], 0, rev_list, 0)
+        nc.vector.tensor_copy(y[1][:], y_banks[3][:])
+        fetch_plain(back_first[1][:], 1, rev_list, 0)
+        for t in (2, 3):
+            nc.scalar.copy(y[t][:], y_banks[2 + t][:])
+            fetch_plain(back_first[t][:], t, rev_list, 0)
+        early_banks = [psum.tile([P, PACK, BLOCK], F32, name="o_bank", tag="bank%d" % b) for b in (6, 7, 4)]
+        for b in range(2):
+            for t in range(PACK):
+                weight_pass(0, early_banks[b][:, t, :], t, x_picked, x_picked_scales, b * BLOCK, t == 0, False)
+        last_banks = [psum.tile([P, BLOCK], F32, name="o_bank", tag="bank%d" % t) for t in range(PACK)]
         for t in range(PACK):
-            nc.vector.tensor_copy(back[t][:], y_wide[t][:].indirect(rev_list[:]))
+            weight_pass(0, last_banks[t][:], t, x_picked, x_picked_scales, EARLY, True, False)
+
+
+        fetch(diff_first[0][:], 0, in2_list, 0, back_first[0][:], SUBTRACT)
         for t in range(PACK):
-            fetch(diff[:, t, :], y_wide, t, in2_list, 0, back[t][:, :EARLY], SUBTRACT)
+            if t + 1 < PACK:
+                fetch(diff_first[t + 1][:], t + 1, in2_list, 0, back_first[t + 1][:], SUBTRACT)
+            fetch(z_first[:, t, :], t, in1_list, 0, diff_first[t][:], ADD)
+        in2_second = keep.tile([P, PACK, HALF], F32, tag="back0", align_bytes=64)
+        back_second = keep.tile([P, PACK, HALF], F32, tag="back1", align_bytes=64)
         for t in range(PACK):
-            fetch(z_first[:, t, :], y_wide, t, in1_list, 0, diff[:, t, :HALF], ADD)
+            fetch_plain(in2_second[:, t, :], t, in2_list, HALF)
         for t in range(PACK):
-            fetch(z_third[:, t, :], y, t, in1_list, HALF, diff[:, t, HALF:], ADD)
+            fetch_plain(back_second[:, t, :], t, rev_list, HALF)
         for b in range(2):
             cols = slice(b * BLOCK, (b + 1) * BLOCK)
-            interleave(nc.scalar.copy, z_first_grouped[b][:], z_first[:, :, cols])
-            quantise_z(z_first_grouped[b], cols)
-        interleave(nc.scalar.copy, z_third_grouped[:], z_third)
-        quantise_z(z_third_grouped, slice(HALF, EARLY))
-
-        last_diff = [z_first[:, t, :BLOCK] for t in range(PACK)]
-        last_pairs = [z_third[:, 0:2, :], z_third[:, 2:4, :]]
-        for t in range(PACK):
-            fetch(last_diff[t], y, t, in2_list, EARLY, back[t][:, EARLY:], SUBTRACT)
-        for t in range(PACK):
-            fetch(last_pairs[t // 2][:, t % 2, :], y, t, in1_list, EARLY, last_diff[t], ADD)
-        for u in range(2):
-            nc.vector.tensor_copy(z_last_grouped[:, :, 2 * u : 2 * u + 2], last_pairs[u].rearrange("p t c -> p c t"))
-        quantise_z(z_last_grouped, slice(EARLY, S))
+            interleave(nc.vector.tensor_copy, z_grouped[b][:], z_first[:, :, cols])
+            quantise_z(z_grouped[b], cols)
+        for b in range(2):
+            within = slice(b * BLOCK, (b + 1) * BLOCK)
+            for t in range(PACK):
+                fetch(sums[b][:, t, :], t, in1_list, HALF + b * BLOCK, in2_second[:, t, within], ADD)
+            nc.vector.tensor_tensor(
+                z_grouped[2 + b][:].rearrange("p (c i) t -> p c t i", i=4),
+                sums[b][:].rearrange("p t (c i) -> p c t i", i=4),
+                back_second[:, :, within].rearrange("p t (c i) -> p c t i", i=4),
+                SUBTRACT,
+            )
+            quantise_z(z_grouped[2 + b], slice(HALF + b * BLOCK, HALF + (b + 1) * BLOCK))
 
         o_early = keep.tile([P, PACK, EARLY], F32, align_bytes=64)
         o_last = keep.tile([P, PACK, BLOCK], F32, align_bytes=64)
@@ -249,15 +259,16 @@ def tile_picked_dmpnn8_none_po_kernel(
             cols = slice(b * BLOCK, (b + 1) * BLOCK)
             nc.scalar.copy(o_early[:, :, cols], early_banks[b][:])
             nc.sync.dma_start(out_planes[:, :, cols], o_early[:, :, cols])
+        for b in range(2):
             nc.scalar.copy(o_first_grouped[b][:], early_banks[b][:].rearrange("p t c -> p c t"))
-            quantise_o(o_first_grouped[b], cols)
+            quantise_o(o_first_grouped[b], slice(b * BLOCK, (b + 1) * BLOCK))
         nc.sync.dma_start(out_words[:, :HALF], o_codes[:, :HALF].bitcast(I32))
         for t in range(PACK):
             weight_pass(0, early_banks[2][:, t, :], t, x_picked, x_picked_scales, HALF, True, False)
             weight_pass(1, early_banks[2][:, t, :], t, z_codes, z_scales, HALF, False, True)
         nc.scalar.copy(o_early[:, :, HALF:], early_banks[2][:])
         nc.sync.dma_start(out_planes[:, :, HALF:EARLY], o_early[:, :, HALF:])
-        nc.vector.tensor_copy(o_third_grouped[:], early_banks[2][:].rearrange("p t c -> p c t"))
+        nc.scalar.copy(o_third_grouped[:], early_banks[2][:].rearrange("p t c -> p c t"))
         quantise_o(o_third_grouped, slice(HALF, EARLY))
 
         for t in range(PACK):

@@ -119,9 +119,13 @@ def tile_picked_dmpnn8_none_po_kernel(
                 in_=grouped[u][:, within * H : (within + count) * H],
             )
 
-        w2_dealt = spent.tile([P, 2 * N], U8, offset=0, align_bytes=64)
-        w3_dealt = spent.tile([P, 2 * N], U8, offset=2 * N, align_bytes=64)
-        w_scales = spent.tile([P, N], U8, offset=4 * N, align_bytes=64)
+        w2_dealt = spent.tile([P, 2 * N], U8, offset=3 * N, align_bytes=64)
+        w3_dealt = spent.tile([P, 2 * N], U8, offset=0, align_bytes=64)
+        w_scales = spent.tile([P, N], U8, offset=2 * N, align_bytes=64)
+        nc.gpsimd.tensor_copy(
+            w_scales[:].rearrange("p (t m) -> p t m", t=PACK),
+            raw_scales[:].rearrange("p (m t) -> p t m", t=PACK),
+        )
         deal_words(nc.gpsimd.tensor_copy, w2_dealt[:], raw_words[0][:])
         deal_words(nc.gpsimd.tensor_copy, w3_dealt[:], raw_words[1][:])
         dealt_words = [w2_dealt, w3_dealt]
@@ -129,9 +133,10 @@ def tile_picked_dmpnn8_none_po_kernel(
 
         y = [keep.tile([P, S], F32, name="y%d" % t, align_bytes=64) for t in range(PACK)]
         y_banks = []
+        pieces = [((0, HALF), (HALF, BLOCK), (EARLY, BLOCK)), ((0, HALF), (HALF, HALF)), ((0, S),), ((0, S),)]
         for t in range(PACK):
             places = slice(t * P, (t + 1) * P)
-            for c0, width in ((0, HALF), (HALF, BLOCK), (HALF + BLOCK, BLOCK)) if t == 0 else ((0, S),):
+            for c0, width in pieces[t]:
                 cols = slice(c0, c0 + width)
                 bank = psum.tile([P, width], F32, name="y_bank", tag="bank%d" % len(y_banks))
                 y_banks.append(bank)
@@ -148,10 +153,6 @@ def tile_picked_dmpnn8_none_po_kernel(
                     drain = nc.vector.tensor_copy if width == HALF else nc.scalar.copy
                     drain(y[t][:, cols], bank[:])
 
-        nc.vector.tensor_copy(
-            w_scales[:].rearrange("p (t m) -> p t m", t=PACK),
-            raw_scales[:].rearrange("p (m t) -> p t m", t=PACK),
-        )
         for r in range(1, 4):
             nc.sync.dma_start(w_scales[r:P:32, :].bitcast(I32), w_scales[8 * r : P : 32, :].bitcast(I32))
         for r in range(4):
@@ -160,7 +161,6 @@ def tile_picked_dmpnn8_none_po_kernel(
         z_codes = keep.tile([P, S], U32, align_bytes=64)
         z_scales = keep.tile([P, S], U8, align_bytes=64)
         o_codes = keep.tile([P, S], U32, align_bytes=64)
-        o_scales = keep.tile([P, S], U8, align_bytes=64)
         out_planes = out_0.rearrange("(p t) j -> p t j", t=PACK)
         out_words = out_1[0].rearrange("p c r -> p (c r)").bitcast(I32)
 
@@ -175,74 +175,74 @@ def tile_picked_dmpnn8_none_po_kernel(
                 stop=stop,
             )
 
-        back_first = [
-            keep.tile([P, HALF], F32, name="back", tag="back%d" % t, align_bytes=64) for t in range(PACK)
+        back = [keep.tile([P, PACK, HALF], F32, name="back", tag="back%d" % h, align_bytes=64) for h in range(2)]
+        second = [
+            [keep.tile([P, HALF], F32, name="second%d_%d" % (h, t), align_bytes=64) for h in range(2)] for t in range(PACK)
         ]
-        diff_first = [keep.tile([P, HALF], F32, name="diff%d" % t, align_bytes=64) for t in range(PACK)]
-        z_first = keep.tile([P, PACK, HALF], F32, align_bytes=64)
-        z_grouped = [keep.tile([P, BLOCK, PACK], BF16, name="z_grouped%d" % b, align_bytes=64) for b in range(4)]
-        sums = [keep.tile([P, PACK, BLOCK], F32, name="sums%d" % b, align_bytes=64) for b in range(2)]
+        sums = [keep.tile([P, PACK, HALF], F32, name="sums", tag="sums%d" % h, align_bytes=64) for h in range(2)]
+        z_grouped = [
+            keep.tile([P, BLOCK, PACK], BF16, name="z_grouped", tag="z_grouped%d" % b, align_bytes=64) for b in range(4)
+        ]
 
-        def fetch_plain(target, t, list_tile, start):
-            count = target.shape[-1]
-            nc.scalar.activation(target, y[t][:].indirect(entries(list_tile, start, count)), COPY)
+        def window(t, list_tile, start, target):
+            return y[t][:].indirect(entries(list_tile, start, target.shape[-1]))
 
-        def fetch(target, t, list_tile, start, other, op):
-            count = target.shape[-1]
-            nc.vector.tensor_tensor(target, y[t][:].indirect(entries(list_tile, start, count)), other, op)
+        def fetch_scalar(target, t, list_tile, start):
+            nc.scalar.activation(target, window(t, list_tile, start, target), COPY)
+
+        def fetch_add(target, t, start, other):
+            nc.vector.tensor_tensor(target, window(t, in1_list, start, target), other, ADD)
+
+        def round_z(grouped_z, plus, minus):
+            nc.vector.tensor_tensor(
+                grouped_z.rearrange("p (c i) t -> p c t i", i=4),
+                plus.rearrange("p t (c i) -> p c t i", i=4),
+                minus.rearrange("p t (c i) -> p c t i", i=4),
+                SUBTRACT,
+            )
 
         def quantise_z(grouped_z, cols):
             nc.vector.quantize_mx(
                 out=z_codes[:, cols].bitcast(FP8X4),
                 scales=z_scales[:, cols],
-                in_=grouped_z[:].rearrange("p c t -> p (c t)"),
+                in_=grouped_z.rearrange("p c t -> p (c t)"),
             )
 
-        fetch_plain(back_first[0][:], 0, rev_list, 0)
-        nc.vector.tensor_copy(y[1][:], y_banks[3][:])
-        fetch_plain(back_first[1][:], 1, rev_list, 0)
+        for h in range(2):
+            nc.vector.tensor_copy(y[1][:, h * HALF : (h + 1) * HALF], y_banks[3 + h][:])
         for t in (2, 3):
-            nc.scalar.copy(y[t][:], y_banks[2 + t][:])
-            fetch_plain(back_first[t][:], t, rev_list, 0)
-        early_banks = [psum.tile([P, PACK, BLOCK], F32, name="o_bank", tag="bank%d" % b) for b in (6, 7, 4)]
-        for b in range(2):
+            nc.vector.tensor_copy(y[t][:], y_banks[3 + t][:])
+        early_banks = [psum.tile([P, PACK, BLOCK], F32, name="o_bank", tag="bank%d" % b) for b in (7, 0, 1)]
+        for b in range(3):
             for t in range(PACK):
                 weight_pass(0, early_banks[b][:, t, :], t, x_picked, x_picked_scales, b * BLOCK, t == 0, False)
-        last_banks = [psum.tile([P, BLOCK], F32, name="o_bank", tag="bank%d" % t) for t in range(PACK)]
+
+        last_banks = [psum.tile([P, BLOCK], F32, name="o_bank", tag="bank%d" % (2 + t)) for t in range(PACK)]
         for t in range(PACK):
             weight_pass(0, last_banks[t][:], t, x_picked, x_picked_scales, EARLY, True, False)
 
-
-        fetch(diff_first[0][:], 0, in2_list, 0, back_first[0][:], SUBTRACT)
+        nc.vector.tensor_copy(back[0][:, 0, :], window(0, rev_list, 0, back[0][:, 0, :]))
         for t in range(PACK):
-            if t + 1 < PACK:
-                fetch(diff_first[t + 1][:], t + 1, in2_list, 0, back_first[t + 1][:], SUBTRACT)
-            fetch(z_first[:, t, :], t, in1_list, 0, diff_first[t][:], ADD)
-        in2_second = keep.tile([P, PACK, HALF], F32, tag="back0", align_bytes=64)
-        back_second = keep.tile([P, PACK, HALF], F32, tag="back1", align_bytes=64)
-        for t in range(PACK):
-            fetch_plain(in2_second[:, t, :], t, in2_list, HALF)
-        for t in range(PACK):
-            fetch_plain(back_second[:, t, :], t, rev_list, HALF)
+            for h in range(2):
+                fetch_scalar(second[t][h][:], t, in2_list, h * HALF)
+                fetch_add(sums[h][:, t, :], t, h * HALF, second[t][h][:])
+        for t in range(1, PACK):
+            fetch_scalar(back[0][:, t, :], t, rev_list, 0)
         for b in range(2):
-            cols = slice(b * BLOCK, (b + 1) * BLOCK)
-            interleave(nc.vector.tensor_copy, z_grouped[b][:], z_first[:, :, cols])
-            quantise_z(z_grouped[b], cols)
-        for b in range(2):
-            within = slice(b * BLOCK, (b + 1) * BLOCK)
             for t in range(PACK):
-                fetch(sums[b][:, t, :], t, in1_list, HALF + b * BLOCK, in2_second[:, t, within], ADD)
-            nc.vector.tensor_tensor(
-                z_grouped[2 + b][:].rearrange("p (c i) t -> p c t i", i=4),
-                sums[b][:].rearrange("p t (c i) -> p c t i", i=4),
-                back_second[:, :, within].rearrange("p t (c i) -> p c t i", i=4),
-                SUBTRACT,
-            )
-            quantise_z(z_grouped[2 + b], slice(HALF + b * BLOCK, HALF + (b + 1) * BLOCK))
+                fetch_scalar(back[1][:, t, b * BLOCK : (b + 1) * BLOCK], t, rev_list, HALF + b * BLOCK)
+        for b in range(4):
+            h, within = b // 2, slice(b % 2 * BLOCK, (b % 2 + 1) * BLOCK)
+            for planes in (slice(0, 2), slice(2, PACK)) if b == 3 else (slice(0, PACK),):
+                round_z(z_grouped[b][:, :, planes], sums[h][:, planes, within], back[h][:, planes, within])
+            quantise_z(z_grouped[b][:], slice(b * BLOCK, (b + 1) * BLOCK))
 
         o_early = keep.tile([P, PACK, EARLY], F32, align_bytes=64)
         o_last = keep.tile([P, PACK, BLOCK], F32, align_bytes=64)
-        o_first_grouped = [keep.tile([P, BLOCK, PACK], BF16, name="o_grouped%d" % b, align_bytes=64) for b in range(2)]
+        o_scales = keep.tile([P, S], U8, align_bytes=64)
+        o_first_grouped = [
+            keep.tile([P, BLOCK, PACK], BF16, name="o_grouped", tag=tag, align_bytes=64) for tag in ("z_grouped3", "back1")
+        ]
         o_third_grouped = keep.tile([P, BLOCK, PACK], BF16, align_bytes=64)
         o_last_grouped = keep.tile([P, BLOCK, PACK], BF16, align_bytes=64)
 
@@ -253,23 +253,12 @@ def tile_picked_dmpnn8_none_po_kernel(
                 in_=grouped_o[:].rearrange("p c t -> p (c t)"),
             )
 
-        for b in range(2):
+        for b in range(3):
             for t in range(PACK):
                 weight_pass(1, early_banks[b][:, t, :], t, z_codes, z_scales, b * BLOCK, False, t == PACK - 1)
             cols = slice(b * BLOCK, (b + 1) * BLOCK)
             nc.scalar.copy(o_early[:, :, cols], early_banks[b][:])
             nc.sync.dma_start(out_planes[:, :, cols], o_early[:, :, cols])
-        for b in range(2):
-            nc.scalar.copy(o_first_grouped[b][:], early_banks[b][:].rearrange("p t c -> p c t"))
-            quantise_o(o_first_grouped[b], slice(b * BLOCK, (b + 1) * BLOCK))
-        nc.sync.dma_start(out_words[:, :HALF], o_codes[:, :HALF].bitcast(I32))
-        for t in range(PACK):
-            weight_pass(0, early_banks[2][:, t, :], t, x_picked, x_picked_scales, HALF, True, False)
-            weight_pass(1, early_banks[2][:, t, :], t, z_codes, z_scales, HALF, False, True)
-        nc.scalar.copy(o_early[:, :, HALF:], early_banks[2][:])
-        nc.sync.dma_start(out_planes[:, :, HALF:EARLY], o_early[:, :, HALF:])
-        nc.scalar.copy(o_third_grouped[:], early_banks[2][:].rearrange("p t c -> p c t"))
-        quantise_o(o_third_grouped, slice(HALF, EARLY))
 
         for t in range(PACK):
             weight_pass(1, last_banks[t][:], t, z_codes, z_scales, EARLY, False, True)
@@ -279,6 +268,13 @@ def tile_picked_dmpnn8_none_po_kernel(
             pair = slice(2 * u, 2 * u + 2)
             nc.vector.tensor_copy(o_last_grouped[:, :, pair], o_last[:, pair, :].rearrange("p t c -> p c t"))
         quantise_o(o_last_grouped, slice(EARLY, S))
+        for b in range(2):
+            interleave(nc.vector.tensor_copy, o_first_grouped[b][:], o_early[:, :, b * BLOCK : (b + 1) * BLOCK])
+        for b in range(2):
+            quantise_o(o_first_grouped[b], slice(b * BLOCK, (b + 1) * BLOCK))
+        nc.sync.dma_start(out_words[:, :HALF], o_codes[:, :HALF].bitcast(I32))
+        interleave(nc.vector.tensor_copy, o_third_grouped[:], o_early[:, :, HALF:])
+        quantise_o(o_third_grouped, slice(HALF, EARLY))
         nc.sync.dma_start(out_words[:, HALF:], o_codes[:, HALF:].bitcast(I32))
         for r in range(4):
             queue = nc.sync if r % 2 else nc.scalar

@@ -16,7 +16,6 @@ COPY = mybir.ActivationFunctionType.Copy
 
 P = 128
 PACK = 4
-QUADRANTS = 4
 GROUP = 16
 K, T, S, H, N = 512, 2048, 512, 512, 512
 HALF = S // 2
@@ -30,8 +29,12 @@ def entries(list_tile, start, count):
     return list_tile[:, start // GROUP : (start + count) // GROUP]
 
 
-def interleave(copy, dst, src):
-    copy(dst.rearrange("p (c i) t -> p c t i", i=4), src.rearrange("p t (c i) -> p c t i", i=4))
+def by_fours(planes):
+    return planes.rearrange("p t (c i) -> p c t i", i=4)
+
+
+def words_by_fours(grouped):
+    return grouped.rearrange("p (c i) t -> p c t i", i=4)
 
 
 def tile_picked_dmpnn8_none_po_kernel(
@@ -153,6 +156,7 @@ def tile_picked_dmpnn8_none_po_kernel(
                     drain = nc.vector.tensor_copy if width == HALF else nc.scalar.copy
                     drain(y[t][:, cols], bank[:])
 
+
         for r in range(1, 4):
             nc.sync.dma_start(w_scales[r:P:32, :].bitcast(I32), w_scales[8 * r : P : 32, :].bitcast(I32))
         for r in range(4):
@@ -161,6 +165,7 @@ def tile_picked_dmpnn8_none_po_kernel(
         z_codes = keep.tile([P, S], U32, align_bytes=64)
         z_scales = keep.tile([P, S], U8, align_bytes=64)
         o_codes = keep.tile([P, S], U32, align_bytes=64)
+        o_scales = keep.tile([P, S], U8, align_bytes=64)
         out_planes = out_0.rearrange("(p t) j -> p t j", t=PACK)
         out_words = out_1[0].rearrange("p c r -> p (c r)").bitcast(I32)
 
@@ -184,28 +189,43 @@ def tile_picked_dmpnn8_none_po_kernel(
             keep.tile([P, BLOCK, PACK], BF16, name="z_grouped", tag="z_grouped%d" % b, align_bytes=64) for b in range(4)
         ]
 
-        def window(t, list_tile, start, target):
-            return y[t][:].indirect(entries(list_tile, start, target.shape[-1]))
+        def window(t, list_tile, start, count):
+            return y[t][:].indirect(entries(list_tile, start, count))
 
-        def fetch_scalar(target, t, list_tile, start):
-            nc.scalar.activation(target, window(t, list_tile, start, target), COPY)
+        def place(c0, count):
+            return c0 // HALF, slice(c0 % HALF, c0 % HALF + count)
 
-        def fetch_add(target, t, start, other):
-            nc.vector.tensor_tensor(target, window(t, in1_list, start, target), other, ADD)
+        def fetch_second(t, c0, count):
+            h, within = place(c0, count)
+            nc.scalar.activation(second[t][h][:, within], window(t, in2_list, c0, count), COPY)
 
-        def round_z(grouped_z, plus, minus):
+        def fetch_sum(t, c0, count):
+            h, within = place(c0, count)
+            nc.vector.tensor_tensor(sums[h][:, t, within], window(t, in1_list, c0, count), second[t][h][:, within], ADD)
+
+        def fetch_back(t, c0, count):
+            h, within = place(c0, count)
+            nc.scalar.activation(back[h][:, t, within], window(t, rev_list, c0, count), COPY)
+
+        def fetch_back_vector(t, c0, count):
+            h, within = place(c0, count)
+            nc.vector.tensor_copy(back[h][:, t, within], window(t, rev_list, c0, count))
+
+        def round_z(b, planes=slice(0, PACK)):
+            h, within = place(b * BLOCK, BLOCK)
             nc.vector.tensor_tensor(
-                grouped_z.rearrange("p (c i) t -> p c t i", i=4),
-                plus.rearrange("p t (c i) -> p c t i", i=4),
-                minus.rearrange("p t (c i) -> p c t i", i=4),
+                words_by_fours(z_grouped[b][:, :, planes]),
+                by_fours(sums[h][:, planes, within]),
+                by_fours(back[h][:, planes, within]),
                 SUBTRACT,
             )
 
-        def quantise_z(grouped_z, cols):
+        def quantise_z(b):
+            cols = slice(b * BLOCK, (b + 1) * BLOCK)
             nc.vector.quantize_mx(
                 out=z_codes[:, cols].bitcast(FP8X4),
                 scales=z_scales[:, cols],
-                in_=grouped_z.rearrange("p c t -> p (c t)"),
+                in_=z_grouped[b][:].rearrange("p c t -> p (c t)"),
             )
 
         for h in range(2):
@@ -216,65 +236,74 @@ def tile_picked_dmpnn8_none_po_kernel(
         for b in range(3):
             for t in range(PACK):
                 weight_pass(0, early_banks[b][:, t, :], t, x_picked, x_picked_scales, b * BLOCK, t == 0, False)
-
         last_banks = [psum.tile([P, BLOCK], F32, name="o_bank", tag="bank%d" % (2 + t)) for t in range(PACK)]
         for t in range(PACK):
             weight_pass(0, last_banks[t][:], t, x_picked, x_picked_scales, EARLY, True, False)
 
-        nc.vector.tensor_copy(back[0][:, 0, :], window(0, rev_list, 0, back[0][:, 0, :]))
-        for t in range(PACK):
-            for h in range(2):
-                fetch_scalar(second[t][h][:], t, in2_list, h * HALF)
-                fetch_add(sums[h][:, t, :], t, h * HALF, second[t][h][:])
+        fetch_back_vector(0, 0, HALF)
+        for t, h in ((0, 0), (0, 1), (1, 0), (1, 1), (2, 0), (2, 1), (3, 0)):
+            fetch_second(t, h * HALF, HALF)
+        for t, h in ((0, 0), (0, 1), (1, 0), (1, 1), (2, 0), (3, 0), (2, 1)):
+            fetch_sum(t, h * HALF, HALF)
         for t in range(1, PACK):
-            fetch_scalar(back[0][:, t, :], t, rev_list, 0)
-        for b in range(2):
+            fetch_back(t, 0, HALF)
+        for b in (2, 3):
+            fetch_second(3, b * BLOCK, BLOCK)
             for t in range(PACK):
-                fetch_scalar(back[1][:, t, b * BLOCK : (b + 1) * BLOCK], t, rev_list, HALF + b * BLOCK)
-        for b in range(4):
-            h, within = b // 2, slice(b % 2 * BLOCK, (b % 2 + 1) * BLOCK)
-            for planes in (slice(0, 2), slice(2, PACK)) if b == 3 else (slice(0, PACK),):
-                round_z(z_grouped[b][:, :, planes], sums[h][:, planes, within], back[h][:, planes, within])
-            quantise_z(z_grouped[b][:], slice(b * BLOCK, (b + 1) * BLOCK))
+                fetch_back(t, b * BLOCK, BLOCK)
+        round_z(0)
+        fetch_sum(3, HALF, BLOCK)
+        quantise_z(0)
+        round_z(1)
+        round_z(2)
+        quantise_z(1)
+        fetch_sum(3, EARLY, BLOCK)
+        quantise_z(2)
+        round_z(3, slice(0, 2))
+        round_z(3, slice(2, PACK))
+        quantise_z(3)
 
         o_early = keep.tile([P, PACK, EARLY], F32, align_bytes=64)
         o_last = keep.tile([P, PACK, BLOCK], F32, align_bytes=64)
-        o_scales = keep.tile([P, S], U8, align_bytes=64)
-        o_first_grouped = [
-            keep.tile([P, BLOCK, PACK], BF16, name="o_grouped", tag=tag, align_bytes=64) for tag in ("z_grouped3", "back1")
+        spans = ((0, HALF), (HALF, BLOCK), (EARLY, BLOCK))
+        o_grouped = [
+            keep.tile([P, HALF, PACK], BF16, name="o_grouped0", align_bytes=64),
+            spent.tile([P, BLOCK, PACK], BF16, name="o_grouped1", offset=0, align_bytes=64),
+            keep.tile([P, BLOCK, PACK], BF16, name="o_grouped2", align_bytes=64),
         ]
-        o_third_grouped = keep.tile([P, BLOCK, PACK], BF16, align_bytes=64)
-        o_last_grouped = keep.tile([P, BLOCK, PACK], BF16, align_bytes=64)
 
-        def quantise_o(grouped_o, cols):
-            nc.vector.quantize_mx(
-                out=o_codes[:, cols].bitcast(FP8X4),
-                scales=o_scales[:, cols],
-                in_=grouped_o[:].rearrange("p c t -> p (c t)"),
-            )
-
-        for b in range(3):
+        def product(b):
             for t in range(PACK):
                 weight_pass(1, early_banks[b][:, t, :], t, z_codes, z_scales, b * BLOCK, False, t == PACK - 1)
             cols = slice(b * BLOCK, (b + 1) * BLOCK)
             nc.scalar.copy(o_early[:, :, cols], early_banks[b][:])
             nc.sync.dma_start(out_planes[:, :, cols], o_early[:, :, cols])
 
+        def quantise_o(n):
+            cols = slice(spans[n][0], spans[n][0] + spans[n][1])
+            nc.vector.quantize_mx(
+                out=o_codes[:, cols].bitcast(FP8X4),
+                scales=o_scales[:, cols],
+                in_=o_grouped[n][:].rearrange("p c t -> p (c t)"),
+            )
+
+        for b in range(3):
+            product(b)
         for t in range(PACK):
             weight_pass(1, last_banks[t][:], t, z_codes, z_scales, EARLY, False, True)
             nc.scalar.copy(o_last[:, t, :], last_banks[t][:])
-        nc.scalar.dma_start(out_planes[:, :, EARLY:], o_last[:])
+        nc.sync.dma_start(out_planes[:, :, EARLY:], o_last[:])
+        nc.scalar.copy(o_grouped[1][:], early_banks[2][:].rearrange("p t c -> p c t"))
+        for b in range(2):
+            cols = slice(b * BLOCK, (b + 1) * BLOCK)
+            nc.vector.tensor_copy(words_by_fours(o_grouped[0][:, cols, :]), by_fours(o_early[:, :, cols]))
+        quantise_o(0)
+        nc.sync.dma_start(out_words[:, :HALF], o_codes[:, :HALF].bitcast(I32))
         for u in range(2):
             pair = slice(2 * u, 2 * u + 2)
-            nc.vector.tensor_copy(o_last_grouped[:, :, pair], o_last[:, pair, :].rearrange("p t c -> p c t"))
-        quantise_o(o_last_grouped, slice(EARLY, S))
-        for b in range(2):
-            interleave(nc.vector.tensor_copy, o_first_grouped[b][:], o_early[:, :, b * BLOCK : (b + 1) * BLOCK])
-        for b in range(2):
-            quantise_o(o_first_grouped[b], slice(b * BLOCK, (b + 1) * BLOCK))
-        nc.sync.dma_start(out_words[:, :HALF], o_codes[:, :HALF].bitcast(I32))
-        interleave(nc.vector.tensor_copy, o_third_grouped[:], o_early[:, :, HALF:])
-        quantise_o(o_third_grouped, slice(HALF, EARLY))
+            nc.vector.tensor_copy(o_grouped[2][:, :, pair], o_last[:, pair, :].rearrange("p t c -> p c t"))
+        quantise_o(2)
+        quantise_o(1)
         nc.sync.dma_start(out_words[:, HALF:], o_codes[:, HALF:].bitcast(I32))
         for r in range(4):
             queue = nc.sync if r % 2 else nc.scalar

@@ -162,28 +162,35 @@ def tile_picked_dmpnn8_none_po_kernel(
         for r in range(4):
             nc.sync.dma_start(w3_plane[r:P:32, :].bitcast(I32), w_scales[8 * r + 4 : P : 32, :].bitcast(I32))
 
-        z_codes = keep.tile([P, S], U32, align_bytes=64)
+        z_first_codes = spent.tile([P, BLOCK], U32, offset=8 * N, align_bytes=64)
+        z_later_codes = keep.tile([P, EARLY], U32, align_bytes=64)
+        z_codes = [z_first_codes[:]] + [z_later_codes[:, b * BLOCK : (b + 1) * BLOCK] for b in range(3)]
         z_scales = keep.tile([P, S], U8, align_bytes=64)
         o_codes = keep.tile([P, S], U32, align_bytes=64)
         o_scales = keep.tile([P, S], U8, align_bytes=64)
         out_planes = out_0.rearrange("(p t) j -> p t j", t=PACK)
         out_words = out_1[0].rearrange("p c r -> p (c r)").bitcast(I32)
 
-        def weight_pass(w, target, t, moving, moving_scales, c0, start, stop):
+        def weight_pass(w, target, t, moving, moving_scales, start, stop):
             nc.tensor.matmul_mx(
                 out=target,
                 lhsT=dealt_words[w][:, 2 * P * t : 2 * P * (t + 1)].bitcast(FP4X4),
                 lhsT_scale=dealt_scales[w][:, P * t : P * (t + 1)],
-                rhs=moving[:, c0 : c0 + BLOCK].bitcast(FP8X4),
-                rhs_scale=moving_scales[:, c0 : c0 + BLOCK],
+                rhs=moving.bitcast(FP8X4),
+                rhs_scale=moving_scales,
                 start=start,
                 stop=stop,
             )
 
-        back = [keep.tile([P, PACK, HALF], F32, name="back", tag="back%d" % h, align_bytes=64) for h in range(2)]
+        reused = {(2, 1): "second1_0"}
         second = [
-            [keep.tile([P, HALF], F32, name="second%d_%d" % (h, t), align_bytes=64) for h in range(2)] for t in range(PACK)
+            [
+                keep.tile([P, HALF], F32, name="second", tag=reused.get((t, h), "second%d_%d" % (t, h)), align_bytes=64)
+                for h in range(2)
+            ]
+            for t in range(PACK)
         ]
+        back = [keep.tile([P, PACK, HALF], F32, name="back", tag="second0_%d" % h, align_bytes=64) for h in range(2)]
         sums = [keep.tile([P, PACK, HALF], F32, name="sums", tag="sums%d" % h, align_bytes=64) for h in range(2)]
         z_grouped = [
             keep.tile([P, BLOCK, PACK], BF16, name="z_grouped", tag="z_grouped%d" % b, align_bytes=64) for b in range(4)
@@ -207,9 +214,6 @@ def tile_picked_dmpnn8_none_po_kernel(
             h, within = place(c0, count)
             nc.scalar.activation(back[h][:, t, within], window(t, rev_list, c0, count), COPY)
 
-        def fetch_back_vector(t, c0, count):
-            h, within = place(c0, count)
-            nc.vector.tensor_copy(back[h][:, t, within], window(t, rev_list, c0, count))
 
         def round_z(b, planes=slice(0, PACK)):
             h, within = place(b * BLOCK, BLOCK)
@@ -223,7 +227,7 @@ def tile_picked_dmpnn8_none_po_kernel(
         def quantise_z(b):
             cols = slice(b * BLOCK, (b + 1) * BLOCK)
             nc.vector.quantize_mx(
-                out=z_codes[:, cols].bitcast(FP8X4),
+                out=z_codes[b].bitcast(FP8X4),
                 scales=z_scales[:, cols],
                 in_=z_grouped[b][:].rearrange("p c t -> p (c t)"),
             )
@@ -232,36 +236,14 @@ def tile_picked_dmpnn8_none_po_kernel(
             nc.vector.tensor_copy(y[1][:, h * HALF : (h + 1) * HALF], y_banks[3 + h][:])
         for t in (2, 3):
             nc.vector.tensor_copy(y[t][:], y_banks[3 + t][:])
+        blocks = [slice(b * BLOCK, (b + 1) * BLOCK) for b in range(4)]
         early_banks = [psum.tile([P, PACK, BLOCK], F32, name="o_bank", tag="bank%d" % b) for b in (7, 0, 1)]
-        for b in range(3):
+        for b in (1, 2):
             for t in range(PACK):
-                weight_pass(0, early_banks[b][:, t, :], t, x_picked, x_picked_scales, b * BLOCK, t == 0, False)
+                weight_pass(0, early_banks[b][:, t, :], t, x_picked[:, blocks[b]], x_picked_scales[:, blocks[b]], t == 0, False)
         last_banks = [psum.tile([P, BLOCK], F32, name="o_bank", tag="bank%d" % (2 + t)) for t in range(PACK)]
         for t in range(PACK):
-            weight_pass(0, last_banks[t][:], t, x_picked, x_picked_scales, EARLY, True, False)
-
-        fetch_back_vector(0, 0, HALF)
-        for t, h in ((0, 0), (0, 1), (1, 0), (1, 1), (2, 0), (2, 1), (3, 0)):
-            fetch_second(t, h * HALF, HALF)
-        for t, h in ((0, 0), (0, 1), (1, 0), (1, 1), (2, 0), (3, 0), (2, 1)):
-            fetch_sum(t, h * HALF, HALF)
-        for t in range(1, PACK):
-            fetch_back(t, 0, HALF)
-        for b in (2, 3):
-            fetch_second(3, b * BLOCK, BLOCK)
-            for t in range(PACK):
-                fetch_back(t, b * BLOCK, BLOCK)
-        round_z(0)
-        fetch_sum(3, HALF, BLOCK)
-        quantise_z(0)
-        round_z(1)
-        round_z(2)
-        quantise_z(1)
-        fetch_sum(3, EARLY, BLOCK)
-        quantise_z(2)
-        round_z(3, slice(0, 2))
-        round_z(3, slice(2, PACK))
-        quantise_z(3)
+            weight_pass(0, last_banks[t][:], t, x_picked[:, blocks[3]], x_picked_scales[:, blocks[3]], True, False)
 
         o_early = keep.tile([P, PACK, EARLY], F32, align_bytes=64)
         o_last = keep.tile([P, PACK, BLOCK], F32, align_bytes=64)
@@ -274,10 +256,12 @@ def tile_picked_dmpnn8_none_po_kernel(
 
         def product(b):
             for t in range(PACK):
-                weight_pass(1, early_banks[b][:, t, :], t, z_codes, z_scales, b * BLOCK, False, t == PACK - 1)
-            cols = slice(b * BLOCK, (b + 1) * BLOCK)
-            nc.scalar.copy(o_early[:, :, cols], early_banks[b][:])
-            nc.sync.dma_start(out_planes[:, :, cols], o_early[:, :, cols])
+                first, last = b == 0 and t == 0, b > 0 and t == PACK - 1
+                weight_pass(1, early_banks[b][:, t, :], t, z_codes[b], z_scales[:, blocks[b]], first, last)
+            for t in range(PACK if b == 0 else 0):
+                weight_pass(0, early_banks[b][:, t, :], t, x_picked[:, blocks[b]], x_picked_scales[:, blocks[b]], False, t == PACK - 1)
+            nc.scalar.copy(o_early[:, :, blocks[b]], early_banks[b][:])
+            nc.sync.dma_start(out_planes[:, :, blocks[b]], o_early[:, :, blocks[b]])
 
         def quantise_o(n):
             cols = slice(spans[n][0], spans[n][0] + spans[n][1])
@@ -287,16 +271,38 @@ def tile_picked_dmpnn8_none_po_kernel(
                 in_=o_grouped[n][:].rearrange("p c t -> p (c t)"),
             )
 
+        nc.vector.tensor_copy(second[0][1][:], window(0, in2_list, HALF, HALF))
+        for t, h in ((0, 0), (1, 0), (1, 1), (2, 0), (3, 0)):
+            fetch_second(t, h * HALF, HALF)
+        for t, h in ((0, 0), (0, 1), (1, 0), (2, 0), (3, 0), (1, 1)):
+            fetch_sum(t, h * HALF, HALF)
+        for t in range(PACK):
+            fetch_back(t, 0, HALF)
+        for t in (2, 3):
+            fetch_second(t, HALF, HALF)
+        for b in (2, 3):
+            for t in range(PACK):
+                fetch_back(t, b * BLOCK, BLOCK)
+        round_z(0)
+        fetch_sum(2, HALF, HALF)
+        quantise_z(0)
+        round_z(1)
+        fetch_sum(3, HALF, HALF)
+        quantise_z(1)
+        round_z(2)
+        round_z(3, slice(0, 2))
+        quantise_z(2)
+        round_z(3, slice(2, PACK))
+        quantise_z(3)
         for b in range(3):
             product(b)
         for t in range(PACK):
-            weight_pass(1, last_banks[t][:], t, z_codes, z_scales, EARLY, False, True)
+            weight_pass(1, last_banks[t][:], t, z_codes[3], z_scales[:, blocks[3]], False, True)
             nc.scalar.copy(o_last[:, t, :], last_banks[t][:])
         nc.sync.dma_start(out_planes[:, :, EARLY:], o_last[:])
-        nc.scalar.copy(o_grouped[1][:], early_banks[2][:].rearrange("p t c -> p c t"))
+        nc.scalar.copy(words_by_fours(o_grouped[1][:]), by_fours(early_banks[2][:]))
         for b in range(2):
-            cols = slice(b * BLOCK, (b + 1) * BLOCK)
-            nc.vector.tensor_copy(words_by_fours(o_grouped[0][:, cols, :]), by_fours(o_early[:, :, cols]))
+            nc.vector.tensor_copy(words_by_fours(o_grouped[0][:, blocks[b], :]), by_fours(o_early[:, :, blocks[b]]))
         quantise_o(0)
         nc.sync.dma_start(out_words[:, :HALF], o_codes[:, :HALF].bitcast(I32))
         for u in range(2):

@@ -250,7 +250,7 @@ def tile_picked_dmpnn8_none_po_kernel(
         spans = ((0, HALF), (HALF, BLOCK), (EARLY, BLOCK))
         o_grouped = [
             keep.tile([P, HALF, PACK], BF16, name="o_grouped0", align_bytes=64),
-            spent.tile([P, BLOCK, PACK], BF16, name="o_grouped1", offset=0, align_bytes=64),
+            keep.tile([P, BLOCK, PACK], BF16, name="o_grouped1", align_bytes=64),
             keep.tile([P, BLOCK, PACK], BF16, name="o_grouped2", align_bytes=64),
         ]
 
@@ -300,16 +300,18 @@ def tile_picked_dmpnn8_none_po_kernel(
             weight_pass(1, last_banks[t][:], t, z_codes[3], z_scales[:, blocks[3]], False, True)
             nc.scalar.copy(o_last[:, t, :], last_banks[t][:])
         nc.sync.dma_start(out_planes[:, :, EARLY:], o_last[:])
-        nc.scalar.copy(words_by_fours(o_grouped[1][:]), by_fours(early_banks[2][:]))
+        share = BLOCK // 2
+        nc.scalar.copy(words_by_fours(o_grouped[1][:, share:, :]), by_fours(early_banks[2][:, :, share:]))
         for b in range(2):
             nc.vector.tensor_copy(words_by_fours(o_grouped[0][:, blocks[b], :]), by_fours(o_early[:, :, blocks[b]]))
+        nc.vector.tensor_copy(words_by_fours(o_grouped[1][:, :share, :]), by_fours(o_early[:, :, HALF : HALF + share]))
         quantise_o(0)
         nc.sync.dma_start(out_words[:, :HALF], o_codes[:, :HALF].bitcast(I32))
         for u in range(2):
             pair = slice(2 * u, 2 * u + 2)
             nc.vector.tensor_copy(o_grouped[2][:, :, pair], o_last[:, pair, :].rearrange("p t c -> p c t"))
-        quantise_o(2)
         quantise_o(1)
+        quantise_o(2)
         nc.sync.dma_start(out_words[:, HALF:], o_codes[:, HALF:].bitcast(I32))
         for r in range(4):
             queue = nc.sync if r % 2 else nc.scalar

@@ -162,9 +162,8 @@ def tile_picked_dmpnn8_none_po_kernel(
         for r in range(4):
             nc.sync.dma_start(w3_plane[r:P:32, :].bitcast(I32), w_scales[8 * r + 4 : P : 32, :].bitcast(I32))
 
-        z_first_codes = spent.tile([P, BLOCK], U32, offset=8 * N, align_bytes=64)
-        z_later_codes = keep.tile([P, EARLY], U32, align_bytes=64)
-        z_codes = [z_first_codes[:]] + [z_later_codes[:, b * BLOCK : (b + 1) * BLOCK] for b in range(3)]
+        z_words = keep.tile([P, S], U32, align_bytes=64)
+        z_codes = [z_words[:, b * BLOCK : (b + 1) * BLOCK] for b in range(4)]
         z_scales = keep.tile([P, S], U8, align_bytes=64)
         o_codes = keep.tile([P, S], U32, align_bytes=64)
         o_scales = keep.tile([P, S], U8, align_bytes=64)
@@ -234,6 +233,7 @@ def tile_picked_dmpnn8_none_po_kernel(
 
         for h in range(2):
             nc.vector.tensor_copy(y[1][:, h * HALF : (h + 1) * HALF], y_banks[3 + h][:])
+        nc.vector.tensor_copy(second[0][1][:], window(0, in2_list, HALF, HALF))
         for t in (2, 3):
             nc.vector.tensor_copy(y[t][:], y_banks[3 + t][:])
         blocks = [slice(b * BLOCK, (b + 1) * BLOCK) for b in range(4)]
@@ -271,15 +271,13 @@ def tile_picked_dmpnn8_none_po_kernel(
                 in_=o_grouped[n][:].rearrange("p c t -> p (c t)"),
             )
 
-        nc.vector.tensor_copy(second[0][1][:], window(0, in2_list, HALF, HALF))
-        for t, h in ((0, 0), (1, 0), (1, 1), (2, 0), (3, 0)):
+        for t, h in ((0, 0), (1, 0), (1, 1), (2, 0), (3, 0), (3, 1)):
             fetch_second(t, h * HALF, HALF)
-        for t, h in ((0, 0), (0, 1), (1, 0), (2, 0), (3, 0), (1, 1)):
+        for t, h in ((0, 0), (0, 1), (1, 0), (2, 0), (3, 0), (1, 1), (3, 1)):
             fetch_sum(t, h * HALF, HALF)
         for t in range(PACK):
             fetch_back(t, 0, HALF)
-        for t in (2, 3):
-            fetch_second(t, HALF, HALF)
+        fetch_second(2, HALF, HALF)
         for b in (2, 3):
             for t in range(PACK):
                 fetch_back(t, b * BLOCK, BLOCK)
@@ -287,9 +285,8 @@ def tile_picked_dmpnn8_none_po_kernel(
         fetch_sum(2, HALF, HALF)
         quantise_z(0)
         round_z(1)
-        fetch_sum(3, HALF, HALF)
-        quantise_z(1)
         round_z(2)
+        quantise_z(1)
         round_z(3, slice(0, 2))
         quantise_z(2)
         round_z(3, slice(2, PACK))

@@ -16,11 +16,14 @@ COPY = mybir.ActivationFunctionType.Copy
 
 P = 128
 PACK = 4
+QUADRANT = 32
+SPREAD = 8
 GROUP = 16
 K, T, S, H, N = 512, 2048, 512, 512, 512
 HALF = S // 2
-BLOCK = 128
-EARLY = S - BLOCK
+STRIP = 128
+EARLY = S - STRIP
+SHARE = STRIP // 2
 
 FLOPS = 2 * K * H * S + 2 * K * N * S + 2 * H * N * S
 
@@ -50,7 +53,6 @@ def tile_picked_dmpnn8_none_po_kernel(
         nc.vector.memset(x_scale_table[:].bitcast(I32), 0)
         w3_plane = keep.tile([P, N], U8, align_bytes=64)
         nc.vector.memset(w3_plane[:].bitcast(I32), 0)
-
         raw_scales = keep.tile([P, N], U8, align_bytes=64)
         nc.vector.memset(raw_scales[:].bitcast(I32), 0)
 
@@ -59,8 +61,8 @@ def tile_picked_dmpnn8_none_po_kernel(
             nc.sync.dma_start(list_tile[:], source)
             return list_tile
 
-        def deal_words(copy, dealt, raw):
-            copy(
+        def deal_words(dealt, raw):
+            nc.gpsimd.tensor_copy(
                 dealt.bitcast(U16).rearrange("p (t m) -> p t m", t=PACK),
                 raw.bitcast(U16).rearrange("p (m t) -> p t m", t=PACK),
             )
@@ -72,7 +74,7 @@ def tile_picked_dmpnn8_none_po_kernel(
         picked = load_list("picked", offs)
         in2_list = load_list("in2", in2)
         in1_list = load_list("in1", in1)
-        nc.sync.dma_start(x_scale_table[0:P:8, :].bitcast(I32), x_scales[0].bitcast(I32))
+        nc.sync.dma_start(x_scale_table[0:P:SPREAD, :].bitcast(I32), x_scales[0].bitcast(I32))
         nc.sync.dma_start(x_table[:].bitcast(I32), x_words[0].rearrange("p c r -> p (c r)").bitcast(I32))
         rev_list = load_list("rev", rev)
         nc.sync.dma_start(w1_raw[1][:], w1_rows[:, 2:4, :])
@@ -80,7 +82,7 @@ def tile_picked_dmpnn8_none_po_kernel(
         for w, words in enumerate((w2_words, w3_words)):
             nc.sync.dma_start(raw_words[w][:].bitcast(I32), words[0].bitcast(I32))
         for w, scales in enumerate((w2_scales, w3_scales)):
-            nc.sync.dma_start(raw_scales[4 * w : P : 8, :].bitcast(I32), scales[0].bitcast(I32))
+            nc.sync.dma_start(raw_scales[PACK * w : P : SPREAD, :].bitcast(I32), scales[0].bitcast(I32))
 
         x_spread_scales = keep.tile([P, S], U8, tag="spread_scales", align_bytes=64)
         nc.vector.tensor_copy(x_spread_scales[:], x_scale_table[:].indirect(picked[:]))
@@ -94,19 +96,21 @@ def tile_picked_dmpnn8_none_po_kernel(
             spent.tile([P, 3 * H], BF16, name="w1_grouped1", offset=0, align_bytes=64),
         ]
 
-        def round_w1(cast, h, first, count, columns=slice(0, P)):
+        def round_w1(cast, h, first, count, places=slice(0, P)):
             u, within = divmod(first, 2)
             source = w1_raw[h][:].rearrange("p j (m t) -> p m t j", t=PACK)
             target = grouped[u][:, : 2 * H].rearrange("p (t m j) -> p m t j", t=2, j=PACK)
             cast(
-                target[:, columns, within : within + count, 2 * h : 2 * h + 2],
-                source[:, columns, first : first + count, :],
+                target[:, places, within : within + count, 2 * h : 2 * h + 2],
+                source[:, places, first : first + count, :],
             )
 
         round_w1(nc.vector.tensor_copy, 0, 0, 2)
         round_w1(lambda dst, src: nc.scalar.activation(dst, src, COPY), 0, 2, 2)
-        for r in range(1, 4):
-            nc.scalar.dma_start(x_picked_scales[r:P:32, :].bitcast(I32), x_spread_scales[8 * r : P : 32, :].bitcast(I32))
+        for r in range(1, PACK):
+            nc.scalar.dma_start(
+                x_picked_scales[r:P:QUADRANT, :].bitcast(I32), x_spread_scales[SPREAD * r : P : QUADRANT, :].bitcast(I32)
+            )
         x_picked = keep.tile([P, S], U32, align_bytes=64)
         nc.vector.tensor_copy(x_picked[:], x_table[:].indirect(picked[:]))
         round_w1(nc.vector.tensor_copy, 1, 0, 1, slice(0, P // 2))
@@ -129,14 +133,14 @@ def tile_picked_dmpnn8_none_po_kernel(
             w_scales[:].rearrange("p (t m) -> p t m", t=PACK),
             raw_scales[:].rearrange("p (m t) -> p t m", t=PACK),
         )
-        deal_words(nc.gpsimd.tensor_copy, w2_dealt[:], raw_words[0][:])
-        deal_words(nc.gpsimd.tensor_copy, w3_dealt[:], raw_words[1][:])
+        deal_words(w2_dealt[:], raw_words[0][:])
+        deal_words(w3_dealt[:], raw_words[1][:])
         dealt_words = [w2_dealt, w3_dealt]
         dealt_scales = [w_scales, w3_plane]
 
         y = [keep.tile([P, S], F32, name="y%d" % t, align_bytes=64) for t in range(PACK)]
         y_banks = []
-        pieces = [((0, HALF), (HALF, BLOCK), (EARLY, BLOCK)), ((0, HALF), (HALF, HALF)), ((0, S),), ((0, S),)]
+        pieces = [((0, HALF), (HALF, STRIP), (EARLY, STRIP)), ((0, HALF), (HALF, HALF)), ((0, S),), ((0, S),)]
         for t in range(PACK):
             places = slice(t * P, (t + 1) * P)
             for c0, width in pieces[t]:
@@ -156,14 +160,15 @@ def tile_picked_dmpnn8_none_po_kernel(
                     drain = nc.vector.tensor_copy if width == HALF else nc.scalar.copy
                     drain(y[t][:, cols], bank[:])
 
+        for r in range(1, PACK):
+            nc.sync.dma_start(w_scales[r:P:QUADRANT, :].bitcast(I32), w_scales[SPREAD * r : P : QUADRANT, :].bitcast(I32))
+        for r in range(PACK):
+            nc.sync.dma_start(
+                w3_plane[r:P:QUADRANT, :].bitcast(I32), w_scales[SPREAD * r + PACK : P : QUADRANT, :].bitcast(I32)
+            )
 
-        for r in range(1, 4):
-            nc.sync.dma_start(w_scales[r:P:32, :].bitcast(I32), w_scales[8 * r : P : 32, :].bitcast(I32))
-        for r in range(4):
-            nc.sync.dma_start(w3_plane[r:P:32, :].bitcast(I32), w_scales[8 * r + 4 : P : 32, :].bitcast(I32))
-
-        z_words = keep.tile([P, S], U32, align_bytes=64)
-        z_codes = [z_words[:, b * BLOCK : (b + 1) * BLOCK] for b in range(4)]
+        strips = [slice(b * STRIP, (b + 1) * STRIP) for b in range(4)]
+        z_codes = keep.tile([P, S], U32, align_bytes=64)
         z_scales = keep.tile([P, S], U8, align_bytes=64)
         o_codes = keep.tile([P, S], U32, align_bytes=64)
         o_scales = keep.tile([P, S], U8, align_bytes=64)
@@ -181,6 +186,12 @@ def tile_picked_dmpnn8_none_po_kernel(
                 stop=stop,
             )
 
+        def h0_pass(target, b, t, start, stop):
+            weight_pass(0, target, t, x_picked[:, strips[b]], x_picked_scales[:, strips[b]], start, stop)
+
+        def z_pass(target, b, t, start, stop):
+            weight_pass(1, target, t, z_codes[:, strips[b]], z_scales[:, strips[b]], start, stop)
+
         reused = {(2, 1): "second1_0"}
         second = [
             [
@@ -192,30 +203,32 @@ def tile_picked_dmpnn8_none_po_kernel(
         back = [keep.tile([P, PACK, HALF], F32, name="back", tag="second0_%d" % h, align_bytes=64) for h in range(2)]
         sums = [keep.tile([P, PACK, HALF], F32, name="sums", tag="sums%d" % h, align_bytes=64) for h in range(2)]
         z_grouped = [
-            keep.tile([P, BLOCK, PACK], BF16, name="z_grouped", tag="z_grouped%d" % b, align_bytes=64) for b in range(4)
+            keep.tile([P, STRIP, PACK], BF16, name="z_grouped", tag="z_grouped%d" % b, align_bytes=64) for b in range(4)
         ]
 
         def window(t, list_tile, start, count):
             return y[t][:].indirect(entries(list_tile, start, count))
 
-        def place(c0, count):
+        def in_half(c0, count):
             return c0 // HALF, slice(c0 % HALF, c0 % HALF + count)
 
         def fetch_second(t, c0, count):
-            h, within = place(c0, count)
+            h, within = in_half(c0, count)
             nc.scalar.activation(second[t][h][:, within], window(t, in2_list, c0, count), COPY)
 
-        def fetch_sum(t, c0, count):
-            h, within = place(c0, count)
-            nc.vector.tensor_tensor(sums[h][:, t, within], window(t, in1_list, c0, count), second[t][h][:, within], ADD)
+        def fetch_second_on_vector(t, c0, count):
+            h, within = in_half(c0, count)
+            nc.vector.tensor_copy(second[t][h][:, within], window(t, in2_list, c0, count))
+
+        def fetch_sum(t, h):
+            nc.vector.tensor_tensor(sums[h][:, t, :], window(t, in1_list, h * HALF, HALF), second[t][h][:], ADD)
 
         def fetch_back(t, c0, count):
-            h, within = place(c0, count)
+            h, within = in_half(c0, count)
             nc.scalar.activation(back[h][:, t, within], window(t, rev_list, c0, count), COPY)
 
-
         def round_z(b, planes=slice(0, PACK)):
-            h, within = place(b * BLOCK, BLOCK)
+            h, within = in_half(b * STRIP, STRIP)
             nc.vector.tensor_tensor(
                 words_by_fours(z_grouped[b][:, :, planes]),
                 by_fours(sums[h][:, planes, within]),
@@ -224,65 +237,61 @@ def tile_picked_dmpnn8_none_po_kernel(
             )
 
         def quantise_z(b):
-            cols = slice(b * BLOCK, (b + 1) * BLOCK)
             nc.vector.quantize_mx(
-                out=z_codes[b].bitcast(FP8X4),
-                scales=z_scales[:, cols],
+                out=z_codes[:, strips[b]].bitcast(FP8X4),
+                scales=z_scales[:, strips[b]],
                 in_=z_grouped[b][:].rearrange("p c t -> p (c t)"),
             )
 
         for h in range(2):
             nc.vector.tensor_copy(y[1][:, h * HALF : (h + 1) * HALF], y_banks[3 + h][:])
-        nc.vector.tensor_copy(second[0][1][:], window(0, in2_list, HALF, HALF))
+        fetch_second_on_vector(0, HALF, HALF)
         for t in (2, 3):
             nc.vector.tensor_copy(y[t][:], y_banks[3 + t][:])
-        blocks = [slice(b * BLOCK, (b + 1) * BLOCK) for b in range(4)]
-        early_banks = [psum.tile([P, PACK, BLOCK], F32, name="o_bank", tag="bank%d" % b) for b in (7, 0, 1)]
+
+        early_banks = [psum.tile([P, PACK, STRIP], F32, name="o_bank", tag="bank%d" % n) for n in (7, 0, 1)]
         for b in (1, 2):
             for t in range(PACK):
-                weight_pass(0, early_banks[b][:, t, :], t, x_picked[:, blocks[b]], x_picked_scales[:, blocks[b]], t == 0, False)
-        last_banks = [psum.tile([P, BLOCK], F32, name="o_bank", tag="bank%d" % (2 + t)) for t in range(PACK)]
+                h0_pass(early_banks[b][:, t, :], b, t, t == 0, False)
+        last_banks = [psum.tile([P, STRIP], F32, name="o_bank", tag="bank%d" % (2 + t)) for t in range(PACK)]
         for t in range(PACK):
-            weight_pass(0, last_banks[t][:], t, x_picked[:, blocks[3]], x_picked_scales[:, blocks[3]], True, False)
+            h0_pass(last_banks[t][:], 3, t, True, False)
 
         o_early = keep.tile([P, PACK, EARLY], F32, align_bytes=64)
-        o_last = keep.tile([P, PACK, BLOCK], F32, align_bytes=64)
-        spans = ((0, HALF), (HALF, BLOCK), (EARLY, BLOCK))
+        o_last = keep.tile([P, PACK, STRIP], F32, align_bytes=64)
+        spans = (slice(0, HALF), strips[2], strips[3])
         o_grouped = [
-            keep.tile([P, HALF, PACK], BF16, name="o_grouped0", align_bytes=64),
-            keep.tile([P, BLOCK, PACK], BF16, name="o_grouped1", align_bytes=64),
-            keep.tile([P, BLOCK, PACK], BF16, name="o_grouped2", align_bytes=64),
+            keep.tile([P, span.stop - span.start, PACK], BF16, name="o_grouped%d" % n, align_bytes=64)
+            for n, span in enumerate(spans)
         ]
 
-        def product(b):
-            for t in range(PACK):
-                first, last = b == 0 and t == 0, b > 0 and t == PACK - 1
-                weight_pass(1, early_banks[b][:, t, :], t, z_codes[b], z_scales[:, blocks[b]], first, last)
-            for t in range(PACK if b == 0 else 0):
-                weight_pass(0, early_banks[b][:, t, :], t, x_picked[:, blocks[b]], x_picked_scales[:, blocks[b]], False, t == PACK - 1)
-            nc.scalar.copy(o_early[:, :, blocks[b]], early_banks[b][:])
-            nc.sync.dma_start(out_planes[:, :, blocks[b]], o_early[:, :, blocks[b]])
+        def store_early(b):
+            nc.scalar.copy(o_early[:, :, strips[b]], early_banks[b][:])
+            nc.sync.dma_start(out_planes[:, :, strips[b]], o_early[:, :, strips[b]])
 
         def quantise_o(n):
-            cols = slice(spans[n][0], spans[n][0] + spans[n][1])
             nc.vector.quantize_mx(
-                out=o_codes[:, cols].bitcast(FP8X4),
-                scales=o_scales[:, cols],
+                out=o_codes[:, spans[n]].bitcast(FP8X4),
+                scales=o_scales[:, spans[n]],
                 in_=o_grouped[n][:].rearrange("p c t -> p (c t)"),
             )
 
-        for t, h in ((0, 0), (1, 0), (1, 1), (2, 0), (3, 0), (3, 1)):
-            fetch_second(t, h * HALF, HALF)
-        for t, h in ((0, 0), (0, 1), (1, 0), (2, 0), (3, 0), (1, 1), (3, 1)):
-            fetch_sum(t, h * HALF, HALF)
+        for t, c0 in ((0, 0), (1, 0), (1, HALF), (2, 0), (3, 0)):
+            fetch_second(t, c0, HALF)
+        fetch_second(3, HALF, STRIP)
+        for t, h in ((0, 0), (0, 1)):
+            fetch_sum(t, h)
+        fetch_second_on_vector(3, EARLY, STRIP)
+        for t, h in ((1, 0), (2, 0), (3, 0), (1, 1), (3, 1)):
+            fetch_sum(t, h)
         for t in range(PACK):
             fetch_back(t, 0, HALF)
         fetch_second(2, HALF, HALF)
         for b in (2, 3):
             for t in range(PACK):
-                fetch_back(t, b * BLOCK, BLOCK)
+                fetch_back(t, b * STRIP, STRIP)
         round_z(0)
-        fetch_sum(2, HALF, HALF)
+        fetch_sum(2, 1)
         quantise_z(0)
         round_z(1)
         round_z(2)
@@ -291,17 +300,25 @@ def tile_picked_dmpnn8_none_po_kernel(
         quantise_z(2)
         round_z(3, slice(2, PACK))
         quantise_z(3)
-        for b in range(3):
-            product(b)
+
         for t in range(PACK):
-            weight_pass(1, last_banks[t][:], t, z_codes[3], z_scales[:, blocks[3]], False, True)
+            z_pass(early_banks[0][:, t, :], 0, t, t == 0, False)
+        for t in range(PACK):
+            h0_pass(early_banks[0][:, t, :], 0, t, False, t == PACK - 1)
+        store_early(0)
+        for b in (1, 2):
+            for t in range(PACK):
+                z_pass(early_banks[b][:, t, :], b, t, False, t == PACK - 1)
+            store_early(b)
+        for t in range(PACK):
+            z_pass(last_banks[t][:], 3, t, False, True)
             nc.scalar.copy(o_last[:, t, :], last_banks[t][:])
         nc.sync.dma_start(out_planes[:, :, EARLY:], o_last[:])
-        share = BLOCK // 2
-        nc.scalar.copy(words_by_fours(o_grouped[1][:, share:, :]), by_fours(early_banks[2][:, :, share:]))
+
+        nc.scalar.copy(words_by_fours(o_grouped[1][:, SHARE:, :]), by_fours(early_banks[2][:, :, SHARE:]))
         for b in range(2):
-            nc.vector.tensor_copy(words_by_fours(o_grouped[0][:, blocks[b], :]), by_fours(o_early[:, :, blocks[b]]))
-        nc.vector.tensor_copy(words_by_fours(o_grouped[1][:, :share, :]), by_fours(o_early[:, :, HALF : HALF + share]))
+            nc.vector.tensor_copy(words_by_fours(o_grouped[0][:, strips[b], :]), by_fours(o_early[:, :, strips[b]]))
+        nc.vector.tensor_copy(words_by_fours(o_grouped[1][:, :SHARE, :]), by_fours(o_early[:, :, HALF : HALF + SHARE]))
         quantise_o(0)
         nc.sync.dma_start(out_words[:, :HALF], o_codes[:, :HALF].bitcast(I32))
         for u in range(2):
@@ -310,6 +327,6 @@ def tile_picked_dmpnn8_none_po_kernel(
         quantise_o(1)
         quantise_o(2)
         nc.sync.dma_start(out_words[:, HALF:], o_codes[:, HALF:].bitcast(I32))
-        for r in range(4):
+        for r in range(PACK):
             queue = nc.sync if r % 2 else nc.scalar
-            queue.dma_start(out_2[0, r:16:4, :].bitcast(I32), o_scales[r:P:32, :].bitcast(I32))
+            queue.dma_start(out_2[0, r : N // 32 : PACK, :].bitcast(I32), o_scales[r:P:QUADRANT, :].bitcast(I32))

from contextlib import ExitStack

import concourse.mybir as mybir

F32 = mybir.dt.float32
BF16 = mybir.dt.bfloat16
I32 = mybir.dt.int32
U32 = mybir.dt.uint32
U16 = mybir.dt.uint16
U8 = mybir.dt.uint8
FP8X4 = mybir.dt.float8_e4m3fn_x4
FP4X4 = mybir.dt.float4_e2m1fn_x4
ADD = mybir.AluOpType.add
SUBTRACT = mybir.AluOpType.subtract
COPY = mybir.ActivationFunctionType.Copy

P = 128
PACK = 4
QUADRANT = 32
SPREAD = 8
GROUP = 16
K, T, S, H, N = 512, 2048, 512, 512, 512
HALF = S // 2
STRIP = 128
EARLY = S - STRIP
SHARE = STRIP // 2

FLOPS = 2 * K * H * S + 2 * K * N * S + 2 * H * N * S


def entries(list_tile, start, count):
    return list_tile[:, start // GROUP : (start + count) // GROUP]


def by_fours(planes):
    return planes.rearrange("p t (c i) -> p c t i", i=4)


def words_by_fours(grouped):
    return grouped.rearrange("p (c i) t -> p c t i", i=4)


def tile_picked_dmpnn8_none_po_kernel(
    tc, x_words, x_scales, w1, w2_words, w2_scales, w3_words, w3_scales, offs, in1, in2, rev, out_0, out_1, out_2
):
    nc = tc.nc
    with ExitStack() as ctx:
        keep = ctx.enter_context(tc.tile_pool(name="keep", bufs=1))
        spent = ctx.enter_context(tc.tile_pool(name="spent", bufs=1))
        psum = ctx.enter_context(tc.psum_pool(name="psum", bufs=1))

        x_scale_table = keep.tile([P, T], U8, tag="x_scale_table", align_bytes=64)
        nc.vector.memset(x_scale_table[:].bitcast(I32), 0)
        w3_plane = keep.tile([P, N], U8, align_bytes=64)
        nc.vector.memset(w3_plane[:].bitcast(I32), 0)
        raw_scales = keep.tile([P, N], U8, align_bytes=64)
        nc.vector.memset(raw_scales[:].bitcast(I32), 0)

        def load_list(name, source):
            list_tile = keep.tile([P, S // GROUP], U16, name=name + "_list")
            nc.sync.dma_start(list_tile[:], source)
            return list_tile

        def deal_words(dealt, raw):
            nc.gpsimd.tensor_copy(
                dealt.bitcast(U16).rearrange("p (t m) -> p t m", t=PACK),
                raw.bitcast(U16).rearrange("p (m t) -> p t m", t=PACK),
            )

        w1_rows = w1.rearrange("(p j) c -> p j c", j=PACK)
        w1_raw = [keep.tile([P, 2, H], F32, name="w1_raw%d" % h, align_bytes=64) for h in range(2)]
        x_table = keep.tile([P, T], U32, tag="x_table", align_bytes=64)
        nc.sync.dma_start(w1_raw[0][:], w1_rows[:, 0:2, :])
        picked = load_list("picked", offs)
        in2_list = load_list("in2", in2)
        in1_list = load_list("in1", in1)
        nc.sync.dma_start(x_scale_table[0:P:SPREAD, :].bitcast(I32), x_scales[0].bitcast(I32))
        nc.sync.dma_start(x_table[:].bitcast(I32), x_words[0].rearrange("p c r -> p (c r)").bitcast(I32))
        rev_list = load_list("rev", rev)
        nc.sync.dma_start(w1_raw[1][:], w1_rows[:, 2:4, :])
        raw_words = [keep.tile([P, 2 * N], U8, name="raw_words%d" % w, align_bytes=64) for w in range(2)]
        for w, words in enumerate((w2_words, w3_words)):
            nc.sync.dma_start(raw_words[w][:].bitcast(I32), words[0].bitcast(I32))
        for w, scales in enumerate((w2_scales, w3_scales)):
            nc.sync.dma_start(raw_scales[PACK * w : P : SPREAD, :].bitcast(I32), scales[0].bitcast(I32))

        x_spread_scales = keep.tile([P, S], U8, tag="spread_scales", align_bytes=64)
        nc.vector.tensor_copy(x_spread_scales[:], x_scale_table[:].indirect(picked[:]))
        x_picked_scales = keep.tile([P, S], U8, align_bytes=64)
        nc.vector.tensor_copy(x_picked_scales[:].bitcast(I32), x_spread_scales[:].bitcast(I32))

        w1_codes = keep.tile([P, H], U32, tag="w1_codes", align_bytes=64)
        w1_scales = keep.tile([P, H], U8, align_bytes=64)
        grouped = [
            keep.tile([P, 2 * H], BF16, name="w1_grouped0", tag="x_scale_table", align_bytes=64),
            spent.tile([P, 3 * H], BF16, name="w1_grouped1", offset=0, align_bytes=64),
        ]

        def round_w1(cast, h, first, count, places=slice(0, P)):
            u, within = divmod(first, 2)
            source = w1_raw[h][:].rearrange("p j (m t) -> p m t j", t=PACK)
            target = grouped[u][:, : 2 * H].rearrange("p (t m j) -> p m t j", t=2, j=PACK)
            cast(
                target[:, places, within : within + count, 2 * h : 2 * h + 2],
                source[:, places, first : first + count, :],
            )

        round_w1(nc.vector.tensor_copy, 0, 0, 2)
        round_w1(lambda dst, src: nc.scalar.activation(dst, src, COPY), 0, 2, 2)
        for r in range(1, PACK):
            nc.scalar.dma_start(
                x_picked_scales[r:P:QUADRANT, :].bitcast(I32), x_spread_scales[SPREAD * r : P : QUADRANT, :].bitcast(I32)
            )
        x_picked = keep.tile([P, S], U32, align_bytes=64)
        nc.vector.tensor_copy(x_picked[:], x_table[:].indirect(picked[:]))
        round_w1(nc.vector.tensor_copy, 1, 0, 1, slice(0, P // 2))
        round_w1(nc.scalar.copy, 1, 0, 1, slice(P // 2, P))
        round_w1(nc.vector.tensor_copy, 1, 1, 1)
        round_w1(nc.scalar.copy, 1, 2, 2)
        for first, count in ((0, 1), (1, 1), (2, 2)):
            places = slice(first * P, (first + count) * P)
            u, within = divmod(first, 2)
            nc.vector.quantize_mx(
                out=w1_codes[:, places].bitcast(FP8X4),
                scales=w1_scales[:, places],
                in_=grouped[u][:, within * H : (within + count) * H],
            )

        w2_dealt = spent.tile([P, 2 * N], U8, offset=3 * N, align_bytes=64)
        w3_dealt = spent.tile([P, 2 * N], U8, offset=0, align_bytes=64)
        w_scales = spent.tile([P, N], U8, offset=2 * N, align_bytes=64)
        nc.gpsimd.tensor_copy(
            w_scales[:].rearrange("p (t m) -> p t m", t=PACK),
            raw_scales[:].rearrange("p (m t) -> p t m", t=PACK),
        )
        deal_words(w2_dealt[:], raw_words[0][:])
        deal_words(w3_dealt[:], raw_words[1][:])
        dealt_words = [w2_dealt, w3_dealt]
        dealt_scales = [w_scales, w3_plane]

        y = [keep.tile([P, S], F32, name="y%d" % t, align_bytes=64) for t in range(PACK)]
        y_banks = []
        pieces = [((0, HALF), (HALF, STRIP), (EARLY, STRIP)), ((0, HALF), (HALF, HALF)), ((0, S),), ((0, S),)]
        for t in range(PACK):
            places = slice(t * P, (t + 1) * P)
            for c0, width in pieces[t]:
                cols = slice(c0, c0 + width)
                bank = psum.tile([P, width], F32, name="y_bank", tag="bank%d" % len(y_banks))
                y_banks.append(bank)
                nc.tensor.matmul_mx(
                    out=bank[:],
                    lhsT=w1_codes[:, places].bitcast(FP8X4),
                    lhsT_scale=w1_scales[:, places],
                    rhs=x_picked[:, cols].bitcast(FP8X4),
                    rhs_scale=x_picked_scales[:, cols],
                    start=True,
                    stop=True,
                )
                if t == 0:
                    drain = nc.vector.tensor_copy if width == HALF else nc.scalar.copy
                    drain(y[t][:, cols], bank[:])

        for r in range(1, PACK):
            nc.sync.dma_start(w_scales[r:P:QUADRANT, :].bitcast(I32), w_scales[SPREAD * r : P : QUADRANT, :].bitcast(I32))
        for r in range(PACK):
            nc.sync.dma_start(
                w3_plane[r:P:QUADRANT, :].bitcast(I32), w_scales[SPREAD * r + PACK : P : QUADRANT, :].bitcast(I32)
            )

        strips = [slice(b * STRIP, (b + 1) * STRIP) for b in range(4)]
        z_codes = keep.tile([P, S], U32, align_bytes=64)
        z_scales = keep.tile([P, S], U8, align_bytes=64)
        o_codes = keep.tile([P, S], U32, align_bytes=64)
        o_scales = keep.tile([P, S], U8, align_bytes=64)
        out_planes = out_0.rearrange("(p t) j -> p t j", t=PACK)
        out_words = out_1[0].rearrange("p c r -> p (c r)").bitcast(I32)

        def weight_pass(w, target, t, moving, moving_scales, start, stop):
            nc.tensor.matmul_mx(
                out=target,
                lhsT=dealt_words[w][:, 2 * P * t : 2 * P * (t + 1)].bitcast(FP4X4),
                lhsT_scale=dealt_scales[w][:, P * t : P * (t + 1)],
                rhs=moving.bitcast(FP8X4),
                rhs_scale=moving_scales,
                start=start,
                stop=stop,
            )

        def h0_pass(target, b, t, start, stop):
            weight_pass(0, target, t, x_picked[:, strips[b]], x_picked_scales[:, strips[b]], start, stop)

        def z_pass(target, b, t, start, stop):
            weight_pass(1, target, t, z_codes[:, strips[b]], z_scales[:, strips[b]], start, stop)

        reused = {(2, 1): "second1_0"}
        second = [
            [
                keep.tile([P, HALF], F32, name="second", tag=reused.get((t, h), "second%d_%d" % (t, h)), align_bytes=64)
                for h in range(2)
            ]
            for t in range(PACK)
        ]
        back = [keep.tile([P, PACK, HALF], F32, name="back", tag="second0_%d" % h, align_bytes=64) for h in range(2)]
        sums = [keep.tile([P, PACK, HALF], F32, name="sums", tag="sums%d" % h, align_bytes=64) for h in range(2)]
        z_grouped = [
            keep.tile([P, STRIP, PACK], BF16, name="z_grouped", tag="z_grouped%d" % b, align_bytes=64) for b in range(4)
        ]

        def window(t, list_tile, start, count):
            return y[t][:].indirect(entries(list_tile, start, count))

        def in_half(c0, count):
            return c0 // HALF, slice(c0 % HALF, c0 % HALF + count)

        def fetch_second(t, c0, count):
            h, within = in_half(c0, count)
            nc.scalar.activation(second[t][h][:, within], window(t, in2_list, c0, count), COPY)

        def fetch_second_on_vector(t, c0, count):
            h, within = in_half(c0, count)
            nc.vector.tensor_copy(second[t][h][:, within], window(t, in2_list, c0, count))

        def fetch_sum(t, h):
            nc.vector.tensor_tensor(sums[h][:, t, :], window(t, in1_list, h * HALF, HALF), second[t][h][:], ADD)

        def fetch_back(t, c0, count):
            h, within = in_half(c0, count)
            nc.scalar.activation(back[h][:, t, within], window(t, rev_list, c0, count), COPY)

        def round_z(b, planes=slice(0, PACK)):
            h, within = in_half(b * STRIP, STRIP)
            nc.vector.tensor_tensor(
                words_by_fours(z_grouped[b][:, :, planes]),
                by_fours(sums[h][:, planes, within]),
                by_fours(back[h][:, planes, within]),
                SUBTRACT,
            )

        def quantise_z(b):
            nc.vector.quantize_mx(
                out=z_codes[:, strips[b]].bitcast(FP8X4),
                scales=z_scales[:, strips[b]],
                in_=z_grouped[b][:].rearrange("p c t -> p (c t)"),
            )

        for h in range(2):
            nc.vector.tensor_copy(y[1][:, h * HALF : (h + 1) * HALF], y_banks[3 + h][:])
        fetch_second_on_vector(0, HALF, HALF)
        for t in (2, 3):
            nc.vector.tensor_copy(y[t][:], y_banks[3 + t][:])

        early_banks = [psum.tile([P, PACK, STRIP], F32, name="o_bank", tag="bank%d" % n) for n in (7, 0, 1)]
        for b in (1, 2):
            for t in range(PACK):
                h0_pass(early_banks[b][:, t, :], b, t, t == 0, False)
        last_banks = [psum.tile([P, STRIP], F32, name="o_bank", tag="bank%d" % (2 + t)) for t in range(PACK)]
        for t in range(PACK):
            h0_pass(last_banks[t][:], 3, t, True, False)

        o_early = keep.tile([P, PACK, EARLY], F32, align_bytes=64)
        o_last = keep.tile([P, PACK, STRIP], F32, align_bytes=64)
        spans = (slice(0, HALF), strips[2], strips[3])
        o_grouped = [
            keep.tile([P, span.stop - span.start, PACK], BF16, name="o_grouped%d" % n, align_bytes=64)
            for n, span in enumerate(spans)
        ]

        def store_early(b):
            nc.scalar.copy(o_early[:, :, strips[b]], early_banks[b][:])
            nc.sync.dma_start(out_planes[:, :, strips[b]], o_early[:, :, strips[b]])

        def quantise_o(n):
            nc.vector.quantize_mx(
                out=o_codes[:, spans[n]].bitcast(FP8X4),
                scales=o_scales[:, spans[n]],
                in_=o_grouped[n][:].rearrange("p c t -> p (c t)"),
            )

        for t, c0 in ((0, 0), (1, 0), (1, HALF), (2, 0), (3, 0)):
            fetch_second(t, c0, HALF)
        fetch_second(3, HALF, STRIP)
        for t, h in ((0, 0), (0, 1)):
            fetch_sum(t, h)
        fetch_second_on_vector(3, EARLY, STRIP)
        for t, h in ((1, 0), (2, 0), (3, 0), (1, 1), (3, 1)):
            fetch_sum(t, h)
        for t in range(PACK):
            fetch_back(t, 0, HALF)
        fetch_second(2, HALF, HALF)
        for b in (2, 3):
            for t in range(PACK):
                fetch_back(t, b * STRIP, STRIP)
        round_z(0)
        fetch_sum(2, 1)
        quantise_z(0)
        round_z(1)
        round_z(2)
        quantise_z(1)
        round_z(3, slice(0, 2))
        quantise_z(2)
        round_z(3, slice(2, PACK))
        quantise_z(3)

        for t in range(PACK):
            z_pass(early_banks[0][:, t, :], 0, t, t == 0, False)
        for t in range(PACK):
            h0_pass(early_banks[0][:, t, :], 0, t, False, t == PACK - 1)
        store_early(0)
        for b in (1, 2):
            for t in range(PACK):
                z_pass(early_banks[b][:, t, :], b, t, False, t == PACK - 1)
            store_early(b)
        for t in range(PACK):
            z_pass(last_banks[t][:], 3, t, False, True)
            nc.scalar.copy(o_last[:, t, :], last_banks[t][:])
        nc.sync.dma_start(out_planes[:, :, EARLY:], o_last[:])

        nc.scalar.copy(words_by_fours(o_grouped[1][:, SHARE:, :]), by_fours(early_banks[2][:, :, SHARE:]))
        for b in range(2):
            nc.vector.tensor_copy(words_by_fours(o_grouped[0][:, strips[b], :]), by_fours(o_early[:, :, strips[b]]))
        nc.vector.tensor_copy(words_by_fours(o_grouped[1][:, :SHARE, :]), by_fours(o_early[:, :, HALF : HALF + SHARE]))
        quantise_o(0)
        nc.sync.dma_start(out_words[:, :HALF], o_codes[:, :HALF].bitcast(I32))
        for u in range(2):
            pair = slice(2 * u, 2 * u + 2)
            nc.vector.tensor_copy(o_grouped[2][:, :, pair], o_last[:, pair, :].rearrange("p t c -> p c t"))
        quantise_o(1)
        quantise_o(2)
        nc.sync.dma_start(out_words[:, HALF:], o_codes[:, HALF:].bitcast(I32))
        for r in range(PACK):
            queue = nc.sync if r % 2 else nc.scalar
            queue.dma_start(out_2[0, r : N // 32 : PACK, :].bitcast(I32), o_scales[r:P:QUADRANT, :].bitcast(I32))
